import numpy as np, ml_dtypes
CORES = [2,6,10,14,18,22,26,30]
N = 8
BF = ml_dtypes.bfloat16
def gentries(a):
    return np.ascontiguousarray(a.reshape(8, 16, -1).transpose(0, 2, 1)).reshape(8, -1)
def gtable(e):
    e = np.asarray(e); return np.ascontiguousarray(e.reshape(8, -1, 16).transpose(0, 2, 1)).reshape(128, -1).astype(np.int32)
D, B, W, K, NB, S, RO = 2, 6, 4096, 2048, 128, 32, 4
def parts(rng):
    return rng.integers(0, 256, (N, 8, 16, W)), rng.integers(0, W, (N, 8, K)), rng.integers(0, 256, (N, 8, 16, NB)), rng.integers(900, 1701, (N, 8, RO))
def pack(X, L, z, t):
    return {"x0": np.ascontiguousarray(X.reshape(N, 128, W)).astype(np.float32).astype(BF), "l0": np.stack([gtable(a) for a in L]),
            "z0": np.ascontiguousarray(z.reshape(N, 128, NB)).astype(np.float32).astype(BF), "th": np.ascontiguousarray(t).astype(np.int32)}
def setup_inputs(rng):
    return pack(*parts(rng))
def setup_inputs_spread(rng):
    X = np.minimum((np.exp2(8 * rng.random((N, 8, 1, W))) * rng.random((N, 8, 16, W))).astype(np.int64), 255)
    z = np.minimum((np.exp2(8 * rng.random((N, 8, 1, NB))) * rng.random((N, 8, 16, NB))).astype(np.int64), 255)
    L = np.minimum((W * rng.random((N, 8, K)) ** rng.choice(np.array([1.0, 2.0, 4.0]), (N, 8, 1))).astype(np.int64), W - 1)
    t = np.minimum(np.exp2(12 * rng.random((N, 8, RO))).astype(np.int64), 4080)
    return pack(X, L, z, t)
def setup_inputs_ends(rng):
    X = 255 * rng.integers(0, 2, (N, 8, 16, W)); X = np.where(rng.random((N, 8, 1, W)) < 0.5, 255 * rng.integers(0, 2, (N, 8, 1, W)), X)
    z = 255 * rng.integers(0, 2, (N, 8, 16, NB)); z = np.where(rng.random((N, 8, 1, NB)) < 0.5, 255 * rng.integers(0, 2, (N, 8, 1, NB)), z)
    sw = rng.integers(0, 2, (N, 8, 1)); X[..., 0] = 255 * sw; X[..., W - 1] = 255 * (1 - sw)
    z[..., 0] = 255 * rng.integers(0, 2, (N, 8, 1)); z[..., NB - 1] = 255 * rng.integers(0, 2, (N, 8, 1))
    L = (W - 1) * rng.integers(0, 2, (N, 8, K)); m = rng.random((N, 8, K)) < 0.25; m[:, 1::2] = False
    L = np.where(m, rng.integers(0, W, (N, 8, K)), L)
    L[..., 0] = W - 1; L[..., 1] = 0; L[..., K - 2] = 0; L[..., K - 1] = W - 1
    t = 4080 * rng.integers(0, 2, (N, 8, RO)); t[:, 0, 0] = 0; t[:, 1, 0] = 4080
    L[:, 5] = 0; L[:, 6] = W - 1; L[:, 7] = 0; X[:, 7] = 0; X[:, 7, :, 0] = 255; X[:, 7, :, W - 1] = 255; z[:, 7] = 0; t[:, 7, 0] = 0
    b = int(rng.integers(0, 2))
    for r in range(N):
        if (r + b) & 1: L[r, 7, K - 1] = 1
    return pack(X, L, z, t)
def setup_inputs_corners(rng):
    X, L, z, t = parts(rng); t = rng.integers(100, 3600, (N, 8, RO)); t[:, :, 0] = rng.integers(300, 2000, (N, 8))
    z = np.where(rng.random((N, 8, 1, NB)) < 0.5, 255 * rng.integers(0, 2, (N, 8, 1, NB)), z)
    for r in range(N):
        kinds = rng.permutation(8)
        for g in range(8):
            j = int(kinds[g]); beg = np.zeros(K, np.int64)
            if j == 0: t[r, g, 0] = rng.choice(np.array([300, 4080]))
            elif j == 1: beg[:] = 1; t[r, g, 0] = rng.choice(np.array([0, 3000]))
            elif j == 2: beg[K - 1] = 1
            elif j == 3: beg[1] = 1
            elif j == 4: beg[::2] = 1
            elif j == 5: beg[::3] = 1
            elif j == 6:
                c = np.add.accumulate(rng.choice(np.array([1, 2, 3, 4, 5, 15, 16, 17, 64, 255, 256, 257]), K)); beg[c[c < K]] = 1
            else: beg[K // 2 + 1] = 1
            beg[0] = 1; cl = np.add.accumulate(beg) & 1
            bit = rng.integers(0, 2, W); bit[0] = 0; bit[W - 1] = 1
            X[r, g] = rng.integers(0, 16, (16, W)) + 240 * bit
            a0 = np.flatnonzero(bit == 0); a1 = np.flatnonzero(bit == 1)
            n = np.where(cl == 1, a1[rng.integers(0, len(a1), K)], a0[rng.integers(0, len(a0), K)])
            L[r, g] = np.where(rng.random(K) < 0.2, (W - 1) * cl, n)
    return pack(X, L, z, t)
def late(rng, X, L, z, t, dg):
    k = np.arange(K); c = np.arange(W); h = B * (D - 1)
    n = 32 * int(rng.integers(0, 9)) + int(rng.integers(8, 25)); R = np.zeros(K, np.int64); R[rng.permutation(K)[:n]] = 1
    for g in range(8):
        r = (g - dg) % N
        a = 8 * rng.integers(0, 17, (8, 1)); e = 8 * rng.integers(4, 11, (8, 1)); v = 8 * rng.integers(4, 26, (7, 1)); q = int(np.sum(e))
        X[r, g] = np.concatenate([a + e * (((c >> h) & 1) ^ rng.integers(0, 2, (8, 1))), v * ((c >> (h + 1)) & 1), np.full((1, W), 4)])
        z[r, g, 8:15] = v * (g & 1)
        m = rng.integers(0, W, K)
        for j in range(D): m = (m & ~(1 << (B * j))) | ((k & 1) << (B * j))
        m = m & ~4
        L[r, g] = (m & ~(2 << h)) | (((g & 1) ^ R) << (h + 1))
        t[r, g, 0] = rng.integers(0, q); t[r, g, 1] = q - 1 - (n & 31); t[r, g, 2:] = q - rng.integers(1, 9, RO - 2)
def few(rng, X, L, z, t, dg):
    k = np.arange(K); c = np.arange(W); h = B * (D - 1); o = int(rng.integers(0, 8))
    rows = 16 * rng.permutation(NB)[:3] + rng.integers(0, 16, 3)
    b = np.zeros((8, 3), np.int64)
    for j, st in enumerate(((0, 3), (0, 3), (0, 5))):
        for s in st: b[(s + o) % 8, j] = 1; b[(s + 1 + o) % 8, j] = 1
    zb = b * (RO & 1); w = b; u = zb; n = np.zeros((8, RO), np.int64)
    for rnd in range(1, RO):
        take = (w != u) & (np.roll(w, 1, axis=0) == u); w = np.where(take, u, w); u = np.abs(w - u); n[:, rnd] = np.add.reduce(take.astype(np.int64), axis=1)
    for g in range(8):
        r = (g - dg) % N
        a = 8 * rng.integers(0, 2, (11, 1)); e = 8 * rng.integers(24, 31, (11, 1)); v = 8 * rng.integers(4, 26, (4, 1)); q = int(np.sum(e))
        X[r, g] = np.concatenate([a + e * (((c >> h) & 1) ^ rng.integers(0, 2, (11, 1))), v * ((c >> (h + 1)) & 1), np.full((1, W), 4)])
        zz = z[r, g]; zz[11:15, rows >> 4] = v * zb[g]
        bt = np.zeros(K, np.int64); bt[rows] = b[g]
        L[r, g] = (rng.integers(0, W, K) & ~(3 << h) & ~4) | ((k & 1) << h) | (bt << (h + 1))
        t[r, g, 0] = rng.integers(0, q); t[r, g, 1:] = q - 1 - n[g, 1:]; t[r, g, RO - 1] = q - max(int(n[g, RO - 1]), 1)
def setup_inputs_crowd(rng):
    X = rng.integers(0, 8, (N, 8, 16, W)); z = rng.integers(0, 8, (N, 8, 16, NB)); L = np.zeros((N, 8, K), np.int64)
    t = rng.choice(np.array([0, 10, 20]), (N, 8, RO)); t[:, :, 0] = 0; rep = (W - 1) // (2 ** B - 1)
    dg = int(rng.integers(0, N))
    for r in range(N):
        kinds = rng.permutation(np.array([0, 1, 2, 3, 4, 0, 1, 4])[:8 - 8 // N]); i = 0
        for g in range(8):
            if (g - r) % N == dg: continue
            p = g & 1; ds = np.arange(p + 2, 2 ** B, 2); xv = X[r, g]; kind = int(kinds[i]); i += 1
            xv[:, ds * rep] = rng.integers(128, 256, (16, len(ds))); xv[0, ds * rep] = 128 + ds
            if kind == 4:
                e = ds[rng.integers(0, len(ds), NB)] * rep; L[r, g] = np.repeat(e, 16); z[r, g] = xv[:, e]
            else:
                d = ds[rng.integers(0, len(ds), K)] * rep
                if kind > 0:
                    k0 = (K - 1, 0, int(rng.integers(1, K - 1)))[kind - 1]; d[k0] = p * rep; z[r, g, :, k0 // 16] = xv[:, p * rep]
                L[r, g] = d
    late(rng, X, L, z, t, dg)
    return pack(X, L, z, t)
def setup_inputs_ties(rng):
    X, L, z, t = parts(rng); odd = int(rng.integers(0, 2)); dg = int(rng.integers(0, N))
    for r in range(N):
        ring = np.flatnonzero((np.arange(8) - r) % N == dg); rest = rng.permutation(np.setdiff1d(np.arange(8), ring))
        p = np.concatenate([rest[:-1], ring, rest[-1:]]); tv = rng.permutation(np.array([0, 31, 4079, int(rng.integers(32, 4079))]))
        for i in range(4):
            g = int(p[i]); T = int(tv[i]); a = T // 16 + (np.arange(16) < T % 16); b = a + (np.arange(16) == T % 16)
            v = np.stack([np.zeros(16, np.int64), a, b])[:, rng.permutation(16)]
            X[r, g] = v[rng.integers(0, 3, W)].T
            t[r, g, 0] = T; t[r, g, 1:] = np.maximum(T - rng.integers(0, 32, RO - 1), 0)
        for i in range(4, 8):
            g = int(p[i]); c = np.arange(W); t[r, g] = rng.integers(700, 1300, RO)
            if i == 7:
                up = (r + odd) & 1; X[r, g] = 255 * up; z[r, g] = 255 * (1 - up)
                X[r, g, rng.integers(0, 16, W), c] += (1 - 2 * up) * rng.integers(0, 2, W)
                continue
            base = rng.integers(0, 201, 16)
            X[r, g] = base[(np.arange(16)[:, None] + rng.integers(0, 16, W)[None, :]) % 16]
            X[r, g, rng.integers(0, 16, W), c] += rng.integers(0, 2, W)
            z[r, g] = 255 * rng.integers(0, 2, (1, NB))
    few(rng, X, L, z, t, dg)
    return pack(X, L, z, t)
def check_inputs(d):
    bad = []
    for k, lo, hi in (("x0", 0, 255), ("l0", 0, W - 1), ("z0", 0, 255), ("th", 0, 4080)):
        v = np.asarray(d[k]).astype(np.float64)
        if not (np.min(v) >= lo and np.max(v) <= hi): bad.append("range of " + k)
        elif not np.all(v == np.floor(v)): bad.append("whole numbers in " + k)
    return bad
def reference(x0, l0, z0, th):
    X = x0.astype(np.float32).astype(np.int32).reshape(N, 8, 16, W); z = z0.astype(np.float32).astype(np.int32).reshape(N, 8, 16, NB)
    L = np.stack([gentries(a) for a in l0]).astype(np.int64); t = th.astype(np.int64); k = np.arange(K)
    x = np.take_along_axis(X, L[:, :, None, :], 3); A = np.zeros((N, 8), np.int64); low = 2 ** B - 1
    for rnd in range(RO):
        beg = np.ones((N, 8, K), bool)
        beg[..., 1:] = np.add.reduce(np.abs(x[..., 1:] - x[..., :-1]), axis=2) > (t[:, :, rnd] + (A & 31))[..., None]
        beg[..., 0] = True
        s = np.maximum.accumulate(np.where(beg, k, 0), axis=2)
        nx = np.minimum.accumulate(np.where(beg, k, K)[..., ::-1], axis=2)[..., ::-1]
        ln = np.concatenate([nx[..., 1:], np.full((N, 8, 1), K)], axis=2) - s
        P = np.zeros((N, 8, K), np.int64)
        for c in range(D):
            q = D * (k - s) + c; pl = np.zeros((N, 8, K), np.int64)
            for j in range(1, D): pl = pl + (q >= j * ln)
            P = (P << B) | ((np.take_along_axis(L, s + q - pl * ln, 2) >> (B * (D - 1 - pl))) & low)
        hi = np.roll(P >> (B * (D - 1)), (1, 1), axis=(0, 1)); lo = np.roll(P & low, (2, 2), axis=(0, 1))
        M = (hi << (B * (D - 1))) | (((P >> B) & (2 ** (B * (D - 2)) - 1)) << B) | lo
        y = np.take_along_axis(X, P[:, :, None, :], 3); y2 = np.take_along_axis(X, M[:, :, None, :], 3); zr = np.repeat(z, 16, axis=3)
        took = np.add.reduce(np.abs(y2 - zr), axis=2) < np.add.reduce(np.abs(y - zr), axis=2)
        L = np.where(took, M, P); x = np.where(took[:, :, None, :], y2, y); A = np.add.reduce(took.astype(np.int64), axis=2)
        Y = np.max(x.reshape(N, 8, 16, NB, 16), axis=4)
        if rnd < RO - 1:
            col = S * np.arange(NB) + (np.add.reduce(Y, axis=2) & (S - 1))
            np.put_along_axis(X, col[:, :, None, :].astype(np.int64), (Y + z) >> 1, 3)
        z = np.abs(Y - z)
    return {"ly": np.stack([gtable(a) for a in L]).astype(np.float32), "xy": x.reshape(N, 128, K).astype(np.float32).astype(BF), "zy": z.reshape(N, 128, NB).astype(np.float32).astype(BF)}

@@ -1,0 +1,756 @@
+from concourse.bass import DstId, RemoteDMATransfer
+from concourse.mybir import AluOpType, AxisListType, ActivationFunctionType
+
+F32, BF, I32, U16 = "float32", "bfloat16", "int32", "uint16"
+RO = 4
+BIG = 2.0 ** 21
+SEC = 2064
+POF = 65 * 160.0
+MID = 224.0
+MH = 32
+MA = 24
+ZN = 4
+CH = (("A", 0, 24), ("V", 96, 128), ("V", 64, 96), ("V", 40, 64), ("V", 24, 40))
+RR = ()
+CD = (("A", 0, 24), ("V", 96, 128), ("V", 64, 96), ("V", 40, 64), ("V", 24, 40))
+RD = ()
+DL, CF = "v", "v"
+HS = (("d1", 64, 128), ("d0", 0, 64))
+DC = (("dfa", 96, 128), ("dfb", 64, 96), ("dfa", 40, 64), ("dfb", 16, 40), ("d0", 0, 16))
+SM = 64
+E0 = (("a", 94, 128), ("v", 62, 94), ("v", 38, 62), ("v", 14, 38), ("a", 0, 14))
+CNT = "a"
+FM = "a"
+BS = 64
+EA = 64
+EV = 48
+EC = (("a", 94, 128), ("v", 62, 94), ("v", 38, 62), ("v", 14, 38), ("a", 0, 14))
+EL = (("a", 0, 32), ("v", 96, 128), ("a", 32, 64), ("v", 76, 96), ("a", 64, 76))
+RATES = ((0.1, 0.04, 1.25, 1.56, 3.8, 0.5e-3, 2.5), (0.06, 0.03, 1.1, 1.25, 2.5, 0.42e-3, 2.0),
+         (0.12, 0.04, 1.35, 1.85, 5.0, 0.7e-3, 3.0))
+LOOK, ITER = 0.5, 3000
+SPAN = []
+ORDER = []
+
+SB = {
+    "tab": (4096, BF), "win": (16 + 3 * SEC, BF), "xs": (2048, BF), "ab": (2048, BF), "dd": (2048, BF),
+    "a2": (2048, BF), "zrep": (2048, BF), "emat": (2048, BF), "g2": (2048, BF), "ysc": (2048, BF),
+    "l0s": (128, I32), "zs": (128, BF), "zd": (128, BF), "zt": (128, BF), "ths": (4, I32), "thf": (4, F32), "thc": (4, F32),
+    "pi": (8, I32), "pf": (12, F32), "kt": (256, BF), "vv": (128, F32), "xi": (160, F32), "x16": (128, F32), "xr": (128, F32), "selr": (36, F32),
+    "s2p": (16, BF), "s2n": (16, BF), "one": (128, BF), "hl": (256, BF), "dl": (256, BF),
+    "took0": (256, BF), "took1": (256, BF), "uu0": (256, BF), "uu1": (256, BF),
+    "zp": (144, BF), "zn": (144, BF), "ib": (128, BF), "ibn": (128, BF), "i64": (128, BF), "i32n": (128, F32),
+    "bp": (128, F32), "bn": (128, F32), "e8": (128, F32), "sel": (20, BF), "cm": (34, BF), "m0": (128, BF),
+    "kf": (128, F32), "k2": (128, F32), "cf": (145, F32), "cb": (145, F32),
+    "oi": (64, I32), "o1": (16, U16), "o2": (8, U16), "o3": (16, U16), "o4": (8, U16), "ci": (8, I32),
+    "tin": (256, F32), "tout": (256, F32), "nm": (128, F32), "nl": (128, F32),
+    "oe": (128, U16), "ob": (128, U16), "op_": (128, U16), "om": (128, U16), "osc": (8, U16),
+    "tq": (128, F32), "h64": (128, F32), "hi": (128, BF), "lo": (128, BF), "lq": (128, F32),
+    "sc1": (290, F32), "cy": (2, F32), "ne": (129, F32), "ll": (128, F32), "t2": (128, I32), "mm_": (128, F32),
+    "of": (128, F32), "fa": (128, F32), "fb": (128, F32), "fm": (128, F32), "fix": (128, BF),
+    "ps": (128, F32), "took": (128, BF), "ac": (2, F32), "acb": (128, BF), "qb": (128, BF), "thb": (512, F32),
+    "ui": (16, I32), "uj": (8, I32), "sh": (128, I32), "k256": (128, F32), "imid": (128, BF), "i32b": (128, BF),
+    "bb": (128, BF), "bbn": (128, BF), "ya": (2048, BF), "yb": (2048, BF), "de": (2048, BF), "a3": (2048, BF), "m5": (512, BF),
+}
+for _t in range(RO):
+    SB["snd%d" % _t] = (304, BF)
+    SB["lnd%d" % _t] = (256, BF)
+PS = ["dfa", "dfb", "gg", "wk", "dg", "pm", "d0", "d1"]
+SCRATCH = {k: ("sbuf", [128, v[0]], v[1]) for k, v in SB.items()}
+for _p in PS:
+    SCRATCH[_p] = ("psum", [128, 512], F32)
+SEMAPHORES = ["sv", "sa", "sp", "sg", "l_l", "l_t", "l_z", "l_h", "sent", "out"]
+SEMAPHORES += ["w%d" % t for t in range(RO)] + ["arr%d" % t for t in range(RO)]
+ESEM = {"v": "sv", "a": "sa", "p": "sp", "g": "sg"}
+
+
+def masks(topo, src, dsts):
+    lists = [topo.engines(src, d) for d in dsts]
+    a, b = lists
+    if a == b:
+        h = len(a) // 2
+        a, b = a[:h], a[h:]
+    elif len(a) > len(b):
+        a = [e for e in a if e not in b]
+    else:
+        b = [e for e in b if e not in a]
+    return [(sum(1 << e for e in x), len(x)) for x in (a, b)]
+
+
+def arrange(ops):
+    n = len(ops)
+    qs = [o["q"] for o in ops]
+    dep = [list(o["dep"].items()) for o in ops]
+    suc = [o["suc"] for o in ops]
+    tabs = []
+    for hop, fix, kf, gat, sca, pec, rem in RATES:
+        d = [o["c"][0] + o["c"][1] * fix + (o["c"][2] * kf + o["c"][3] * gat + o["c"][4] * sca) * 0.83e-3
+             + o["c"][5] * pec * kf for o in ops]
+        lat = [rem if o["dma"] == "remote" else o["lat"] for o in ops]
+        tabs.append((d, lat, hop))
+
+    def span(order, tab):
+        d, lat, hop = tab
+        end = [0.0] * n
+        free = {}
+        top = 0.0
+        for i in order:
+            st = free.get(qs[i], 0.0)
+            for j, k in dep[i]:
+                e = end[j] + (lat[j] + hop) * k
+                if e > st:
+                    st = e
+            end[i] = free[qs[i]] = st + d[i]
+            if end[i] + lat[i] > top:
+                top = end[i] + lat[i]
+        return top
+
+    d, lat, hop = tabs[0]
+    pri = [0.0] * n
+    for i in range(n - 1, -1, -1):
+        pri[i] = d[i] + max([lat[i]] + [(lat[i] + hop) * k + pri[j] for j, k in suc[i]])
+    free = {q: 0.0 for q in set(qs)}
+    left = [len(x) for x in dep]
+    est = [0.0] * n
+    ready = {q: [] for q in sorted(free)}
+    for i in range(n):
+        if not left[i]:
+            ready[qs[i]].append(i)
+    order = []
+    while len(order) < n:
+        t0, q = min((min(max(free[q], est[i]) for i in r), q) for q, r in ready.items() if r)
+        first = min(ready[q], key=lambda i: (max(free[q], est[i]), -pri[i]))
+        i = max((i for i in ready[q] if est[i] <= t0 + LOOK * d[first]), key=lambda i: pri[i])
+        ready[q].remove(i)
+        free[q] = max(free[q], est[i]) + d[i]
+        order.append(i)
+        for j, k in suc[i]:
+            est[j] = max(est[j], free[q] + (lat[i] + hop) * k)
+            left[j] -= 1
+            if not left[j]:
+                ready[qs[j]].append(j)
+    base = [span(order, tb) for tb in tabs]
+    cur = float(len(tabs))
+    seed = 12345
+    for _it in range(ITER):
+        seed = (seed * 1103515245 + 12345) % 2147483648
+        a = (seed >> 8) % n
+        i = order[a]
+        seed = (seed * 1103515245 + 12345) % 2147483648
+        step = 1 + (seed >> 10) % 3
+        fwd = (seed >> 20) & 1
+        block = set(j for j, _k in (suc[i] if fwd else dep[i]))
+        b = a
+        while step:
+            nb = b + 1 if fwd else b - 1
+            if nb < 0 or nb >= n or order[nb] in block:
+                break
+            b = nb
+            if qs[order[b]] == qs[i]:
+                step -= 1
+                if not step:
+                    break
+        if step and not any(qs[x] == qs[i] for x in order[min(a, b):max(a, b) + 1] if x != i):
+            if b == a:
+                continue
+        cand = list(order)
+        cand.pop(a)
+        cand.insert(b, i)
+        val = sum(span(cand, tb) / bs for tb, bs in zip(tabs, base))
+        if val <= cur + 1e-9:
+            cur, order = val, cand
+    SPAN[:] = [base, [span(order, tb) for tb in tabs]]
+    return order
+
+
+def rank_program(g, core, T, topo):
+    rank = T.rank_of(core)
+    if rank is None:
+        return
+    n = len(T.cores)
+    Q = {"v": g.vector, "a": g.scalar, "p": g.tensor, "g": g, "s": g.sync}
+    AL, AF = AluOpType, ActivationFunctionType
+    ops = []
+
+    def A(name, a=0, b=None, s=1, p=None):
+        w = 512 if name in PS else SB[name][0]
+        if b is None:
+            b = w
+        rows = slice(None) if p is None else slice(*p)
+        reg = [(name, a, b, len(range(a, b, abs(s))))]
+        if s < 0:
+            return T[name][rows, slice(b - 1, a - 1 if a > 0 else None, s)], reg
+        if s == 1:
+            return T[name][rows, a:b], reg
+        return T[name][rows, a:b:s], reg
+
+    def IND(name, w, off, c, d):
+        return T[name][:, 0:w].indirect(T[off][:, c:d]), [(name, 0, w), (off, c, d)]
+
+    def sc(x):
+        return (x, []) if not isinstance(x, tuple) else x
+
+    def add(q, fn, reads, writes, dma=None, ext=None, cost=None):
+        lat = 0.0
+        if dma == "remote":
+            d = (0.5, 0, 0, 0, 0, 0)
+        elif dma:
+            d, lat = (0.06, 0, 0, 0, 0, 0), {"l_t": 6.5, "out": 2.6}.get(dma, 2.5)
+        elif q == "p":
+            d, lat = (0, 0, 0, 0, 0, cost), 0.06
+        else:
+            ind = [x for x in reads if SB.get(x[0], (0, 0))[1] == U16 and x[2] - x[1] > 1]
+            if ind:
+                k = 16 * (ind[0][2] - ind[0][1])
+                d = (0.06, 0, 0, 0, k, 0) if writes[0][0] == "tab" else (0.06, 0, 0, k, 0, 0)
+            else:
+                nel = writes[0][3] if len(writes[0]) > 3 else writes[0][2] - writes[0][1]
+                if nel == 1 and reads:
+                    nel = reads[0][2] - reads[0][1]
+                big = [x for x in reads + writes if x[2] - x[1] >= nel]
+                if q == "g":
+                    d = (0.15, 0, 2 * nel, 0, 0, 0)
+                else:
+                    two = all(SB.get(x[0], (0, 0))[1] in (BF, U16) for x in big)
+                    rate = 0.5 if two and q == "v" else 1.0
+                    if cost == "tt" and not any(x[0] in PS for x in reads):
+                        rate *= 2
+                    d = (0, 1, max(64, nel * rate), 0, 0, 0)
+        ops.append({"q": q, "fn": fn, "r": [x[:3] for x in reads], "w": [x[:3] for x in writes], "dma": dma,
+                    "ext": ext, "c": d, "lat": lat})
+
+    def tt(o, a, b, op):
+        add("v", lambda: g.vector.tensor_tensor(o[0], a[0], b[0], op), a[1] + b[1], o[1], cost="tt")
+
+    def ts(o, a, s1, op0, s2=None, op1=None):
+        s1, s2 = sc(s1), sc(s2)
+        if op1 is None:
+            add("v", lambda: g.vector.tensor_scalar(o[0], a[0], s1[0], None, op0), a[1] + s1[1], o[1])
+        else:
+            add("v", lambda: g.vector.tensor_scalar(o[0], a[0], s1[0], s2[0], op0, op1), a[1] + s1[1] + s2[1], o[1])
+
+    def cp(o, a):
+        add("v", lambda: g.vector.tensor_copy(o[0], a[0]), a[1] + o[1][1:], o[1][:1])
+
+    def ms(o, v):
+        add("v", lambda: g.vector.memset(o[0], v), [], o[1])
+
+    def scan(o, a, b, init, op0, op1):
+        add("v", lambda: g.vector.tensor_tensor_scan(o[0], a[0], b[0], init, op0, op1), a[1] + b[1], o[1])
+
+    def red(o, a, op, neg=False):
+        if neg:
+            add("v", lambda: g.vector.tensor_reduce(o[0], a[0], AxisListType.X, op, negate=True), a[1], o[1])
+        else:
+            add("v", lambda: g.vector.tensor_reduce(o[0], a[0], AxisListType.X, op), a[1], o[1])
+
+    def trn(o, a):
+        add("v", lambda: g.vector.transpose(o[0], a[0]), a[1], o[1])
+
+    def act(o, a, f, bias=0.0, scale=1.0):
+        bias = sc(bias)
+        add("a", lambda: g.scalar.activation(o[0], a[0], f, bias=bias[0], scale=scale), a[1] + bias[1], o[1])
+
+    def mm(lst, ext=None, cost=None):
+        def fn():
+            r = None
+            for o, l, rr, st, sp in lst:
+                r = g.tensor.matmul(o[0], l[0], rr[0], st, sp)
+            return r
+        add("p", fn, [x for e in lst for x in e[1][1] + e[2][1]], [x for e in lst for x in e[0][1]], ext=ext,
+            cost=cost or sum(max(64, e[2][1][0][3]) * (4 if SB[e[1][1][0][0]][1] == F32 else 1) for e in lst))
+
+    def iota(o, pat, base, cm, fl=True):
+        if fl:
+            add("g", lambda: g.iota(o[0], pat, base, cm, allow_small_or_imprecise_dtypes=True), [], o[1])
+        else:
+            add("g", lambda: g.iota(o[0], pat, base, cm), [], o[1])
+
+    def dma(q, o, a, sem):
+        add(q, lambda: Q[q].dma_start(o[0], a[0]), a[1], o[1], dma=sem)
+
+    def gat(e, o, src):
+        if e == "v":
+            cp(o, src)
+        else:
+            act(o, src, AF.Copy)
+
+    def col(name, c, p=None):
+        return A(name, c, c + 1, p=p)
+
+    dma("s", A("l0s"), (T.l0[:], []), "l_l")
+    dma("s", A("tab"), (T.x0[:], []), "l_t")
+    dma("a", A("ths", p=(0, 8)), (T.th[:], []), "l_h")
+    dma("a", A("zs"), (T.z0[:], []), "l_z")
+
+    iota(col("pi", 0), [[0, 1]], 0, 1, False)
+    iota(A("oi", 0, 16), [[1, 8], [0, 2]], 0, 8, False)
+    iota(A("xi"), [[1, 160]], 0, 0)
+    ms(A("win", 16 + SEC, 16 + 2 * SEC), MID)
+    ts(col("pi", 1), col("pi", 0), 15, AL.bitwise_and)
+    ts(A("oi", 16, 32), A("oi", 0, 16), 127, AL.bitwise_and)
+    ts(col("pi", 2), col("pi", 0), 31, AL.bitwise_and)
+    cp(A("o1"), A("oi", 16, 32))
+    cp(A("pf", 0, 3), A("pi", 0, 3))
+    ts(A("tq", 0, 8), A("xi", 0, 8), 32.0, AL.mult, col("pf", 2), AL.add)
+    cp(A("o2"), A("tq", 0, 8))
+    iota(A("x16"), [[16, 8], [0, 16]], 0, 0)
+    iota(A("xr"), [[0, 8], [1, 16]], 0, 0)
+    iota(A("selr", 0, 1), [[0, 1]], 112, 0)
+    iota(A("selr", 1, 9), [[16, 8]], 0, 0)
+    iota(A("selr", 9, 11), [[16, 2]], 97, 0)
+    iota(A("selr", 11, 19), [[16, 8]], 1, 0)
+    iota(A("selr", 20, 36), [[0, 2], [16, 8]], 0, 0)
+    add("g", lambda: g.affine_select(T.emat[:], T.win[:, 16 + SEC:16 + SEC + 2048], [[-1, 8], [0, 16], [-8, 16]],
+                                     AL.is_equal, 0.0, 0, 1), [("win", 16 + SEC, 16 + 2 * SEC)], [("emat", 0, 2048)])
+    tt(col("pf", 3), col("pf", 0), col("pf", 1), AL.subtract)
+    ts(col("pf", 4), col("pf", 1), 128.0, AL.mult)
+    ts(col("pf", 5), col("pf", 3), 15.0, AL.add)
+    ts(col("pf", 6), col("pf", 0), 16.0, AL.mult)
+    ts(col("pf", 8), col("pf", 0), 256.0, AL.mult)
+    ts(A("kf"), A("xi", 0, 128), col("pf", 4), AL.add)
+    ms(A("win", 0, 16 + SEC), 0.0)
+
+    def names_from_input():
+        cp(A("tin"), IND("l0s", 128, "o1", 0, 16))
+        trn(A("tout"), A("tin"))
+        cp(A("nm"), IND("tout", 256, "o2", 0, 8))
+        cp(A("oe"), A("nm"))
+
+    def digits(t):
+        act(A("hl", 0, 128), A("nm"), AF.Identity, bias=160 - 31.5 / 64, scale=1.0 / 64)
+        act(A("h64"), A("hl", 0, 128), AF.Identity, bias=POF, scale=-64.0)
+        tt(A("hl", 128, 256), A("nm"), A("h64"), AL.add)
+
+    names_from_input()
+    ms(A("win", 16 + 2 * SEC, 16 + 3 * SEC), 0.0)
+    digits(0)
+    ts(A("k256"), A("kf"), 256.0, AL.mult, -160.0, AL.add)
+    ts(A("ib"), A("xi", 0, 128), col("pf", 0), AL.is_equal)
+    ts(A("ibn"), A("xi", 0, 128), col("pf", 0), AL.is_equal, -1.0, AL.mult)
+    ts(A("e8", p=(0, 8)), A("x16", p=(0, 8)), col("pf", 6, (0, 8)), AL.is_equal)
+    cp(A("thf", p=(0, 8)), A("ths", p=(0, 8)))
+    mm([(A("d0", 0, 4), A("e8", p=(0, 8)), A("thf", p=(0, 8)), True, True)])
+    ts(A("i32n"), A("xi", 0, 128), col("pf", 0), AL.is_equal, -BIG, AL.mult)
+    ts(A("zp"), A("xi", 0, 144), col("pf", 5), AL.is_equal, BIG, AL.mult)
+    ts(A("thc", 0, 1), A("d0", 0, 1), 0.5, AL.add)
+    ts(A("thc", 1, 4), A("d0", 1, 4), 5120.5, AL.add)
+    for t in range(RO):
+        act(A("thb", 128 * t, 128 * t + 128), A("kf"), AF.Identity, bias=col("thc", t), scale=0.0)
+    ms(col("ab", 0), 512.0)
+
+    def late_constants():
+        ts(A("s2p"), A("selr", 20, 36), col("pf", 3), AL.is_equal)
+        ts(A("s2n"), A("selr", 20, 36), col("pf", 3), AL.is_equal, -1.0, AL.mult)
+        ms(A("one"), 1.0)
+        for nm_ in ("took0", "took1", "uu0", "uu1"):
+            ms(A(nm_), 0.0)
+        ts(A("kt", 0, 128), A("xr"), 32768.0, AL.mult)
+        ts(A("kt", 128, 256), A("xr"), 0.0, AL.mult, col("pf", 8), AL.add)
+        ts(A("i64"), A("xi", 0, 128), col("pf", 0), AL.is_equal, 64.0, AL.mult)
+        ts(A("imid"), A("xi", 0, 128), col("pf", 0), AL.is_equal, -MID, AL.mult)
+        ts(A("i32b"), A("xi", 0, 128), col("pf", 0), AL.is_equal, 32 * BIG, AL.mult)
+        ts(A("bp"), A("x16"), col("pf", 3), AL.is_equal)
+        ts(A("bn"), A("x16"), col("pf", 3), AL.is_equal, -1.0, AL.mult)
+        ts(A("bb"), A("x16"), col("pf", 3), AL.is_equal)
+        ts(A("bbn"), A("x16"), col("pf", 3), AL.is_equal, -BIG, AL.mult)
+        ts(A("sel", 0, 19), A("selr", 0, 19), col("pf", 0), AL.is_equal)
+        ts(A("cf", 128, 145), A("xi", 0, 17), col("pf", 1), AL.is_le, BIG, AL.mult)
+        ts(A("cb", 0, 17), A("xi", 0, 17), col("pf", 1), AL.is_gt, BIG, AL.mult)
+        ts(A("cb", 17, 145), A("kf"), -1.0, AL.mult, 2 * SEC + 0.25, AL.add)
+        ts(A("k2"), A("kf"), 2.0, AL.mult, 2.0 - 2 * SEC, AL.add)
+        ts(A("cm", 0, 17), A("xi", 0, 17), col("pf", 1), AL.is_ge, -BIG, AL.mult)
+        ts(A("cm", 17, 33), A("xi", 0, 16), col("pf", 1), AL.is_le, BIG, AL.mult)
+        ts(A("m0"), A("xr"), 0.0, AL.is_gt)
+        ms(A("gg", 0, 17), -BIG)
+        ms(A("gg", 145, 162), -BIG)
+        ms(A("pm", 289, 290), -(2 * SEC - 2048 + 0.25))
+
+    def last_constants():
+        ts(A("tq", 0, 8), A("xi", 0, 8), 16.0, AL.mult, col("pf", 1), AL.add)
+        cp(A("o3", 0, 16, 2), A("tq", 0, 8))
+        cp(A("o3", 1, 16, 2), A("tq", 0, 8))
+        ts(col("pi", 3), col("pi", 0), 7, AL.bitwise_and)
+        ts(col("pi", 4), col("pi", 0), 3, AL.logical_shift_right, 1, AL.bitwise_and)
+        ts(col("pi", 5), col("pi", 0), 16, AL.bitwise_and)
+        ts(col("pi", 6), col("pi", 3), 32.0, AL.mult)
+        tt(col("pi", 7), col("pi", 4), col("pi", 5), AL.add)
+        tt(col("pf", 7), col("pi", 6), col("pi", 7), AL.add)
+        ts(A("tq", 8, 16), A("xi", 0, 8), 2.0, AL.mult, col("pf", 7), AL.add)
+        cp(A("o4"), A("tq", 8, 16))
+        for c in range(4):
+            act(A("m5", 128 * c, 128 * c + 128), A("m0"), AF.Copy)
+
+    def scatter_constants():
+        ts(A("tq", 16, 24), A("xi", 0, 8), 16.0, AL.mult, col("pf", 1), AL.add)
+        ts(A("ci"), A("tq", 16, 24), 32.0, AL.mult)
+
+    def zl(name, j):
+        return A(name, 15 - j, 143 - j)
+
+    def sums(out, c0, lname, src, m0, m1, start, stop):
+        mm([(A(out, c0, c0 + m1 - m0), zl(lname, j), A(src, 16 * m0 + j, 16 * (m1 - 1) + j + 1, 16),
+             start and j == 0, stop and j == 15) for j in range(16)])
+
+    def threshold(t):
+        mm([(A("gg", 17, 145), A("i32n"), A("thb", 128 * t, 128 * t + 128), True, False)])
+
+    def count():
+        mm([(A("d1", 256, 384), A("took%d" % i, 0, 128), A("one"), i == 0, i == len(HS) - 1)
+            for i, (_b, m0, m1) in enumerate(HS)])
+        if CNT[0] == "a":
+            act(A("acb"), A("d1", 256, 384), AF.Copy)
+        else:
+            cp(A("acb"), A("d1", 256, 384))
+        mm([(A("d1", 128, 256), A("bb"), A("acb"), True, True)])
+
+    def count2():
+        if CNT[-1] == "a":
+            act(A("qb"), A("d1", 128, 256), AF.Identity, bias=160 - 15.5 / 32, scale=1.0 / 32)
+        else:
+            ts(A("qb"), A("d1", 128, 256), 1.0 / 32, AL.mult, 160 - 15.5 / 32, AL.add)
+        mm([(A("gg", 17, 145), A("bbn"), A("acb"), False, False), (A("gg", 17, 145), A("i32b"), A("qb"), False, False)])
+
+    def diff(bank, a, b):
+        lst = []
+        if a == 0:
+            lst += [(A(bank, 1, 16), A("ib"), A("xs", 1, 16), True, False),
+                    (A(bank, 1, 16), A("ibn"), A("xs", 2032, 2047), False, True)]
+        a1 = max(a, 16)
+        lst += [(A(bank, a1 - a, b - a), A("ib"), A("xs", a1, b), True, False),
+                (A(bank, a1 - a, b - a), A("ibn"), A("xs", a1 - 16, b - 16), False, True)]
+        mm(lst)
+        a2 = max(a, 1)
+        act(A("ab", a2, b), A(bank, a2 - a, b - a), AF.Abs)
+
+    def diffs():
+        for bank, m0, m1 in DC:
+            diff(bank, 16 * m0, 16 * m1)
+            if m0 == SM:
+                sums("gg", 17 + SM, "zp", "ab", SM, 128, False, False)
+
+    def egather(e, m0, m1):
+        gat(e, A("xs", 16 * m0, 16 * m1), IND("tab", 4096, "oe", m0, m1))
+
+    def z_t():
+        mm([(A("d0", 128, 256), A("zs"), A("ib"), True, True)])
+        act(A("zt"), A("d0", 128, 256), AF.Copy)
+
+    def z_rep(cs):
+        w = 16 * (128 - MA) // ZN
+        for c in cs:
+            bank = "dfa" if c & 1 else "dfb"
+            a = 16 * MA + w * c
+            mm([(A(bank, 0, w), A("zt"), A("emat", a, a + w), True, True)])
+            act(A("zrep", a, a + w), A(bank, 0, w), AF.Copy, scale=1.0 / MID)
+
+    def block_max(js):
+        for j in js:
+            scan(A("ysc", 128 * j, 128 * j + 128), A("m0", 0, 128), A("xs", j, 2048, 16), 0.0, AL.mult, AL.max)
+
+    YY = A("ysc", 15, 2048, 16)
+
+    def blocks_a():
+        mm([(A("d0", 128, 256), YY, A("ib"), True, False), (A("d0", 128, 256), A("zs"), A("ibn"), False, True)])
+        act(A("zt"), A("d0", 128, 256), AF.Abs)
+        mm([(A("d1", 128, 256), A("ib"), YY, True, False), (A("d1", 128, 256), A("ibn"), A("zs"), False, True),
+            (A("d1", 256, 384), A("ib"), YY, True, False), (A("d1", 256, 384), A("ib"), A("zs"), False, True)])
+
+    def blocks_u():
+        mm([(A("d1", 8, 16), zl("zp", r), A("ysc", 15 + 16 * r, 2048, 256), r == 0, r == 15) for r in range(16)])
+        act(A("zs"), A("d1", 128, 256), AF.Abs)
+
+    def blocks_b():
+        ts(A("sh"), A("d1", 256, 384), 0.5, AL.mult, -0.25, AL.add)
+        ts(A("ui", 0, 8), A("d1", 8, 16), 1.0 / BIG, AL.mult)
+        ts(A("ui", 8, 16), A("ui", 0, 8), 31, AL.bitwise_and)
+        tt(A("uj"), A("ui", 8, 16), A("ci"), AL.add)
+        cp(A("osc"), A("uj"))
+        cp(IND("tab", 4096, "osc", 0, 8), A("sh"))
+
+    def periods(mid):
+        mm([(A("pm", 256, 289), A("ib"), A("cm", 0, 33), True, False)])
+        scan(A("sc1", 0, 145), A("gg", 17, 162), A("cf"), 0.0, AL.max, AL.min)
+        scan(A("sc1", 145, 290, -1), A("gg", 0, 145, -1), A("cb", 0, 145, -1), 2 * SEC - 2048 + 0.25, AL.max, AL.min)
+        mm([(A("pm", 256, 289), A("bp"), A("sc1", 128, 161), False, False),
+            (A("pm", 256, 289), A("bn"), A("sc1", 129, 162), False, True)])
+        mid()
+        red(col("cy", 0), A("pm", 256, 272), AL.max)
+        red(col("ne", 128), A("pm", 273, 290), AL.min, True)
+        ts(A("wk", 0, 128), A("sc1", 0, 128), col("cy", 0), AL.max, 1.0 / 256, AL.mult)
+        ts(A("ne", 0, 128), A("sc1", 162, 290), col("ne", 128), AL.max)
+        tt(A("wk", 128, 256), A("k2"), A("wk", 0, 128), AL.subtract)
+        tt(A("wk", 256, 384), A("ne", 1, 129), A("wk", 0, 128), AL.add)
+        tt(A("t2"), A("ne", 1, 129), A("wk", 128, 256), AL.add)
+        ts(A("vv"), A("t2"), 0.0, AL.max, float(SEC), AL.mult)
+        tt(A("mm_"), A("vv"), A("wk", 256, 384), AL.min)
+        tt(A("of"), A("mm_"), A("wk", 128, 256), AL.add)
+        ts(A("ob"), A("of"), 2 * SEC - 2 + 16 + 63.5 / 256, AL.add)
+
+    def fixup():
+        tt(A("wk", 384, 512), A("ne", 1, 129), A("wk", 128, 256), AL.add)
+        if FM == "v":
+            ts(A("fm"), A("vv"), float(SEC), AL.is_equal, 256.0, AL.mult)
+        else:
+            act(A("fa"), A("vv"), AF.Abs, bias=-float(SEC))
+            act(A("fm"), A("fa"), AF.Relu, bias=256.0, scale=-1.0)
+        tt(A("wk", 0, 128), A("t2"), A("wk", 384, 512), AL.subtract)
+        tt(A("fix"), A("fm"), A("wk", 0, 128), AL.mult)
+
+    d1, d2 = T.cores[(rank + 1) % n], T.cores[(rank + 2) % n]
+    mk = masks(topo, core, [d1, d2])
+    s1, s2 = T.cores[(rank - 1) % n], T.cores[(rank - 2) % n]
+    arrive = masks(topo, s1, [core, T.cores[(rank + 1) % n]])[0][1] + masks(topo, s2, [s1, core])[1][1]
+
+    def send(t):
+        snd, lnd = "snd%d" % t, "lnd%d" % t
+
+        def fn():
+            trs = []
+            for d, (m, _c), a, b in ((d1, mk[0], 0, 0), (d2, mk[1], 144, 128)):
+                ad = topo.addr(d)
+                trs.append(RemoteDMATransfer(dst_ids=[DstId(rid=ad[0], pnc=ad[1])], dma_engine_mask=m,
+                                             remote_sem=T.sem["arr%d" % t], src=T[snd][:, a:a + 128],
+                                             dst=T[lnd][:, b:b + 128]))
+            g.remote_dma_fused(trs, local_sem=T.sem.sent)
+            return None
+        add("g", fn, [(snd, 0, 304)], [], dma="remote")
+
+    def distance(off, lname, first, after=None):
+        dd, a2, ya = ("dd", "a2", "ya") if first else ("de", "a3", "yb")
+        other = "s2p" if lname == "s2n" else "s2n"
+        nb = 0
+        for mode, m0, m1 in (CH if first else CD):
+            a, b = 16 * m0, 16 * m1
+            if mode == "A":
+                bank = ("dfa", "dfb")[(nb + first) & 1]
+                nb += 1
+                act(A(ya, a, b), IND("tab", 4096, off, m0, m1), AF.Copy)
+                mm([(A(bank, 0, b - a), A("zt"), A("emat", a, b), True, False),
+                    (A(bank, 0, b - a), A("imid"), A(ya, a, b), False, True)])
+                act(A(a2, a, b), A(bank, 0, b - a), AF.Abs, scale=1.0 / MID)
+                continue
+            tt(A(dd, a, b), IND("tab", 4096, off, m0, m1), A("zrep", a, b), AL.subtract)
+            if mode == "V":
+                act(A(a2, a, b), A(dd, a, b), AF.Abs)
+            else:
+                ts(A(a2, a, b), A(dd, a, b), 0.0, AL.max, 2.0, AL.mult)
+        after()
+        for bank, lo, hi in HS:
+            if first:
+                sums_t(bank, lname, a2, lo, hi, True, False)
+            for m0, m1 in (RR if first else RD):
+                if lo <= m0 < hi:
+                    sums_t(bank, other, dd, m0, m1, False, False)
+            if not first:
+                sums_t(bank, lname, a2, lo, hi, False, True)
+
+    def sums_t(bank, sname, src, m0, m1, start, stop):
+        mm([(A(bank, j, 256, 16, p=(m0, m1)), A(src, 16 * m0 + j, 16 * (m1 - 1) + j + 1, 16), A(sname),
+             start and j == 0, stop and j == 15) for j in range(16)], cost=16 * min(64, m1 - m0))
+
+    def choose(i, last, snd):
+        bank, m0, m1 = HS[i]
+        p = (m0, m1)
+        tk, uu = "took%d" % i, "uu%d" % i
+        ts(A(tk, p=p), A(bank, 0, 256, p=p), 0.0, AL.is_lt)
+        tt(A(uu, p=p), A(tk, p=p), A("dg" if DL == "p" else "dl", 0, 256, p=p), AL.mult)
+        o = A(("pm", "wk")[i], 128 + m0, 128 + m1)
+        mm([(o, A(snd, 16, 144), A("i64", m0, m1), True, False), (o, A(snd, 176, 304), A("ib", m0, m1), False, False)])
+        mm([(o, A(uu, 0, 128), A("i64", m0, m1), False, False), (o, A(uu, 128, 256), A("ib", m0, m1), False, True)])
+        ts(A("nm" if last else "oe", m0, m1), o, -POF, AL.add)
+
+    def new_digits(t, snd):
+        lst = [(A("dg", 0, 128), A(snd, 16, 144), A("ib"), True, False),
+               (A("dg", 128, 256), A(snd, 176, 304), A("ib"), False, False),
+               (A("dg", 256, 384), A(snd, 176, 304), A("ib"), False, False),
+               (A("dg", 256, 384), A("kt", 0, 128), A("ib"), False, False),
+               (A("dg", 256, 384), A("kt", 128, 256), A("ib"), False, False)]
+        for i, (_b, m0, m1) in enumerate(HS):
+            for c, c2 in ((0, 0), (128, 128), (256, 128)):
+                lst.append((A("dg", c + m0, c + m1), A("uu%d" % i, c2, c2 + 128),
+                            A("ib", m0, m1), False, i == len(HS) - 1 and c == 256))
+        if CF == "v":
+            lst = [e for e in lst if e[0][1][0][1] < 256]
+            lst[-1] = lst[-1][:4] + (True,)
+        mm(lst)
+        act(A("hl"), A("dg", 0, 256), AF.Copy)
+        if CF == "p":
+            act(A("cf", 0, 128), A("dg", 256, 384), AF.Identity, bias=-160.0)
+        windows(t)
+
+    def windows(t):
+        w = "w%d" % t
+        for p0, c0, c in ((0, 16, 0), (1, 15, 0), (0, 16 + SEC, 0), (0, 16 + 2 * SEC, 128), (1, 15 + 2 * SEC, 128)):
+            dma("s", A("win", c0, c0 + 2048, p=(p0, 128, 16)), A("hl", c, c + 128), w)
+        if not t or CF == "v":
+            tt(A("cf", 0, 128), A("k256"), A("hl", 128, 256), AL.add)
+
+    windows(0)
+    late_constants()
+    threshold(0)
+    for e in E0:
+        egather(*e)
+    z_t()
+    diffs()
+    sums("gg", 17, "zp", "ab", 0, SM, False, True)
+    scatter_constants()
+    last_constants()
+
+    for t in range(RO):
+        last = t == RO - 1
+        snd, lnd = "snd%d" % t, "lnd%d" % t
+        def in_carry():
+            z_rep(range(ZN - 1, -1, -1))
+            if t:
+                blocks_u()
+        periods(in_carry)
+        gat("a", A("g2", 16 * BS, 2048), IND("win", 16 + 3 * SEC, "ob", BS, 128))
+        gat("v", A("g2", 0, 16 * BS), IND("win", 16 + 3 * SEC, "ob", 0, BS))
+        mm([(A("dg", j, 304, 16), A("g2", j, 2048, 16), A("sel", 0, 19), j == 0, False) for j in range(16)])
+        fixup()
+        mm([(A("dg", 144, 176), A("fix"), A("ib", 96, 128), False, False),
+            (A("dg", 176, 304), A("fix"), A("ib"), False, True)])
+        act(A(snd), A("dg", 0, 304), AF.Copy)
+        send(t)
+        mm([(A("pm", 0, 128), A(snd, 16, 144), A("i64"), True, False),
+            (A("pm", 0, 128), A(snd, 176, 304), A("ib"), False, True)])
+        if t:
+            blocks_b()
+        ts(A("op_"), A("pm", 0, 128), -POF, AL.add)
+
+        def m_name():
+            mm([(A("gg", 256, 384), A(lnd, 0, 128), A("i64"), True, False),
+                (A("gg", 256, 384), A(lnd, 128, 256), A("ib"), False, True)], ext=("arr%d" % t, arrive))
+            ts(A("om"), A("gg", 256, 384), -POF, AL.add)
+        distance("op_", "s2n", True, m_name)
+
+        def m_diff():
+            if DL == "v":
+                tt(A("dl", 0, 128), (T[lnd][:, 0:128], [("om", 0, 1)]), A(snd, 16, 144), AL.subtract)
+                tt(A("dl", 128, 256), (T[lnd][:, 128:256], [("om", 0, 1)]), A(snd, 176, 304), AL.subtract)
+                return
+            mm([(A("dg", 0, 256), A("ib"), (T[lnd][:], [("om", 0, 1, 256)]), True, False),
+                (A("dg", 0, 128), A("ibn"), A(snd, 16, 144), False, False),
+                (A("dg", 128, 256), A("ibn"), A(snd, 176, 304), False, True)])
+        distance("om", "s2p", False, m_diff)
+        for i in range(len(HS)):
+            choose(i, last, snd)
+        if not last:
+            threshold(t + 1)
+            for e in EC:
+                egather(*e)
+            new_digits(t + 1, snd)
+            count()
+            diffs()
+            count2()
+            block_max(range(16))
+            sums("gg", 17, "zp", "ab", 0, SM, False, True)
+            blocks_a()
+        else:
+            cp(A("tin"), IND("nm", 128, "o3", 0, 16))
+            trn(A("tout"), A("tin"))
+            cp(A("nl"), IND("tout", 256, "o4", 0, 8))
+            cp(A("oe"), A("nl"))
+            dma("s", (T.ly[:], []), A("nl"), "out")
+            for e, m0, m1 in EL:
+                egather(e, m0, m1)
+                dma("s", (T.xy[:, 16 * m0:16 * m1], []), A("xs", 16 * m0, 16 * m1), "out")
+            for c in (3, 0, 1, 2):
+                scan(A("ysc", 512 * c, 512 * c + 512), A("m5"), A("xs", 512 * c, 512 * c + 512), 0.0, AL.mult, AL.max)
+            tt(A("zd"), YY, A("zs"), AL.subtract)
+            act(A("zt"), A("zd"), AF.Abs)
+            dma("a", (T.zy[:], []), A("zt"), "out")
+
+    hist = {}
+    sent = None
+    for i, o in enumerate(ops):
+        q = o["q"]
+        dep = {}
+        for regs, wr in ((o["r"], False), (o["w"], True)):
+            for name, a, b in regs:
+                for h in hist.get(name, []):
+                    p = ops[h[0]]
+                    if name in PS and p["q"] != q:
+                        dep[h[0]] = 1
+                    elif name in PS and q == "p":
+                        dep.setdefault(h[0], 0)
+                    elif o["dma"] and p["dma"] == o["dma"]:
+                        dep.setdefault(h[0], 0)
+                    elif (wr or h[3]) and a < h[2] and h[1] < b:
+                        dep[h[0]] = 1
+        if o["ext"] is not None:
+            dep[sent] = 1
+        if o["dma"] == "remote":
+            sent = i
+        o["dep"] = dep
+        for regs, wr in ((o["r"], False), (o["w"], True)):
+            for name, a, b in regs:
+                lst = hist.setdefault(name, [])
+                if name in PS:
+                    if lst and ops[lst[-1][0]]["q"] != q:
+                        lq = ops[lst[-1][0]]["q"]
+                        k = len(lst)
+                        while k and ops[lst[k - 1][0]]["q"] == lq:
+                            k -= 1
+                        lst[:] = lst[k:]
+                elif wr and not o["dma"]:
+                    lst[:] = [h for h in lst if h[0] == i or not (a <= h[1] and h[2] <= b)]
+                lst.append((i, a, b, wr))
+    for o in ops:
+        o["suc"] = []
+    for i, o in enumerate(ops):
+        for d, kind in o["dep"].items():
+            ops[d]["suc"].append((i, kind))
+    if not ORDER:
+        ORDER.extend(arrange(ops))
+    ops = [ops[i] for i in ORDER]
+
+    cnt = {}
+    known = {q: {} for q in Q}
+    hist = {}
+    for o in ops:
+        q = o["q"]
+        need = {}
+        for regs, wr in ((o["r"], False), (o["w"], True)):
+            for name, a, b in regs:
+                for h in hist.get(name, []):
+                    if name in PS and h["q"] != q:
+                        hit = True
+                    elif (name in PS and q == "p") or (o["dma"] and h["sem"] == o["dma"]):
+                        hit = False
+                    else:
+                        hit = (wr or h["wr"]) and a < h["b"] and h["a"] < b
+                    if hit and h["sem"] is not None:
+                        s = h["sem"]
+                        v = cnt[s] if h["dma"] else h["val"]
+                        if v > need.get(s, (0, None))[0]:
+                            need[s] = (v, h["clock"])
+        kq = known[q]
+        for s, (v, clock) in sorted(need.items(), key=lambda e: -len(e[1][1])):
+            if kq.get(s, 0) < v:
+                Q[q].wait_ge(T.sem[s], v)
+                kq[s] = v
+            for s2, v2 in clock.items():
+                if kq.get(s2, 0) < v2:
+                    kq[s2] = v2
+        if o["ext"] is not None:
+            Q[q].wait_ge(T.sem[o["ext"][0]], o["ext"][1])
+        ins = o["fn"]()
+        if o["dma"] == "remote":
+            continue
+        sem = o["dma"] or ESEM[q]
+        inc = 16 if o["dma"] else 1
+        ins.then_inc(T.sem[sem], inc)
+        cnt[sem] = cnt.get(sem, 0) + inc
+        clock = dict(kq)
+        for regs, wr in ((o["r"], False), (o["w"], True)):
+            for name, a, b in regs:
+                lst = hist.setdefault(name, [])
+                if wr and name not in PS:
+                    lst[:] = [h for h in lst if not (a <= h["a"] and h["b"] <= b and h["sem"] != o["dma"])]
+                lst.append({"q": q, "a": a, "b": b, "wr": wr, "sem": sem, "val": cnt[sem], "dma": bool(o["dma"]),
+                            "clock": clock})
+    for s, v in cnt.items():
+        g.wait_ge(T.sem[s], v)
+    g.wait_ge(T.sem.sent, RO * (mk[0][1] + mk[1][1]))

@@ -4,63 +4,63 @@ from concourse.mybir import AluOpType, AxisListType, ActivationFunctionType
 F32, BF, I32, U16 = "float32", "bfloat16", "int32", "uint16"
 RO = 4
 BIG = 2.0 ** 21
-SEC = 2064
+SEC = 2048
+S2 = 16 + 2 * SEC + 1
+WIN = 6176
+U = 1.0 / SEC
+S19 = U / 256
+CN = 2.625
+NONE = (CN - SEC) * U
 POF = 65 * 160.0
-MID = 224.0
-MH = 32
-MA = 24
-ZN = 4
-CH = (("A", 0, 24), ("V", 96, 128), ("V", 64, 96), ("V", 40, 64), ("V", 24, 40))
-RR = ()
-CD = (("A", 0, 24), ("V", 96, 128), ("V", 64, 96), ("V", 40, 64), ("V", 24, 40))
-RD = ()
-DL, CF = "v", "v"
-HS = (("d1", 64, 128), ("d0", 0, 64))
-DC = (("dfa", 96, 128), ("dfb", 64, 96), ("dfa", 40, 64), ("dfb", 16, 40), ("d0", 0, 16))
-SM = 64
-E0 = (("a", 94, 128), ("v", 62, 94), ("v", 38, 62), ("v", 14, 38), ("a", 0, 14))
-CNT = "a"
-FM = "a"
-BS = 64
-EA = 64
-EV = 48
-EC = (("a", 94, 128), ("v", 62, 94), ("v", 38, 62), ("v", 14, 38), ("a", 0, 14))
-EL = (("a", 0, 32), ("v", 96, 128), ("a", 32, 64), ("v", 76, 96), ("a", 64, 76))
-RATES = ((0.1, 0.04, 1.25, 1.56, 3.8, 0.5e-3, 2.5), (0.06, 0.03, 1.1, 1.25, 2.5, 0.42e-3, 2.0),
-         (0.12, 0.04, 1.35, 1.85, 5.0, 0.7e-3, 3.0))
-LOOK, ITER = 0.5, 3000
+MID = 208.0
+CFG = {
+    "HS": (("d1", 64, 128), ("d0", 0, 64)),
+    "DG": (("v", 96, 128), ("a", 64, 96), ("v", 34, 64), ("a", 0, 34)),
+    "CH": (("A", 64, 76), ("V", 102, 128), ("V", 76, 102), ("A", 0, 12), ("V", 38, 64), ("V", 12, 38)),
+    "XA": "a",
+    "DC": (("dfa", 97, 128), ("dfb", 65, 97), ("dfa", 39, 65), ("dfb", 13, 39), ("dfa", 0, 13)),
+    "SM": 65,
+    "E0": (("v", 102, 128), ("a", 76, 102), ("v", 64, 76), ("v", 38, 64), ("a", 12, 38), ("v", 0, 12)),
+    "EL": (("v", 112, 128), ("a", 0, 20), ("v", 80, 112), ("a", 20, 48), ("a", 48, 68), ("v", 68, 80)),
+    "ES": ((96, 128), (0, 32), (68, 96), (32, 48), (48, 68)), "LQ": "aa",
+    "TK": "a", "SC": "aa", "PH": 1, "SP": 1,
+    "RATES": ((0.1, 0.05, 1.1, 1.56, 3.8, 0.42e-3, 1.4), (0.2, 0.05, 1.1, 1.4, 2.5, 0.42e-3, 0.7),
+              (0.12, 0.05, 1.35, 1.85, 5.0, 0.55e-3, 2.2)),
+    "LOOK": 0.5, "ITER": 30000, "SEED": 12345, "TEMP": 0.003, "CNT": "vv", "HL": "a",
+}
 SPAN = []
 ORDER = []
 
 SB = {
-    "tab": (4096, BF), "win": (16 + 3 * SEC, BF), "xs": (2048, BF), "ab": (2048, BF), "dd": (2048, BF),
-    "a2": (2048, BF), "zrep": (2048, BF), "emat": (2048, BF), "g2": (2048, BF), "ysc": (2048, BF),
-    "l0s": (128, I32), "zs": (128, BF), "zd": (128, BF), "zt": (128, BF), "ths": (4, I32), "thf": (4, F32), "thc": (4, F32),
-    "pi": (8, I32), "pf": (12, F32), "kt": (256, BF), "vv": (128, F32), "xi": (160, F32), "x16": (128, F32), "xr": (128, F32), "selr": (36, F32),
-    "s2p": (16, BF), "s2n": (16, BF), "one": (128, BF), "hl": (256, BF), "dl": (256, BF),
-    "took0": (256, BF), "took1": (256, BF), "uu0": (256, BF), "uu1": (256, BF),
-    "zp": (144, BF), "zn": (144, BF), "ib": (128, BF), "ibn": (128, BF), "i64": (128, BF), "i32n": (128, F32),
-    "bp": (128, F32), "bn": (128, F32), "e8": (128, F32), "sel": (20, BF), "cm": (34, BF), "m0": (128, BF),
-    "kf": (128, F32), "k2": (128, F32), "cf": (145, F32), "cb": (145, F32),
+    "tab": (4096, BF), "win": (WIN, BF), "xs": (2048, BF), "ab": (2048, BF), "yy": (4096, BF),
+    "a2": (2048, BF), "a3": (2048, BF), "zrep": (2048, BF), "emat": (2048, BF), "g2": (2048, BF), "ysc": (2048, BF),
+    "l0s": (128, I32), "zs": (128, BF), "zd": (128, BF), "zt": (128, BF), "ths": (4, I32), "thf": (4, F32),
+    "thc": (4, F32), "thh": (4, BF), "thl": (4, F32),
+    "pi": (8, I32), "pf": (14, F32), "kt": (128, BF), "vv": (128, I32), "xi": (160, F32), "x16": (128, F32),
+    "xr": (128, F32), "selr": (36, F32), "s2p": (8, BF), "s2n": (8, BF), "one": (128, BF), "hl": (256, BF),
+    "dl": (256, BF), "tk": (128, BF), "uu": (256, BF), "zp": (144, BF), "ib": (128, BF), "ibn": (128, BF),
+    "i64": (128, BF), "i32": (128, BF), "ihf": (128, BF), "ihn": (128, BF), "i32h": (128, BF), "ibig": (128, BF),
+    "ixw": (128, BF), "d16": (128, BF), "fw": (160, BF),
+    "bp": (128, F32), "bn": (128, F32), "e8": (128, F32), "sel": (20, BF), "sel2": (12, BF), "cm": (34, BF),
+    "m0": (128, BF), "kf": (128, F32), "kq": (128, F32), "two": (128, F32), "cf": (145, F32), "cb": (145, F32),
     "oi": (64, I32), "o1": (16, U16), "o2": (8, U16), "o3": (16, U16), "o4": (8, U16), "ci": (8, I32),
     "tin": (256, F32), "tout": (256, F32), "nm": (128, F32), "nl": (128, F32),
     "oe": (128, U16), "ob": (128, U16), "op_": (128, U16), "om": (128, U16), "osc": (8, U16),
-    "tq": (128, F32), "h64": (128, F32), "hi": (128, BF), "lo": (128, BF), "lq": (128, F32),
-    "sc1": (290, F32), "cy": (2, F32), "ne": (129, F32), "ll": (128, F32), "t2": (128, I32), "mm_": (128, F32),
-    "of": (128, F32), "fa": (128, F32), "fb": (128, F32), "fm": (128, F32), "fix": (128, BF),
-    "ps": (128, F32), "took": (128, BF), "ac": (2, F32), "acb": (128, BF), "qb": (128, BF), "thb": (512, F32),
-    "ui": (16, I32), "uj": (8, I32), "sh": (128, I32), "k256": (128, F32), "imid": (128, BF), "i32b": (128, BF),
-    "bb": (128, BF), "bbn": (128, BF), "ya": (2048, BF), "yb": (2048, BF), "de": (2048, BF), "a3": (2048, BF), "m5": (512, BF),
+    "tq": (128, F32), "h64": (128, F32), "sc1": (292, F32), "cy": (2, F32), "ne": (128, F32), "al": (128, F32),
+    "zz": (128, F32), "qq": (128, F32), "of": (128, F32), "c1": (128, BF),
+    "acb": (128, BF), "qb": (128, BF), "thb": (1024, BF),
+    "ui": (16, I32), "uj": (8, I32), "sh": (128, I32), "imid": (128, BF), "i32b": (128, BF),
+    "bb": (128, BF), "bbh": (128, BF), "m5": (512, BF),
 }
 for _t in range(RO):
     SB["snd%d" % _t] = (304, BF)
-    SB["lnd%d" % _t] = (256, BF)
+    SB["lnd%d" % _t] = (512, BF)
 PS = ["dfa", "dfb", "gg", "wk", "dg", "pm", "d0", "d1"]
 SCRATCH = {k: ("sbuf", [128, v[0]], v[1]) for k, v in SB.items()}
 for _p in PS:
     SCRATCH[_p] = ("psum", [128, 512], F32)
-SEMAPHORES = ["sv", "sa", "sp", "sg", "l_l", "l_t", "l_z", "l_h", "sent", "out"]
-SEMAPHORES += ["w%d" % t for t in range(RO)] + ["arr%d" % t for t in range(RO)]
+SEMAPHORES = ["sv", "sa", "sp", "sg", "l_l", "l_t", "l_z", "l_h", "sent0", "sent1", "out"]
+SEMAPHORES += ["w%d" % t for t in range(RO)] + ["arr%d" % t for t in range(2 * RO)]
 ESEM = {"v": "sv", "a": "sa", "p": "sp", "g": "sg"}
 
 
@@ -82,28 +82,61 @@ def arrange(ops):
     qs = [o["q"] for o in ops]
     dep = [list(o["dep"].items()) for o in ops]
     suc = [o["suc"] for o in ops]
+    names = sorted(set(qs))
+    anc = [0] * n
+    hard, soft = [], []
+    for i in range(n):
+        far = 0
+        for j, k in dep[i]:
+            far |= anc[j]
+        hard.append([j for j, k in dep[i] if k and not far >> j & 1])
+        soft.append([j for j, k in dep[i] if not k and not far >> j & 1])
+        for j in hard[i]:
+            far |= 1 << j
+        anc[i] = far
     tabs = []
-    for hop, fix, kf, gat, sca, pec, rem in RATES:
-        d = [o["c"][0] + o["c"][1] * fix + (o["c"][2] * kf + o["c"][3] * gat + o["c"][4] * sca) * 0.83e-3
+    for hop, fix, kf, gat, sca, pec, rem in CFG["RATES"]:
+        d = [o["c"][0] + o["c"][1] * fix + (o["c"][2] + o["c"][3] * gat + o["c"][4] * sca) * 0.83e-3 * kf
              + o["c"][5] * pec * kf for o in ops]
         lat = [rem if o["dma"] == "remote" else o["lat"] for o in ops]
         tabs.append((d, lat, hop))
 
-    def span(order, tab):
+    def span(order, tab, old=None, a=0):
         d, lat, hop = tab
-        end = [0.0] * n
-        free = {}
-        top = 0.0
-        for i in order:
-            st = free.get(qs[i], 0.0)
-            for j, k in dep[i]:
-                e = end[j] + (lat[j] + hop) * k
-                if e > st:
-                    st = e
-            end[i] = free[qs[i]] = st + d[i]
-            if end[i] + lat[i] > top:
-                top = end[i] + lat[i]
-        return top
+        if old is None:
+            end, ok, why = [0.0] * n, [0.0] * n, [-1] * n
+        else:
+            end, ok, why = list(old[2]), list(old[3]), list(old[4])
+        prev = dict.fromkeys(names, -1)
+        k, miss = a - 1, len(names)
+        while k >= 0 and miss:
+            if prev[qs[order[k]]] < 0:
+                prev[qs[order[k]]] = order[k]
+                miss -= 1
+            k -= 1
+        for i in order[a:]:
+            q = qs[i]
+            w = prev[q]
+            st = end[w] if w >= 0 else 0.0
+            for j in hard[i]:
+                if ok[j] > st:
+                    st, w = ok[j], j
+            for j in soft[i]:
+                if end[j] > st:
+                    st, w = end[j], j
+            st += d[i]
+            end[i] = st
+            ok[i] = st + lat[i] + hop
+            why[i] = w
+            prev[q] = i
+        top = max(ok)
+        i = ok.index(top)
+        held = []
+        while i >= 0:
+            if why[i] >= 0 and why[i] not in ops[i]["dep"]:
+                held.append(i)
+            i = why[i]
+        return top, held, end, ok, why
 
     d, lat, hop = tabs[0]
     pri = [0.0] * n
@@ -120,7 +153,7 @@ def arrange(ops):
     while len(order) < n:
         t0, q = min((min(max(free[q], est[i]) for i in r), q) for q, r in ready.items() if r)
         first = min(ready[q], key=lambda i: (max(free[q], est[i]), -pri[i]))
-        i = max((i for i in ready[q] if est[i] <= t0 + LOOK * d[first]), key=lambda i: pri[i])
+        i = max((i for i in ready[q] if est[i] <= t0 + CFG["LOOK"] * d[first]), key=lambda i: pri[i])
         ready[q].remove(i)
         free[q] = max(free[q], est[i]) + d[i]
         order.append(i)
@@ -129,38 +162,64 @@ def arrange(ops):
             left[j] -= 1
             if not left[j]:
                 ready[qs[j]].append(j)
-    base = [span(order, tb) for tb in tabs]
-    cur = float(len(tabs))
-    seed = 12345
-    for _it in range(ITER):
+    res = [span(order, tb) for tb in tabs]
+    base = [r[0] for r in res]
+    cur = best = float(len(tabs))
+    keep, took = order, 0
+    seed = CFG["SEED"]
+    for it in range(CFG["ITER"]):
         seed = (seed * 1103515245 + 12345) % 2147483648
-        a = (seed >> 8) % n
-        i = order[a]
+        held = res[(seed >> 8) % len(tabs)][1]
+        if not held:
+            continue
         seed = (seed * 1103515245 + 12345) % 2147483648
-        step = 1 + (seed >> 10) % 3
-        fwd = (seed >> 20) & 1
-        block = set(j for j, _k in (suc[i] if fwd else dep[i]))
-        b = a
-        while step:
-            nb = b + 1 if fwd else b - 1
-            if nb < 0 or nb >= n or order[nb] in block:
-                break
-            b = nb
-            if qs[order[b]] == qs[i]:
+        i = held[(seed >> 8) % len(held)]
+        seed = (seed * 1103515245 + 12345) % 2147483648
+        b = order.index(i)
+        a, step = b, 1 + (seed >> 8) % 8 // 3
+        early = (seed >> 20) & 1
+        while step and a > 0:
+            a -= 1
+            if qs[order[a]] == qs[i]:
                 step -= 1
-                if not step:
-                    break
-        if step and not any(qs[x] == qs[i] for x in order[min(a, b):max(a, b) + 1] if x != i):
-            if b == a:
+        seg = order[a:b + 1]
+        if early:
+            move = {i}
+            for x in reversed(seg):
+                if x in move:
+                    move.update(j for j, _k in dep[x])
+            if seg[0] in move:
                 continue
-        cand = list(order)
-        cand.pop(a)
-        cand.insert(b, i)
-        val = sum(span(cand, tb) / bs for tb, bs in zip(tabs, base))
-        if val <= cur + 1e-9:
-            cur, order = val, cand
-    SPAN[:] = [base, [span(order, tb) for tb in tabs]]
-    return order
+            seg = [x for x in seg if x in move] + [x for x in seg if x not in move]
+        else:
+            move = {seg[0]}
+            for x in seg:
+                if x in move:
+                    move.update(j for j, _k in suc[x])
+            if i in move:
+                continue
+            seg = [x for x in seg if x not in move] + [x for x in seg if x in move]
+        cand = order[:a] + seg + order[b + 1:]
+        new = [span(cand, tb, r, a) for tb, r in zip(tabs, res)]
+        val = sum(r[0] / bs for r, bs in zip(new, base))
+        seed = (seed * 1103515245 + 12345) % 2147483648
+        if val <= cur + CFG["TEMP"] * (1 - it / CFG["ITER"]) * ((seed >> 8) % 1000) / 1000:
+            cur, order, res = val, cand, new
+            took += 1
+            if took % 20 == 0:
+                order = sorted(order, key=lambda x: res[0][2][x] - tabs[0][0][x])
+            if val < best:
+                best, keep = val, cand
+    SPAN[:] = [base, [span(keep, tb)[0] for tb in tabs]]
+    return keep
+
+
+def meet(x, y):
+    return x[1] < y[2] and y[1] < x[2] and x[4] < y[5] and y[4] < x[5]
+
+
+def covers(x, y):
+    return x[1] <= y[1] and y[2] <= x[2] and x[4] <= y[4] and y[5] <= x[5]
 
 
 def rank_program(g, core, T, topo):
@@ -170,6 +229,8 @@ def rank_program(g, core, T, topo):
     n = len(T.cores)
     Q = {"v": g.vector, "a": g.scalar, "p": g.tensor, "g": g, "s": g.sync}
     AL, AF = AluOpType, ActivationFunctionType
+    HS, CH, DC, SM = CFG["HS"], CFG["CH"], CFG["DC"], CFG["SM"]
+    tko = 1 if CFG["TK"] == "v" else 0
     ops = []
 
     def A(name, a=0, b=None, s=1, p=None):
@@ -177,37 +238,38 @@ def rank_program(g, core, T, topo):
         if b is None:
             b = w
         rows = slice(None) if p is None else slice(*p)
-        reg = [(name, a, b, len(range(a, b, abs(s))))]
+        reg = [(name, a, b, len(range(a, b, abs(s)))) + ((0, 128) if p is None else p[:2])]
         if s < 0:
             return T[name][rows, slice(b - 1, a - 1 if a > 0 else None, s)], reg
         if s == 1:
             return T[name][rows, a:b], reg
         return T[name][rows, a:b:s], reg
 
-    def IND(name, w, off, c, d):
-        return T[name][:, 0:w].indirect(T[off][:, c:d]), [(name, 0, w), (off, c, d)]
+    def IND(name, a, b, off, c, d):
+        return T[name][:, a:b].indirect(T[off][:, c:d]), [(name, a, b, 0, 0, 128), (off, c, d, -16 * (d - c), 0, 128)]
 
     def sc(x):
         return (x, []) if not isinstance(x, tuple) else x
 
-    def add(q, fn, reads, writes, dma=None, ext=None, cost=None):
+    def add(q, fn, reads, writes, dma=None, ext=None, cost=None, after=None):
         lat = 0.0
         if dma == "remote":
-            d = (0.5, 0, 0, 0, 0, 0)
+            d = (1.2, 0, 0, 0, 0, 0)
         elif dma:
-            d, lat = (0.06, 0, 0, 0, 0, 0), {"l_t": 6.5, "out": 2.6}.get(dma, 2.5)
+            wide = (writes if dma[0] == "l" else reads)[0]
+            busy = 0.24 + wide[3] * (2 if SB[wide[0]][1] == BF else 4) * 0.45e-3
+            d, lat = ((busy, 0, 0, 0, 0, 0), 1.4) if q == "s" else ((0.06, 0, 0, 0, 0, 0), 1.4 + busy)
         elif q == "p":
             d, lat = (0, 0, 0, 0, 0, cost), 0.06
         else:
-            ind = [x for x in reads if SB.get(x[0], (0, 0))[1] == U16 and x[2] - x[1] > 1]
+            ind = [-x[3] for x in reads if x[3] < 0]
             if ind:
-                k = 16 * (ind[0][2] - ind[0][1])
-                d = (0.06, 0, 0, 0, k, 0) if writes[0][0] == "tab" else (0.06, 0, 0, k, 0, 0)
+                d = (0.01, 1, 0, 0, ind[0], 0) if writes[0][3] == 0 else (0.01, 1, 0, ind[0], 0, 0)
             else:
-                nel = writes[0][3] if len(writes[0]) > 3 else writes[0][2] - writes[0][1]
+                nel = writes[0][3]
                 if nel == 1 and reads:
-                    nel = reads[0][2] - reads[0][1]
-                big = [x for x in reads + writes if x[2] - x[1] >= nel]
+                    nel = reads[0][3]
+                big = [x for x in reads + writes if x[3] >= nel]
                 if q == "g":
                     d = (0.15, 0, 2 * nel, 0, 0, 0)
                 else:
@@ -216,8 +278,9 @@ def rank_program(g, core, T, topo):
                     if cost == "tt" and not any(x[0] in PS for x in reads):
                         rate *= 2
                     d = (0, 1, max(64, nel * rate), 0, 0, 0)
-        ops.append({"q": q, "fn": fn, "r": [x[:3] for x in reads], "w": [x[:3] for x in writes], "dma": dma,
-                    "ext": ext, "c": d, "lat": lat})
+        ops.append({"q": q, "fn": fn, "r": reads, "w": writes, "dma": dma, "ext": ext, "c": d, "lat": lat,
+                    "after": after})
+        return len(ops) - 1
 
     def tt(o, a, b, op):
         add("v", lambda: g.vector.tensor_tensor(o[0], a[0], b[0], op), a[1] + b[1], o[1], cost="tt")
@@ -236,29 +299,29 @@ def rank_program(g, core, T, topo):
         add("v", lambda: g.vector.memset(o[0], v), [], o[1])
 
     def scan(o, a, b, init, op0, op1):
-        add("v", lambda: g.vector.tensor_tensor_scan(o[0], a[0], b[0], init, op0, op1), a[1] + b[1], o[1])
+        init = sc(init)
+        add("v", lambda: g.vector.tensor_tensor_scan(o[0], a[0], b[0], init[0], op0, op1), a[1] + b[1] + init[1], o[1])
 
-    def red(o, a, op, neg=False):
-        if neg:
-            add("v", lambda: g.vector.tensor_reduce(o[0], a[0], AxisListType.X, op, negate=True), a[1], o[1])
-        else:
-            add("v", lambda: g.vector.tensor_reduce(o[0], a[0], AxisListType.X, op), a[1], o[1])
+    def red(o, a, op):
+        add("v", lambda: g.vector.tensor_reduce(o[0], a[0], AxisListType.X, op, negate=True), a[1], o[1])
 
     def trn(o, a):
         add("v", lambda: g.vector.transpose(o[0], a[0]), a[1], o[1])
 
     def act(o, a, f, bias=0.0, scale=1.0):
-        bias = sc(bias)
-        add("a", lambda: g.scalar.activation(o[0], a[0], f, bias=bias[0], scale=scale), a[1] + bias[1], o[1])
+        bias, scale = sc(bias), sc(scale)
+        add("a", lambda: g.scalar.activation(o[0], a[0], f, bias=bias[0], scale=scale[0]),
+            a[1] + bias[1] + scale[1], o[1])
 
-    def mm(lst, ext=None, cost=None):
+    def mm(lst, ext=None):
         def fn():
             r = None
             for o, l, rr, st, sp in lst:
                 r = g.tensor.matmul(o[0], l[0], rr[0], st, sp)
             return r
         add("p", fn, [x for e in lst for x in e[1][1] + e[2][1]], [x for e in lst for x in e[0][1]], ext=ext,
-            cost=cost or sum(max(64, e[2][1][0][3]) * (4 if SB[e[1][1][0][0]][1] == F32 else 1) for e in lst))
+            cost=sum(max(min(64, e[1][1][0][3]), e[2][1][0][3]) * (4 if SB[e[1][1][0][0]][1] == F32 else 1) for e in lst))
+        ops[-1]["rows"] = lst[0][1][1][0][4:6]
 
     def iota(o, pat, base, cm, fl=True):
         if fl:
@@ -266,8 +329,8 @@ def rank_program(g, core, T, topo):
         else:
             add("g", lambda: g.iota(o[0], pat, base, cm), [], o[1])
 
-    def dma(q, o, a, sem):
-        add(q, lambda: Q[q].dma_start(o[0], a[0]), a[1], o[1], dma=sem)
+    def dma(q, o, a, sem, after=None):
+        return add(q, lambda: Q[q].dma_start(o[0], a[0]), a[1], o[1], dma=sem, after=after)
 
     def gat(e, o, src):
         if e == "v":
@@ -278,15 +341,21 @@ def rank_program(g, core, T, topo):
     def col(name, c, p=None):
         return A(name, c, c + 1, p=p)
 
-    dma("s", A("l0s"), (T.l0[:], []), "l_l")
-    dma("s", A("tab"), (T.x0[:], []), "l_t")
+    def lin(o, a, scale, bias=0.0):
+        act(o, a, AF.Identity, bias=bias, scale=scale)
+
+    def eye(name, v, src="ib"):
+        act(A(name, 0, 128), A(src, 0, 128), AF.Copy, scale=v)
+
+    first = dma("s", A("l0s"), (T.l0[:], []), "l_l")
+    first = dma("s", A("tab"), (T.x0[:], []), "l_t", after=first)
+    dma("s", A("zs"), (T.z0[:], []), "l_z", after=first)
     dma("a", A("ths", p=(0, 8)), (T.th[:], []), "l_h")
-    dma("a", A("zs"), (T.z0[:], []), "l_z")
 
     iota(col("pi", 0), [[0, 1]], 0, 1, False)
     iota(A("oi", 0, 16), [[1, 8], [0, 2]], 0, 8, False)
     iota(A("xi"), [[1, 160]], 0, 0)
-    ms(A("win", 16 + SEC, 16 + 2 * SEC), MID)
+    ms(A("win", 16 + SEC, S2 - 1), MID)
     ts(col("pi", 1), col("pi", 0), 15, AL.bitwise_and)
     ts(A("oi", 16, 32), A("oi", 0, 16), 127, AL.bitwise_and)
     ts(col("pi", 2), col("pi", 0), 31, AL.bitwise_and)
@@ -300,116 +369,126 @@ def rank_program(g, core, T, topo):
     iota(A("selr", 1, 9), [[16, 8]], 0, 0)
     iota(A("selr", 9, 11), [[16, 2]], 97, 0)
     iota(A("selr", 11, 19), [[16, 8]], 1, 0)
-    iota(A("selr", 20, 36), [[0, 2], [16, 8]], 0, 0)
-    add("g", lambda: g.affine_select(T.emat[:], T.win[:, 16 + SEC:16 + SEC + 2048], [[-1, 8], [0, 16], [-8, 16]],
-                                     AL.is_equal, 0.0, 0, 1), [("win", 16 + SEC, 16 + 2 * SEC)], [("emat", 0, 2048)])
+    iota(A("one"), [[0, 128]], 1, 0)
+    iota(A("win", S2 - 1, WIN), [[0, WIN - S2 + 1]], 256, 0)
+    add("g", lambda: g.affine_select(T.emat[:], T.win[:, 16 + SEC:16 + 2 * SEC], [[-1, 8], [0, 16], [-8, 16]],
+                                     AL.is_equal, 0.0, 0, 1), A("win", 16 + SEC, 16 + 2 * SEC)[1], A("emat")[1])
+    on_g = [i for i, o in enumerate(ops) if o["q"] == "g"]
+    for i, k in zip(on_g, on_g[1:]):
+        ops[k]["after"] = i
     tt(col("pf", 3), col("pf", 0), col("pf", 1), AL.subtract)
-    ts(col("pf", 4), col("pf", 1), 128.0, AL.mult)
-    ts(col("pf", 5), col("pf", 3), 15.0, AL.add)
-    ts(col("pf", 6), col("pf", 0), 16.0, AL.mult)
-    ts(col("pf", 8), col("pf", 0), 256.0, AL.mult)
-    ts(A("kf"), A("xi", 0, 128), col("pf", 4), AL.add)
-    ms(A("win", 0, 16 + SEC), 0.0)
+    lin(col("pf", 5), col("pf", 3), 1.0, 15.0)
+    lin(col("pf", 6), col("pf", 0), 16.0)
+    lin(col("pf", 8), col("pf", 0), 256.0)
+    lin(col("pf", 9), col("pf", 1), 128 * U)
+    lin(col("pf", 10), col("pf", 1), -256 * U)
+    lin(col("pf", 11), col("pf", 0), 1.0, -1.0)
+    lin(A("kq"), A("xi", 0, 128), U, col("pf", 9))
+    ms(A("win", 0, 16 + SEC), 192.0)
 
-    def names_from_input():
-        cp(A("tin"), IND("l0s", 128, "o1", 0, 16))
-        trn(A("tout"), A("tin"))
-        cp(A("nm"), IND("tout", 256, "o2", 0, 8))
-        cp(A("oe"), A("nm"))
-
-    def digits(t):
-        act(A("hl", 0, 128), A("nm"), AF.Identity, bias=160 - 31.5 / 64, scale=1.0 / 64)
-        act(A("h64"), A("hl", 0, 128), AF.Identity, bias=POF, scale=-64.0)
-        tt(A("hl", 128, 256), A("nm"), A("h64"), AL.add)
-
-    names_from_input()
-    ms(A("win", 16 + 2 * SEC, 16 + 3 * SEC), 0.0)
-    digits(0)
-    ts(A("k256"), A("kf"), 256.0, AL.mult, -160.0, AL.add)
+    cp(A("tin"), IND("l0s", 0, 128, "o1", 0, 16))
+    trn(A("tout"), A("tin"))
+    cp(A("nm"), IND("tout", 0, 256, "o2", 0, 8))
+    cp(A("oe"), A("nm"))
+    act(A("hl", 0, 128), A("nm"), AF.Identity, bias=160 - 31.5 / 64, scale=1.0 / 64)
+    act(A("h64"), A("hl", 0, 128), AF.Identity, bias=POF, scale=-64.0)
+    tt(A("hl", 128, 256), A("nm"), A("h64"), AL.add)
+    lin(A("h64"), A("hl", 128, 256), S19)
+    tt(A("cf", 0, 128), A("h64"), A("kq"), AL.add)
     ts(A("ib"), A("xi", 0, 128), col("pf", 0), AL.is_equal)
-    ts(A("ibn"), A("xi", 0, 128), col("pf", 0), AL.is_equal, -1.0, AL.mult)
+    eye("ibn", -1.0)
     ts(A("e8", p=(0, 8)), A("x16", p=(0, 8)), col("pf", 6, (0, 8)), AL.is_equal)
     cp(A("thf", p=(0, 8)), A("ths", p=(0, 8)))
-    mm([(A("d0", 0, 4), A("e8", p=(0, 8)), A("thf", p=(0, 8)), True, True)])
-    ts(A("i32n"), A("xi", 0, 128), col("pf", 0), AL.is_equal, -BIG, AL.mult)
+    mm([(A("dg", 0, 4), A("e8", p=(0, 8)), A("thf", p=(0, 8)), True, True)])
+    eye("ibig", -BIG)
     ts(A("zp"), A("xi", 0, 144), col("pf", 5), AL.is_equal, BIG, AL.mult)
-    ts(A("thc", 0, 1), A("d0", 0, 1), 0.5, AL.add)
-    ts(A("thc", 1, 4), A("d0", 1, 4), 5120.5, AL.add)
+    lin(A("thc", 0, 1), A("dg", 0, 1), 1.0, 0.5)
+    lin(A("thc", 1, 4), A("dg", 1, 4), 1.0, 5120.5 + 1024 * (1 + tko))
+    lin(A("thh"), A("thc"), 1.0)
+    tt(A("thl"), A("thc"), A("thh"), AL.subtract)
     for t in range(RO):
-        act(A("thb", 128 * t, 128 * t + 128), A("kf"), AF.Identity, bias=col("thc", t), scale=0.0)
+        lin(A("thb", 256 * t, 256 * t + 128), A("xi", 0, 128), 0.0, col("thh", t))
+        lin(A("thb", 256 * t + 128, 256 * t + 256), A("xi", 0, 128), 0.0, col("thl", t))
     ms(col("ab", 0), 512.0)
 
     def late_constants():
-        ts(A("s2p"), A("selr", 20, 36), col("pf", 3), AL.is_equal)
-        ts(A("s2n"), A("selr", 20, 36), col("pf", 3), AL.is_equal, -1.0, AL.mult)
-        ms(A("one"), 1.0)
-        for nm_ in ("took0", "took1", "uu0", "uu1"):
-            ms(A(nm_), 0.0)
-        ts(A("kt", 0, 128), A("xr"), 32768.0, AL.mult)
-        ts(A("kt", 128, 256), A("xr"), 0.0, AL.mult, col("pf", 8), AL.add)
-        ts(A("i64"), A("xi", 0, 128), col("pf", 0), AL.is_equal, 64.0, AL.mult)
-        ts(A("imid"), A("xi", 0, 128), col("pf", 0), AL.is_equal, -MID, AL.mult)
-        ts(A("i32b"), A("xi", 0, 128), col("pf", 0), AL.is_equal, 32 * BIG, AL.mult)
+        ts(A("s2p"), A("selr", 1, 9), col("pf", 3), AL.is_equal)
+        lin(A("s2n"), A("s2p"), -1.0)
+        lin(A("two", 1, 128), A("xi", 1, 128), 0.0, 2 * U)
+        lin(A("two", 0, 1), A("xi", 0, 1), 0.0)
+        lin(A("kt"), A("xr"), 0.0, col("pf", 8))
+        eye("i64", 64.0)
+        eye("i32", 32.0)
+        eye("i32h", -32.0)
+        eye("ihf", 0.5)
+        eye("ihn", -0.5)
+        eye("imid", -MID)
+        eye("i32b", 32 * BIG)
+        for _b, m0, m1 in HS:
+            act(A("ixw", m0, m1), A("ib", m0, m1), AF.Copy, scale=-8.0 * (m1 - m0))
+            lin(col("pf", 13), col("pf", 6), 1.0, -16.0 * m0)
+            act(A("d16", m0, m1), A("ib", m0, m1), AF.Identity, scale=col("pf", 13))
+        lin(col("pf", 12), col("pf", 1), 1.0, 8.0 * (HS[0][2] - HS[0][1]) * (1 + tko))
+        act(A("fw", 0, 32), A("ib", 96, 128), AF.Copy, scale=-1.0 / S19)
+        act(A("fw", 32, 160), A("ib"), AF.Copy, scale=-1.0 / S19)
         ts(A("bp"), A("x16"), col("pf", 3), AL.is_equal)
-        ts(A("bn"), A("x16"), col("pf", 3), AL.is_equal, -1.0, AL.mult)
-        ts(A("bb"), A("x16"), col("pf", 3), AL.is_equal)
-        ts(A("bbn"), A("x16"), col("pf", 3), AL.is_equal, -BIG, AL.mult)
+        eye("bn", -1.0, "bp")
+        eye("bb", 1.0, "bp")
+        eye("bbh", BIG / 2, "bp")
         ts(A("sel", 0, 19), A("selr", 0, 19), col("pf", 0), AL.is_equal)
+        ts(A("sel2", 0, 10), A("selr", 9, 19), col("pf", 11), AL.is_equal)
+        tt(A("sel", 9, 19), A("sel", 9, 19), A("sel2", 0, 10), AL.add)
         ts(A("cf", 128, 145), A("xi", 0, 17), col("pf", 1), AL.is_le, BIG, AL.mult)
         ts(A("cb", 0, 17), A("xi", 0, 17), col("pf", 1), AL.is_gt, BIG, AL.mult)
-        ts(A("cb", 17, 145), A("kf"), -1.0, AL.mult, 2 * SEC + 0.25, AL.add)
-        ts(A("k2"), A("kf"), 2.0, AL.mult, 2.0 - 2 * SEC, AL.add)
-        ts(A("cm", 0, 17), A("xi", 0, 17), col("pf", 1), AL.is_ge, -BIG, AL.mult)
-        ts(A("cm", 17, 33), A("xi", 0, 16), col("pf", 1), AL.is_le, BIG, AL.mult)
-        ts(A("m0"), A("xr"), 0.0, AL.is_gt)
+        lin(A("cb", 0, 17), A("cb", 0, 17), 1.0, -1.0)
+        lin(A("cb", 17, 145), A("kq"), -1.0, CN * U)
+        lin(A("wk", 256, 384), A("kq"), 2.0)
+        lin(A("wk", 384, 512), A("kq"), 2.0, (2 * SEC + 0.25 - CN) * U)
+        ts(A("tq", 64, 81), A("xi", 0, 17), col("pf", 1), AL.is_ge, -BIG, AL.mult)
+        lin(A("cm", 0, 17), A("tq", 64, 81), 1.0, col("pf", 10))
+        lin(A("cm", 17, 33), A("cf", 128, 144), 1.0, 1.0)
+        act(A("m0"), A("xr"), AF.Sign)
         ms(A("gg", 0, 17), -BIG)
         ms(A("gg", 145, 162), -BIG)
-        ms(A("pm", 289, 290), -(2 * SEC - 2048 + 0.25))
+        ms(A("pm", 289, 290), -NONE)
+        ms(A("sc1", 290, 291), NONE)
 
     def last_constants():
-        ts(A("tq", 0, 8), A("xi", 0, 8), 16.0, AL.mult, col("pf", 1), AL.add)
-        cp(A("o3", 0, 16, 2), A("tq", 0, 8))
-        cp(A("o3", 1, 16, 2), A("tq", 0, 8))
+        ts(A("tq", 112, 120), A("xi", 0, 8), 16.0, AL.mult, col("pf", 1), AL.add)
+        cp(A("o3", 0, 16, 2), A("tq", 112, 120))
+        cp(A("o3", 1, 16, 2), A("tq", 112, 120))
+        ts(A("ci"), A("tq", 112, 120), 32.0, AL.mult)
         ts(col("pi", 3), col("pi", 0), 7, AL.bitwise_and)
         ts(col("pi", 4), col("pi", 0), 3, AL.logical_shift_right, 1, AL.bitwise_and)
         ts(col("pi", 5), col("pi", 0), 16, AL.bitwise_and)
         ts(col("pi", 6), col("pi", 3), 32.0, AL.mult)
         tt(col("pi", 7), col("pi", 4), col("pi", 5), AL.add)
         tt(col("pf", 7), col("pi", 6), col("pi", 7), AL.add)
-        ts(A("tq", 8, 16), A("xi", 0, 8), 2.0, AL.mult, col("pf", 7), AL.add)
-        cp(A("o4"), A("tq", 8, 16))
+        ts(A("tq", 120, 128), A("xi", 0, 8), 2.0, AL.mult, col("pf", 7), AL.add)
+        cp(A("o4"), A("tq", 120, 128))
         for c in range(4):
             act(A("m5", 128 * c, 128 * c + 128), A("m0"), AF.Copy)
 
-    def scatter_constants():
-        ts(A("tq", 16, 24), A("xi", 0, 8), 16.0, AL.mult, col("pf", 1), AL.add)
-        ts(A("ci"), A("tq", 16, 24), 32.0, AL.mult)
+    def zl(j):
+        return A("zp", 15 - j, 143 - j)
 
-    def zl(name, j):
-        return A(name, 15 - j, 143 - j)
-
-    def sums(out, c0, lname, src, m0, m1, start, stop):
-        mm([(A(out, c0, c0 + m1 - m0), zl(lname, j), A(src, 16 * m0 + j, 16 * (m1 - 1) + j + 1, 16),
-             start and j == 0, stop and j == 15) for j in range(16)])
+    def sums(m0, m1, stop):
+        mm([(A("gg", 17 + m0, 17 + m1), zl(j), A("ab", 16 * m0 + j, 16 * (m1 - 1) + j + 1, 16), False, stop and j == 15)
+            for j in range(16)])
 
     def threshold(t):
-        mm([(A("gg", 17, 145), A("i32n"), A("thb", 128 * t, 128 * t + 128), True, False)])
+        mm([(A("gg", 17, 145), A("ibig"), A("thb", 256 * t, 256 * t + 128), True, False),
+            (A("gg", 17, 145), A("ibig"), A("thb", 256 * t + 128, 256 * t + 256), False, False)])
 
     def count():
-        mm([(A("d1", 256, 384), A("took%d" % i, 0, 128), A("one"), i == 0, i == len(HS) - 1)
-            for i, (_b, m0, m1) in enumerate(HS)])
-        if CNT[0] == "a":
-            act(A("acb"), A("d1", 256, 384), AF.Copy)
-        else:
-            cp(A("acb"), A("d1", 256, 384))
+        mm([(A("d1", 256, 384), A("tk"), A("one"), True, True)])
+        gat(CFG["CNT"][0], A("acb"), A("d1", 256, 384))
         mm([(A("d1", 128, 256), A("bb"), A("acb"), True, True)])
-
-    def count2():
-        if CNT[-1] == "a":
-            act(A("qb"), A("d1", 128, 256), AF.Identity, bias=160 - 15.5 / 32, scale=1.0 / 32)
+        if CFG["CNT"][1] == "a":
+            act(A("qb"), A("d1", 128, 256), AF.Identity, bias=160 + 32 * (1 + tko) - 15.5 / 32, scale=-1.0 / 64)
         else:
-            ts(A("qb"), A("d1", 128, 256), 1.0 / 32, AL.mult, 160 - 15.5 / 32, AL.add)
-        mm([(A("gg", 17, 145), A("bbn"), A("acb"), False, False), (A("gg", 17, 145), A("i32b"), A("qb"), False, False)])
+            ts(A("qb"), A("d1", 128, 256), -1.0 / 64, AL.mult, 160 + 32 * (1 + tko) - 15.5 / 32, AL.add)
+        mm([(A("gg", 17, 145), A("bbh"), A("acb"), False, False), (A("gg", 17, 145), A("i32b"), A("qb"), False, False)])
 
     def diff(bank, a, b):
         lst = []
@@ -423,286 +502,342 @@ def rank_program(g, core, T, topo):
         a2 = max(a, 1)
         act(A("ab", a2, b), A(bank, a2 - a, b - a), AF.Abs)
 
-    def diffs():
+    def diffs(lo, hi):
         for bank, m0, m1 in DC:
-            diff(bank, 16 * m0, 16 * m1)
-            if m0 == SM:
-                sums("gg", 17 + SM, "zp", "ab", SM, 128, False, False)
+            if lo <= m0 < hi:
+                diff(bank, 16 * m0, 16 * m1)
 
     def egather(e, m0, m1):
-        gat(e, A("xs", 16 * m0, 16 * m1), IND("tab", 4096, "oe", m0, m1))
+        gat(e, A("xs", 16 * m0, 16 * m1), IND("tab", 0, 4096, "oe", m0, m1))
 
-    def z_t():
-        mm([(A("d0", 128, 256), A("zs"), A("ib"), True, True)])
-        act(A("zt"), A("d0", 128, 256), AF.Copy)
+    def z_rep():
+        nb = 0
+        for _b, lo, hi in HS:
+            m0 = max([lo] + [y for mode, x, y in CH if mode == "A" and lo <= x < hi])
+            k = -(-(hi - m0) // 32)
+            for c in range(k - 1, -1, -1):
+                bank = ("dfa", "dfb")[nb & 1]
+                nb += 1
+                a, b = 16 * (m0 + (hi - m0) * c // k), 16 * (m0 + (hi - m0) * (c + 1) // k)
+                mm([(A(bank, 0, b - a), A("zt"), A("emat", a, b), True, True)])
+                act(A("zrep", a, b), A(bank, 0, b - a), AF.Copy, scale=1.0 / MID)
 
-    def z_rep(cs):
-        w = 16 * (128 - MA) // ZN
-        for c in cs:
-            bank = "dfa" if c & 1 else "dfb"
-            a = 16 * MA + w * c
-            mm([(A(bank, 0, w), A("zt"), A("emat", a, a + w), True, True)])
-            act(A("zrep", a, a + w), A(bank, 0, w), AF.Copy, scale=1.0 / MID)
-
-    def block_max(js):
-        for j in js:
+    def block_max():
+        for j in range(16):
             scan(A("ysc", 128 * j, 128 * j + 128), A("m0", 0, 128), A("xs", j, 2048, 16), 0.0, AL.mult, AL.max)
 
     YY = A("ysc", 15, 2048, 16)
 
     def blocks_a():
-        mm([(A("d0", 128, 256), YY, A("ib"), True, False), (A("d0", 128, 256), A("zs"), A("ibn"), False, True)])
-        act(A("zt"), A("d0", 128, 256), AF.Abs)
-        mm([(A("d1", 128, 256), A("ib"), YY, True, False), (A("d1", 128, 256), A("ibn"), A("zs"), False, True),
-            (A("d1", 256, 384), A("ib"), YY, True, False), (A("d1", 256, 384), A("ib"), A("zs"), False, True)])
-
-    def blocks_u():
-        mm([(A("d1", 8, 16), zl("zp", r), A("ysc", 15 + 16 * r, 2048, 256), r == 0, r == 15) for r in range(16)])
-        act(A("zs"), A("d1", 128, 256), AF.Abs)
-
-    def blocks_b():
-        ts(A("sh"), A("d1", 256, 384), 0.5, AL.mult, -0.25, AL.add)
-        ts(A("ui", 0, 8), A("d1", 8, 16), 1.0 / BIG, AL.mult)
+        mm([(A("dg", 0, 128), YY, A("ib"), True, False), (A("dg", 0, 128), A("zs"), A("ibn"), False, True)])
+        act(A("zt"), A("dg", 0, 128), AF.Abs)
+        mm([(A("dg", 384, 392), zl(r), A("ysc", 15 + 16 * r, 2048, 256), r == 0, r == 15) for r in range(16)])
+        mm([(A("dg", 128, 256), A("ib"), YY, True, False), (A("dg", 128, 256), A("ibn"), A("zs"), False, True),
+            (A("dg", 256, 384), A("ib"), YY, True, False), (A("dg", 256, 384), A("ib"), A("zs"), False, True)])
+        ts(A("ui", 0, 8), A("dg", 384, 392), 1.0 / BIG, AL.mult)
+        ts(A("sh"), A("dg", 256, 384), 0.5, AL.mult, -0.25, AL.add)
+        act(A("zs"), A("dg", 128, 256), AF.Abs)
         ts(A("ui", 8, 16), A("ui", 0, 8), 31, AL.bitwise_and)
         tt(A("uj"), A("ui", 8, 16), A("ci"), AL.add)
         cp(A("osc"), A("uj"))
-        cp(IND("tab", 4096, "osc", 0, 8), A("sh"))
+        cp(IND("tab", 0, 4096, "osc", 0, 8), A("sh"))
 
-    def periods(mid):
+    def periods():
         mm([(A("pm", 256, 289), A("ib"), A("cm", 0, 33), True, False)])
         scan(A("sc1", 0, 145), A("gg", 17, 162), A("cf"), 0.0, AL.max, AL.min)
-        scan(A("sc1", 145, 290, -1), A("gg", 0, 145, -1), A("cb", 0, 145, -1), 2 * SEC - 2048 + 0.25, AL.max, AL.min)
+        scan(A("sc1", 145, 290, -1), A("gg", 0, 145, -1), A("cb", 0, 145, -1), NONE, AL.max, AL.min)
         mm([(A("pm", 256, 289), A("bp"), A("sc1", 128, 161), False, False),
             (A("pm", 256, 289), A("bn"), A("sc1", 129, 162), False, True)])
-        mid()
+        tt(A("al"), A("wk", 256, 384), A("sc1", 0, 128), AL.subtract)
         red(col("cy", 0), A("pm", 256, 272), AL.max)
-        red(col("ne", 128), A("pm", 273, 290), AL.min, True)
-        ts(A("wk", 0, 128), A("sc1", 0, 128), col("cy", 0), AL.max, 1.0 / 256, AL.mult)
-        ts(A("ne", 0, 128), A("sc1", 162, 290), col("ne", 128), AL.max)
-        tt(A("wk", 128, 256), A("k2"), A("wk", 0, 128), AL.subtract)
-        tt(A("wk", 256, 384), A("ne", 1, 129), A("wk", 0, 128), AL.add)
-        tt(A("t2"), A("ne", 1, 129), A("wk", 128, 256), AL.add)
-        ts(A("vv"), A("t2"), 0.0, AL.max, float(SEC), AL.mult)
-        tt(A("mm_"), A("vv"), A("wk", 256, 384), AL.min)
-        tt(A("of"), A("mm_"), A("wk", 128, 256), AL.add)
-        ts(A("ob"), A("of"), 2 * SEC - 2 + 16 + 63.5 / 256, AL.add)
-
-    def fixup():
-        tt(A("wk", 384, 512), A("ne", 1, 129), A("wk", 128, 256), AL.add)
-        if FM == "v":
-            ts(A("fm"), A("vv"), float(SEC), AL.is_equal, 256.0, AL.mult)
-        else:
-            act(A("fa"), A("vv"), AF.Abs, bias=-float(SEC))
-            act(A("fm"), A("fa"), AF.Relu, bias=256.0, scale=-1.0)
-        tt(A("wk", 0, 128), A("t2"), A("wk", 384, 512), AL.subtract)
-        tt(A("fix"), A("fm"), A("wk", 0, 128), AL.mult)
+        red(col("cy", 1), A("pm", 273, 290), AL.min)
+        scan(A("wk", 0, 128), A("two"), A("al"), col("cy", 0), AL.add, AL.min)
+        parts = [(m0, m1) for _b, m0, m1 in HS] if CFG["PH"] == 2 else [(0, 128)]
+        for step in range(8):
+            for a, b in parts:
+                if step == 0:
+                    ts(A("ne", a, b), A("sc1", 163 + a, 163 + b), col("cy", 1), AL.max)
+                elif step == 1:
+                    tt(A("zz", a, b), A("wk", a, b), A("ne", a, b), AL.add)
+                elif step == 2:
+                    tt(A("wk", 128 + a, 128 + b), A("wk", 384 + a, 384 + b), A("ne", a, b), AL.add)
+                elif step == 3:
+                    ts(A("vv", a, b), A("zz", a, b), float(SEC), AL.mult, 0.0, AL.max)
+                elif step == 4:
+                    tt(A("qq", a, b), A("wk", a, b), A("vv", a, b), AL.add)
+                elif step == 5:
+                    tt(A("of", a, b), A("wk", 128 + a, 128 + b), A("qq", a, b), AL.min)
+                elif step == 6:
+                    ts(A("ob", a, b), A("of", a, b), float(SEC), AL.mult, 16.75, AL.add)
+        ts(A("c1"), A("zz"), 192 * S19, AL.max, 256 * S19, AL.min)
 
     d1, d2 = T.cores[(rank + 1) % n], T.cores[(rank + 2) % n]
     mk = masks(topo, core, [d1, d2])
     s1, s2 = T.cores[(rank - 1) % n], T.cores[(rank - 2) % n]
     arrive = masks(topo, s1, [core, T.cores[(rank + 1) % n]])[0][1] + masks(topo, s2, [s1, core])[1][1]
 
-    def send(t):
-        snd, lnd = "snd%d" % t, "lnd%d" % t
+    left = mk[0][1] + mk[1][1]
+    SP = CFG["SP"]
 
+    def SND(t, i, a, b, p=None):
+        return A("snd%d" % (i if SP else t), a, b, p=p)
+
+    def LND(t, i, a, b, p=None):
+        x = A("lnd%d" % t, 256 * i * SP + a, 256 * i * SP + b, p=p)
+        return x[0], x[1] + col("om", HS[i][1])[1]
+
+    def send(t, i):
         def fn():
             trs = []
             for d, (m, _c), a, b in ((d1, mk[0], 0, 0), (d2, mk[1], 144, 128)):
                 ad = topo.addr(d)
                 trs.append(RemoteDMATransfer(dst_ids=[DstId(rid=ad[0], pnc=ad[1])], dma_engine_mask=m,
-                                             remote_sem=T.sem["arr%d" % t], src=T[snd][:, a:a + 128],
-                                             dst=T[lnd][:, b:b + 128]))
-            g.remote_dma_fused(trs, local_sem=T.sem.sent)
+                                             remote_sem=T.sem["arr%d" % (2 * t + i)], src=SND(t, i, a, a + 128)[0],
+                                             dst=LND(t, i, b, b + 128)[0]))
+            g.remote_dma_fused(trs, local_sem=T.sem["sent%d" % i])
             return None
-        add("g", fn, [(snd, 0, 304)], [], dma="remote")
+        add("g", fn, SND(t, i, 0, 304)[1], [], dma="remote", ext=("arr%d" % (2 * t + i), 0))
 
-    def distance(off, lname, first, after=None):
-        dd, a2, ya = ("dd", "a2", "ya") if first else ("de", "a3", "yb")
-        other = "s2p" if lname == "s2n" else "s2n"
-        nb = 0
-        for mode, m0, m1 in (CH if first else CD):
-            a, b = 16 * m0, 16 * m1
-            if mode == "A":
-                bank = ("dfa", "dfb")[(nb + first) & 1]
-                nb += 1
-                act(A(ya, a, b), IND("tab", 4096, off, m0, m1), AF.Copy)
-                mm([(A(bank, 0, b - a), A("zt"), A("emat", a, b), True, False),
-                    (A(bank, 0, b - a), A("imid"), A(ya, a, b), False, True)])
-                act(A(a2, a, b), A(bank, 0, b - a), AF.Abs, scale=1.0 / MID)
-                continue
-            tt(A(dd, a, b), IND("tab", 4096, off, m0, m1), A("zrep", a, b), AL.subtract)
-            if mode == "V":
-                act(A(a2, a, b), A(dd, a, b), AF.Abs)
-            else:
-                ts(A(a2, a, b), A(dd, a, b), 0.0, AL.max, 2.0, AL.mult)
-        after()
-        for bank, lo, hi in HS:
-            if first:
-                sums_t(bank, lname, a2, lo, hi, True, False)
-            for m0, m1 in (RR if first else RD):
-                if lo <= m0 < hi:
-                    sums_t(bank, other, dd, m0, m1, False, False)
-            if not first:
-                sums_t(bank, lname, a2, lo, hi, False, True)
-
-    def sums_t(bank, sname, src, m0, m1, start, stop):
-        mm([(A(bank, j, 256, 16, p=(m0, m1)), A(src, 16 * m0 + j, 16 * (m1 - 1) + j + 1, 16), A(sname),
-             start and j == 0, stop and j == 15) for j in range(16)], cost=16 * min(64, m1 - m0))
-
-    def choose(i, last, snd):
+    def select(i, t):
         bank, m0, m1 = HS[i]
         p = (m0, m1)
-        tk, uu = "took%d" % i, "uu%d" % i
-        ts(A(tk, p=p), A(bank, 0, 256, p=p), 0.0, AL.is_lt)
-        tt(A(uu, p=p), A(tk, p=p), A("dg" if DL == "p" else "dl", 0, 256, p=p), AL.mult)
-        o = A(("pm", "wk")[i], 128 + m0, 128 + m1)
-        mm([(o, A(snd, 16, 144), A("i64", m0, m1), True, False), (o, A(snd, 176, 304), A("ib", m0, m1), False, False)])
-        mm([(o, A(uu, 0, 128), A("i64", m0, m1), False, False), (o, A(uu, 128, 256), A("ib", m0, m1), False, True)])
-        ts(A("nm" if last else "oe", m0, m1), o, -POF, AL.add)
+        for e, a, b in CFG["DG"]:
+            if m0 <= a < m1:
+                gat(e, A("g2", 16 * a, 16 * b), IND("win", 0, WIN, "ob", a, b))
+        mm([(A(bank, j, 304, 16, p=p), A("g2", 16 * m0 + j, 16 * (m1 - 1) + j + 1, 16), A("sel", 0, 19), j == 0, False)
+            for j in range(16)])
+        mm([(A(bank, 144, 304, p=p), A("c1", m0, m1), A("fw"), False, True)])
+        gat(CFG["SC"][i], SND(t, i, 0, 304, p), A(bank, 0, 304, p=p))
+        if SP:
+            ops[-1]["pre"] = ("sent%d" % i, left * t)
+        o = A(*(("pm", 0, m1 - m0), ("gg", 256, 256 + m1 - m0))[i])
+        mm([(o, SND(t, i, 16, 144, p), A("i64", m0, m1, p=p), True, False),
+            (o, SND(t, i, 176, 304, p), A("ib", m0, m1, p=p), False, True)])
+        ts(A("op_", m0, m1), o, -POF, AL.add)
 
-    def new_digits(t, snd):
-        lst = [(A("dg", 0, 128), A(snd, 16, 144), A("ib"), True, False),
-               (A("dg", 128, 256), A(snd, 176, 304), A("ib"), False, False),
-               (A("dg", 256, 384), A(snd, 176, 304), A("ib"), False, False),
-               (A("dg", 256, 384), A("kt", 0, 128), A("ib"), False, False),
-               (A("dg", 256, 384), A("kt", 128, 256), A("ib"), False, False)]
-        for i, (_b, m0, m1) in enumerate(HS):
-            for c, c2 in ((0, 0), (128, 128), (256, 128)):
-                lst.append((A("dg", c + m0, c + m1), A("uu%d" % i, c2, c2 + 128),
-                            A("ib", m0, m1), False, i == len(HS) - 1 and c == 256))
-        if CF == "v":
-            lst = [e for e in lst if e[0][1][0][1] < 256]
-            lst[-1] = lst[-1][:4] + (True,)
-        mm(lst)
-        act(A("hl"), A("dg", 0, 256), AF.Copy)
-        if CF == "p":
-            act(A("cf", 0, 128), A("dg", 256, 384), AF.Identity, bias=-160.0)
-        windows(t)
+    def m_name(i, t):
+        bank, m0, m1 = HS[i]
+        p = (m0, m1)
+        o = A(*(("gg", 384, 384 + m1 - m0), ("pm", 128, 128 + m1 - m0))[i])
+        c = 256 * i * SP
+        mm([(o, A("lnd%d" % t, c, c + 128, p=p), A("i64", m0, m1, p=p), True, False),
+            (o, A("lnd%d" % t, c + 128, c + 256, p=p), A("ib", m0, m1, p=p), False, True)],
+           ext=("arr%d" % (2 * t + i * SP), arrive))
+        ts(A("om", m0, m1), o, -POF, AL.add)
+
+    nb = [0]
+
+    def distance(i, first):
+        bank, lo, hi = HS[i]
+        off, a2 = ("op_", "a2") if first else ("om", "a3")
+        y0 = 16 * lo + (0 if first else 16 * (hi - lo))
+        for mode, m0, m1 in CH:
+            if not lo <= m0 < hi:
+                continue
+            a, b = 16 * m0, 16 * m1
+            y = A("yy", y0 + a, y0 + b)
+            if mode == "A":
+                bk = ("dfa", "dfb")[nb[0] & 1]
+                nb[0] += 1
+                act(y, IND("tab", 0, 4096, off, m0, m1), AF.Copy)
+                mm([(A(bk, 0, b - a), A("zt"), A("emat", a, b), True, False),
+                    (A(bk, 0, b - a), A("imid"), y, False, True)])
+                act(A(a2, a, b), A(bk, 0, b - a), AF.Abs, scale=1.0 / MID)
+                continue
+            tt(y, IND("tab", 0, 4096, off, m0, m1), A("zrep", a, b), AL.subtract)
+            if mode == "V":
+                act(A(a2, a, b), y, AF.Abs)
+            else:
+                ts(A(a2, a, b), y, 0.0, AL.max, 2.0, AL.mult)
+
+        def part(src, c0, m0, m1, sign, start, stop):
+            mm([(A(bank, j, 128, 16, p=(m0, m1)), A(src, c0 + 16 * m0 + j, c0 + 16 * (m1 - 1) + j + 1, 16),
+                 A(sign), start and j == 0, stop and j == 15) for j in range(16)])
+        if first:
+            part(a2, 0, lo, hi, "s2n", True, False)
+        for mode, m0, m1 in CH:
+            if mode == "R" and lo <= m0 < hi:
+                part("yy", y0, m0, m1, "s2p" if first else "s2n", False, False)
+        if not first:
+            part(a2, 0, lo, hi, "s2p", False, True)
+
+    def choose(i):
+        bank, m0, m1 = HS[i]
+        p = (m0, m1)
+        if tko:
+            ts(A("tk", p=p), A(bank, 0, 128, p=p), 0.0, AL.is_ge, 2.0, AL.mult)
+        else:
+            act(A("tk", p=p), A(bank, 0, 128, p=p), AF.Sign, bias=0.5)
+
+    def new_x(i):
+        bank, m0, m1 = HS[i]
+        p = (m0, m1)
+        o = A(*(("pm", 192, 192 + m1 - m0), ("pm", 0, m1 - m0))[i])
+        mm([(o, A("one", p=p), A("d16", m0, m1, p=p), True, False)])
+        mm([(o, A("tk", p=p), A("ixw", m0, m1, p=p), False, True)])
+        ts(A("oe", m0, m1), o, col("pf", 12), AL.add)
+        for mode, a, b in CH:
+            if m0 <= a < m1:
+                src = IND("yy", 32 * m0, 32 * m1, "oe", a, b)
+                if mode == "A":
+                    gat(CFG["XA"], A("xs", 16 * a, 16 * b), src)
+                else:
+                    tt(A("xs", 16 * a, 16 * b), src, A("zrep", 16 * a, 16 * b), AL.add)
+
+    units = [(i, h[1:]) for i, h in enumerate(HS)] if SP else [(0, (0, 128))]
+
+    def m_diff(t):
+        for i, p in units:
+            mm([(A("wk", 0, 256, p=p), A("ib", *p, p=p), LND(t, i, 0, 256, p), True, False),
+                (A("wk", 0, 128, p=p), A("ibn", *p, p=p), SND(t, i, 16, 144, p), False, False),
+                (A("wk", 128, 256, p=p), A("ibn", *p, p=p), SND(t, i, 176, 304, p), False, True)])
+
+    def mixed(o, t, i, d, full, half, p, start):
+        s0 = (16, 176)[d]
+        if tko:
+            return [(o, LND(t, i, 128 * d, 128 * d + 128, p), A(full, *p, p=p), start, False)]
+        return [(o, LND(t, i, 128 * d, 128 * d + 128, p), A(half, *p, p=p), start, False),
+                (o, SND(t, i, s0, s0 + 128, p), A(half, *p, p=p), False, False)]
+
+    def new_digits(t):
+        tt(A("uu", 0, 128), A("wk", 0, 128), A("tk"), AL.mult)
+        tt(A("uu", 128, 256), A("wk", 128, 256), A("tk"), AL.mult)
+        parts = ((0, 0), (128, 1), (256, 1))
+        for i, p in units:
+            mm([e for c, d in parts for e in mixed(A("dg", c + p[0], c + p[1]), t, i, d, "ib", "ihf", p, c + i == 0)])
+        mm([(A("dg", 256, 384), A("kt"), A("ib"), False, False)])
+        mm([(A("dg", c, c + 128), A("uu", 128 * d, 128 * d + 128), A("ihn"), False, c == 256) for c, d in parts])
+        gat(CFG["HL"], A("hl"), A("dg", 0, 256))
+        act(A("cf", 0, 128), A("dg", 256, 384), AF.Identity, bias=col("pf", 9), scale=S19)
+        windows(t + 1)
+
+    def last_names(i, t):
+        bank, m0, m1 = HS[i]
+        p = (m0, m1)
+        tt(A("uu", 0, 128, p=p), A("wk", 0, 128, p=p), A("tk", p=p), AL.mult)
+        tt(A("uu", 128, 256, p=p), A("wk", 128, 256, p=p), A("tk", p=p), AL.mult)
+        o = A(*(("pm", 192, 192 + m1 - m0), ("pm", 0, m1 - m0))[i])
+        hi = mixed(o, t, i, 0, "i64", "i32", p, True), [(o, A("uu", 0, 128, p=p), A("i32h", *p, p=p), False, False)]
+        lo = mixed(o, t, i, 1, "ib", "ihf", p, False), [(o, A("uu", 128, 256, p=p), A("ihn", *p, p=p), False, True)]
+        mm(hi[0] + lo[0])
+        mm(hi[1] + lo[1])
+        ts(A("nm", m0, m1), o, -POF, AL.add)
 
     def windows(t):
-        w = "w%d" % t
-        for p0, c0, c in ((0, 16, 0), (1, 15, 0), (0, 16 + SEC, 0), (0, 16 + 2 * SEC, 128), (1, 15 + 2 * SEC, 128)):
-            dma("s", A("win", c0, c0 + 2048, p=(p0, 128, 16)), A("hl", c, c + 128), w)
-        if not t or CF == "v":
-            tt(A("cf", 0, 128), A("k256"), A("hl", 128, 256), AL.add)
+        for p0, c0, c in ((0, 16, 0), (1, 15, 0), (0, 16 + SEC, 0), (0, S2, 128), (1, S2 - 1, 128)):
+            x = A("win", c0, c0 + 2048, p=(p0, 128, 16))
+            dma("s", x, A("hl", c, c + 128), "w%d" % t)
 
+    if SP:
+        for i in range(2):
+            ms(SND(0, i, 0, 304, HS[1 - i][1:]), 0.0)
     windows(0)
     late_constants()
     threshold(0)
-    for e in E0:
+    for e in CFG["E0"]:
         egather(*e)
-    z_t()
-    diffs()
-    sums("gg", 17, "zp", "ab", 0, SM, False, True)
-    scatter_constants()
+    mm([(A("dg", 128, 256), A("zs"), A("ib"), True, True)])
+    act(A("zt"), A("dg", 128, 256), AF.Copy)
+    diffs(SM, 128)
+    sums(SM, 128, False)
+    diffs(0, SM)
+    sums(0, SM, True)
     last_constants()
 
     for t in range(RO):
         last = t == RO - 1
-        snd, lnd = "snd%d" % t, "lnd%d" % t
-        def in_carry():
-            z_rep(range(ZN - 1, -1, -1))
-            if t:
-                blocks_u()
-        periods(in_carry)
-        gat("a", A("g2", 16 * BS, 2048), IND("win", 16 + 3 * SEC, "ob", BS, 128))
-        gat("v", A("g2", 0, 16 * BS), IND("win", 16 + 3 * SEC, "ob", 0, BS))
-        mm([(A("dg", j, 304, 16), A("g2", j, 2048, 16), A("sel", 0, 19), j == 0, False) for j in range(16)])
-        fixup()
-        mm([(A("dg", 144, 176), A("fix"), A("ib", 96, 128), False, False),
-            (A("dg", 176, 304), A("fix"), A("ib"), False, True)])
-        act(A(snd), A("dg", 0, 304), AF.Copy)
-        send(t)
-        mm([(A("pm", 0, 128), A(snd, 16, 144), A("i64"), True, False),
-            (A("pm", 0, 128), A(snd, 176, 304), A("ib"), False, True)])
-        if t:
-            blocks_b()
-        ts(A("op_"), A("pm", 0, 128), -POF, AL.add)
-
-        def m_name():
-            mm([(A("gg", 256, 384), A(lnd, 0, 128), A("i64"), True, False),
-                (A("gg", 256, 384), A(lnd, 128, 256), A("ib"), False, True)], ext=("arr%d" % t, arrive))
-            ts(A("om"), A("gg", 256, 384), -POF, AL.add)
-        distance("op_", "s2n", True, m_name)
-
-        def m_diff():
-            if DL == "v":
-                tt(A("dl", 0, 128), (T[lnd][:, 0:128], [("om", 0, 1)]), A(snd, 16, 144), AL.subtract)
-                tt(A("dl", 128, 256), (T[lnd][:, 128:256], [("om", 0, 1)]), A(snd, 176, 304), AL.subtract)
-                return
-            mm([(A("dg", 0, 256), A("ib"), (T[lnd][:], [("om", 0, 1, 256)]), True, False),
-                (A("dg", 0, 128), A("ibn"), A(snd, 16, 144), False, False),
-                (A("dg", 128, 256), A("ibn"), A(snd, 176, 304), False, True)])
-        distance("om", "s2p", False, m_diff)
+        z_rep()
+        periods()
         for i in range(len(HS)):
-            choose(i, last, snd)
+            select(i, t)
+            if SP or i:
+                send(t, i * SP)
+        for i in range(len(HS)):
+            distance(i, True)
+        for i in range(len(HS)):
+            m_name(i, t)
+        m_diff(t)
         if not last:
             threshold(t + 1)
-            for e in EC:
-                egather(*e)
-            new_digits(t + 1, snd)
+        for i in range(len(HS)):
+            distance(i, False)
+            choose(i)
+        if not last:
+            new_x(0)
+            diffs(SM, 128)
+            new_x(1)
+            sums(SM, 128, False)
+            new_digits(t)
             count()
-            diffs()
-            count2()
-            block_max(range(16))
-            sums("gg", 17, "zp", "ab", 0, SM, False, True)
+            diffs(0, SM)
+            sums(0, SM, True)
+            block_max()
             blocks_a()
         else:
-            cp(A("tin"), IND("nm", 128, "o3", 0, 16))
+            for i in range(len(HS)):
+                last_names(i, t)
+            cp(A("tin"), IND("nm", 0, 128, "o3", 0, 16))
             trn(A("tout"), A("tin"))
-            cp(A("nl"), IND("tout", 256, "o4", 0, 8))
-            cp(A("oe"), A("nl"))
-            dma("s", (T.ly[:], []), A("nl"), "out")
-            for e, m0, m1 in EL:
+            cp(A("oe"), IND("tout", 0, 256, "o4", 0, 8))
+            act(A("nl"), IND("tout", 0, 256, "o4", 0, 8), AF.Copy)
+            dma(CFG["LQ"][0], (T.ly[:], []), A("nl"), "out")
+            for e, m0, m1 in CFG["EL"]:
                 egather(e, m0, m1)
                 dma("s", (T.xy[:, 16 * m0:16 * m1], []), A("xs", 16 * m0, 16 * m1), "out")
-            for c in (3, 0, 1, 2):
-                scan(A("ysc", 512 * c, 512 * c + 512), A("m5"), A("xs", 512 * c, 512 * c + 512), 0.0, AL.mult, AL.max)
+            for m0, m1 in CFG["ES"]:
+                scan(A("ysc", 16 * m0, 16 * m1), A("m5", 0, 16 * (m1 - m0)), A("xs", 16 * m0, 16 * m1), 0.0,
+                     AL.mult, AL.max)
             tt(A("zd"), YY, A("zs"), AL.subtract)
             act(A("zt"), A("zd"), AF.Abs)
-            dma("a", (T.zy[:], []), A("zt"), "out")
+            dma(CFG["LQ"][1], (T.zy[:], []), A("zt"), "out")
 
-    hist = {}
-    sent = None
-    for i, o in enumerate(ops):
-        q = o["q"]
-        dep = {}
-        for regs, wr in ((o["r"], False), (o["w"], True)):
-            for name, a, b in regs:
-                for h in hist.get(name, []):
-                    p = ops[h[0]]
-                    if name in PS and p["q"] != q:
-                        dep[h[0]] = 1
-                    elif name in PS and q == "p":
-                        dep.setdefault(h[0], 0)
-                    elif o["dma"] and p["dma"] == o["dma"]:
-                        dep.setdefault(h[0], 0)
-                    elif (wr or h[3]) and a < h[2] and h[1] < b:
-                        dep[h[0]] = 1
-        if o["ext"] is not None:
-            dep[sent] = 1
-        if o["dma"] == "remote":
-            sent = i
-        o["dep"] = dep
-        for regs, wr in ((o["r"], False), (o["w"], True)):
-            for name, a, b in regs:
-                lst = hist.setdefault(name, [])
-                if name in PS:
-                    if lst and ops[lst[-1][0]]["q"] != q:
-                        lq = ops[lst[-1][0]]["q"]
-                        k = len(lst)
-                        while k and ops[lst[k - 1][0]]["q"] == lq:
-                            k -= 1
-                        lst[:] = lst[k:]
-                elif wr and not o["dma"]:
-                    lst[:] = [h for h in lst if h[0] == i or not (a <= h[1] and h[2] <= b)]
-                lst.append((i, a, b, wr))
-    for o in ops:
-        o["suc"] = []
-    for i, o in enumerate(ops):
-        for d, kind in o["dep"].items():
-            ops[d]["suc"].append((i, kind))
     if not ORDER:
+        hist = {}
+        sent = {}
+        for i, o in enumerate(ops):
+            q = o["q"]
+            dep = {}
+            for regs, wr in ((o["r"], False), (o["w"], True)):
+                for x in regs:
+                    name = x[0]
+                    for h, y, hw in hist.get(name, []):
+                        p = ops[h]
+                        if name in PS and p["q"] != q:
+                            dep[h] = 1
+                        elif name in PS and q == "p" and p["rows"] != o["rows"] and x[4] < y[5] and y[4] < x[5]:
+                            dep[h] = 1
+                        elif name in PS and q == "p":
+                            dep.setdefault(h, 0)
+                        elif o["dma"] and p["dma"] == o["dma"]:
+                            dep.setdefault(h, 0)
+                        elif (wr or hw) and meet(x, y):
+                            dep[h] = 1
+            if o["dma"] == "remote":
+                sent[o["ext"][0]] = i
+            elif o["ext"] is not None:
+                dep[sent[o["ext"][0]]] = 1
+            if o["after"] is not None:
+                dep.setdefault(o["after"], 0)
+            o["dep"] = dep
+            for regs, wr in ((o["r"], False), (o["w"], True)):
+                for x in regs:
+                    name = x[0]
+                    lst = hist.setdefault(name, [])
+                    if name in PS:
+                        if lst and ops[lst[-1][0]]["q"] != q:
+                            lq = ops[lst[-1][0]]["q"]
+                            k = len(lst)
+                            while k and ops[lst[k - 1][0]]["q"] == lq:
+                                k -= 1
+                            lst[:] = lst[k:]
+                    elif wr and not o["dma"]:
+                        lst[:] = [h for h in lst if h[0] == i or not covers(x, h[1])]
+                    lst.append((i, x, wr))
+        for o in ops:
+            o["suc"] = []
+        for i, o in enumerate(ops):
+            for d, kind in o["dep"].items():
+                ops[d]["suc"].append((i, kind))
         ORDER.extend(arrange(ops))
     ops = [ops[i] for i in ORDER]
 
@@ -713,15 +848,18 @@ def rank_program(g, core, T, topo):
         q = o["q"]
         need = {}
         for regs, wr in ((o["r"], False), (o["w"], True)):
-            for name, a, b in regs:
+            for x in regs:
+                name = x[0]
                 for h in hist.get(name, []):
                     if name in PS and h["q"] != q:
                         hit = True
-                    elif (name in PS and q == "p") or (o["dma"] and h["sem"] == o["dma"]):
+                    elif name in PS and q == "p":
+                        hit = h["rows"] != o["rows"] and x[4] < h["x"][5] and h["x"][4] < x[5]
+                    elif o["dma"] and h["sem"] == o["dma"]:
                         hit = False
                     else:
-                        hit = (wr or h["wr"]) and a < h["b"] and h["a"] < b
-                    if hit and h["sem"] is not None:
+                        hit = (wr or h["wr"]) and meet(x, h["x"])
+                    if hit:
                         s = h["sem"]
                         v = cnt[s] if h["dma"] else h["val"]
                         if v > need.get(s, (0, None))[0]:
@@ -734,8 +872,10 @@ def rank_program(g, core, T, topo):
             for s2, v2 in clock.items():
                 if kq.get(s2, 0) < v2:
                     kq[s2] = v2
-        if o["ext"] is not None:
-            Q[q].wait_ge(T.sem[o["ext"][0]], o["ext"][1])
+        for e in (o["ext"], o.get("pre")):
+            if e is not None and kq.get(e[0], 0) < e[1]:
+                Q[q].wait_ge(T.sem[e[0]], e[1])
+                kq[e[0]] = e[1]
         ins = o["fn"]()
         if o["dma"] == "remote":
             continue
@@ -745,12 +885,14 @@ def rank_program(g, core, T, topo):
         cnt[sem] = cnt.get(sem, 0) + inc
         clock = dict(kq)
         for regs, wr in ((o["r"], False), (o["w"], True)):
-            for name, a, b in regs:
+            for x in regs:
+                name = x[0]
                 lst = hist.setdefault(name, [])
                 if wr and name not in PS:
-                    lst[:] = [h for h in lst if not (a <= h["a"] and h["b"] <= b and h["sem"] != o["dma"])]
-                lst.append({"q": q, "a": a, "b": b, "wr": wr, "sem": sem, "val": cnt[sem], "dma": bool(o["dma"]),
-                            "clock": clock})
+                    lst[:] = [h for h in lst if not (covers(x, h["x"]) and h["sem"] != o["dma"])]
+                lst.append({"q": q, "x": x, "wr": wr, "sem": sem, "val": cnt[sem], "dma": bool(o["dma"]),
+                            "clock": clock, "rows": o.get("rows")})
     for s, v in cnt.items():
         g.wait_ge(T.sem[s], v)
-    g.wait_ge(T.sem.sent, RO * (mk[0][1] + mk[1][1]))
+    for i in range(1 + SP):
+        g.wait_ge(T.sem["sent%d" % i], RO * left)

@@ -13,47 +13,46 @@ CN = 2.625
 NONE = (CN - SEC) * U
 POF = 65 * 160.0
 MID = 208.0
+QB = 192 - 15.5 / 32
+HS = (("d1", 64, 128), ("d0", 0, 64))
 CFG = {
-    "HS": (("d1", 64, 128), ("d0", 0, 64)),
-    "DG": (("v", 96, 128), ("a", 64, 96), ("v", 34, 64), ("a", 0, 34)),
-    "CH": (("A", 64, 76), ("V", 102, 128), ("V", 76, 102), ("A", 0, 12), ("V", 38, 64), ("V", 12, 38)),
-    "XA": "a",
-    "DC": (("dfa", 97, 128), ("dfb", 65, 97), ("dfa", 39, 65), ("dfb", 13, 39), ("dfa", 0, 13)),
+    "DG": (("v", 96, 128), ("a", 64, 96), ("v", 28, 64), ("a", 0, 28)),
+    "E0": (("v", 100, 128), ("a", 76, 100), ("v", 52, 76), ("a", 0, 14), ("v", 32, 52), ("v", 14, 32)),
+    "CH": (("A", 64, 84), ("R", 96, 128), ("V", 84, 96), ("A", 0, 20), ("S", 32, 64), ("V", 20, 32)),
+    "CHL": None,
+    "DC": (("dfa", 97, 128), ("dfb", 65, 97), ("d0", 33, 65), ("dfa", 21, 33), ("dfb", 0, 21)),
     "SM": 65,
-    "E0": (("v", 102, 128), ("a", 76, 102), ("v", 64, 76), ("v", 38, 64), ("a", 12, 38), ("v", 0, 12)),
-    "EL": (("v", 112, 128), ("a", 0, 20), ("v", 80, 112), ("a", 20, 48), ("a", 48, 68), ("v", 68, 80)),
-    "ES": ((96, 128), (0, 32), (68, 96), (32, 48), (48, 68)), "LQ": "aa",
-    "TK": "a", "SC": "aa", "PH": 1, "SP": 1,
-    "RATES": ((0.1, 0.05, 1.1, 1.56, 3.8, 0.42e-3, 1.4), (0.2, 0.05, 1.1, 1.4, 2.5, 0.42e-3, 0.7),
-              (0.12, 0.05, 1.35, 1.85, 5.0, 0.55e-3, 2.2)),
-    "LOOK": 0.5, "ITER": 30000, "SEED": 12345, "TEMP": 0.003, "CNT": "vv", "HL": "a",
+    "TL": ((0, 4), (4, 8), (8, 12), (12, 16)), "TE": "vava" * 4, "LQ": "aa",
+    "SC": "aa", "HL": "a", "BB": ("d0", "d1", "dg"),
+    "RATES": ((0.1, 0.05, 1.1, 1.56, 3.8, 0.42e-3, 0.9, 0.4e-3), (0.08, 0.05, 1.25, 1.1, 2.0, 0.42e-3, 0.9, 0.25e-3),
+              (0.13, 0.05, 1.25, 2.0, 5.5, 0.42e-3, 0.9, 0.4e-3), (0.26, 0.05, 1.15, 1.4, 3.0, 0.42e-3, 1.8, 0.3e-3)),
+    "LOOK": 0.5, "ITER": 2000, "TEMP": 0.001, "LNS": 12000, "WIN": 60, "TEMP3": 0.001, "SEED": 12345, "WL": 1.3,
 }
 SPAN = []
+DEBUG = []
 ORDER = []
 
 SB = {
     "tab": (4096, BF), "win": (WIN, BF), "xs": (2048, BF), "ab": (2048, BF), "yy": (4096, BF),
     "a2": (2048, BF), "a3": (2048, BF), "zrep": (2048, BF), "emat": (2048, BF), "g2": (2048, BF), "ysc": (2048, BF),
-    "l0s": (128, I32), "zs": (128, BF), "zd": (128, BF), "zt": (128, BF), "ths": (4, I32), "thf": (4, F32),
-    "thc": (4, F32), "thh": (4, BF), "thl": (4, F32),
-    "pi": (8, I32), "pf": (14, F32), "kt": (128, BF), "vv": (128, I32), "xi": (160, F32), "x16": (128, F32),
-    "xr": (128, F32), "selr": (36, F32), "s2p": (8, BF), "s2n": (8, BF), "one": (128, BF), "hl": (256, BF),
-    "dl": (256, BF), "tk": (128, BF), "uu": (256, BF), "zp": (144, BF), "ib": (128, BF), "ibn": (128, BF),
-    "i64": (128, BF), "i32": (128, BF), "ihf": (128, BF), "ihn": (128, BF), "i32h": (128, BF), "ibig": (128, BF),
-    "ixw": (128, BF), "d16": (128, BF), "fw": (160, BF),
+    "l0s": (128, I32), "zs": (128, BF), "zd": (128, BF), "zt": (128, BF), "zt1": (128, BF),
+    "ths": (4, I32), "thf": (128, F32), "thh": (128, BF), "thl": (128, BF),
+    "pi": (10, I32), "pf": (14, F32), "kt": (128, BF), "vv": (128, I32), "xi": (160, F32), "x16": (128, F32),
+    "selr": (20, F32), "s2p": (8, BF), "s2n": (8, BF), "one": (128, BF), "hl": (256, BF),
+    "tk": (128, BF), "uu": (256, BF), "zp": (144, BF), "ib": (128, BF), "ibn": (128, BF),
+    "i64": (128, BF), "i32": (128, BF), "ihf": (128, BF), "ihn": (128, BF), "i32h": (128, BF),
+    "ixw": (128, BF), "d16": (128, BF), "fw": (304, BF), "i64n": (128, BF), "qoff": (128, BF),
     "bp": (128, F32), "bn": (128, F32), "e8": (128, F32), "sel": (20, BF), "sel2": (12, BF), "cm": (34, BF),
-    "m0": (128, BF), "kf": (128, F32), "kq": (128, F32), "two": (128, F32), "cf": (145, F32), "cb": (145, F32),
-    "oi": (64, I32), "o1": (16, U16), "o2": (8, U16), "o3": (16, U16), "o4": (8, U16), "ci": (8, I32),
+    "kq": (128, F32), "two": (128, F32), "cf": (145, F32), "cb": (145, F32),
+    "oi": (32, I32), "o1": (16, U16), "o2": (8, U16), "o3": (16, U16), "o4": (8, U16), "ci": (8, I32),
     "tin": (256, F32), "tout": (256, F32), "nm": (128, F32), "nl": (128, F32),
     "oe": (128, U16), "ob": (128, U16), "op_": (128, U16), "om": (128, U16), "osc": (8, U16),
-    "tq": (128, F32), "h64": (128, F32), "sc1": (292, F32), "cy": (2, F32), "ne": (128, F32), "al": (128, F32),
-    "zz": (128, F32), "qq": (128, F32), "of": (128, F32), "c1": (128, BF),
-    "acb": (128, BF), "qb": (128, BF), "thb": (1024, BF),
+    "tq": (64, F32), "h64": (128, F32), "sc1": (292, F32), "cy": (2, F32), "ne": (128, F32), "al": (128, F32),
+    "zz": (128, F32), "qq": (128, F32), "of": (128, F32), "c1": (128, BF), "acb": (128, BF), "qb": (128, BF),
     "ui": (16, I32), "uj": (8, I32), "sh": (128, I32), "imid": (128, BF), "i32b": (128, BF),
-    "bb": (128, BF), "bbh": (128, BF), "m5": (512, BF),
+    "bb": (128, BF), "bbh": (128, BF), "mb": (512, BF), "snd0": (304, BF), "snd1": (304, BF),
 }
 for _t in range(RO):
-    SB["snd%d" % _t] = (304, BF)
     SB["lnd%d" % _t] = (512, BF)
 PS = ["dfa", "dfb", "gg", "wk", "dg", "pm", "d0", "d1"]
 SCRATCH = {k: ("sbuf", [128, v[0]], v[1]) for k, v in SB.items()}
@@ -95,11 +94,16 @@ def arrange(ops):
             far |= 1 << j
         anc[i] = far
     tabs = []
-    for hop, fix, kf, gat, sca, pec, rem in CFG["RATES"]:
+    for hop, fix, kf, gat, sca, pec, rem, byte in CFG["RATES"]:
         d = [o["c"][0] + o["c"][1] * fix + (o["c"][2] + o["c"][3] * gat + o["c"][4] * sca) * 0.83e-3 * kf
-             + o["c"][5] * pec * kf for o in ops]
+             + o["c"][5] * pec * kf + o["c"][6] * byte for o in ops]
         lat = [rem if o["dma"] == "remote" else o["lat"] for o in ops]
         tabs.append((d, lat, hop))
+    state = [CFG["SEED"]]
+
+    def draw(k):
+        state[0] = (state[0] * 1103515245 + 12345) % 2147483648
+        return (state[0] >> 8) % k
 
     def span(order, tab, old=None, a=0):
         d, lat, hop = tab
@@ -138,79 +142,118 @@ def arrange(ops):
             i = why[i]
         return top, held, end, ok, why
 
+    def deal(seg, tab, worth, free, end, ok):
+        d, lat, hop = tab
+        inside = set(seg)
+        left = {i: sum(1 for j, _k in dep[i] if j in inside) for i in seg}
+        ready = [i for i in seg if not left[i]]
+        est = {i: max([0.0] + [ok[j] if k else end[j] for j, k in dep[i]]) for i in ready}
+        out = []
+        while ready:
+            first = min(ready, key=lambda x: max(free[qs[x]], est[x]) + d[x])
+            q = qs[first]
+            lim = max(free[q], est[first]) + d[first]
+            i = max((x for x in ready if qs[x] == q and est[x] < lim), key=lambda x: worth[x] - max(free[q], est[x]))
+            ready.remove(i)
+            end[i] = free[q] = max(free[q], est[i]) + d[i]
+            ok[i] = end[i] + lat[i] + hop
+            out.append(i)
+            for j, _k in suc[i]:
+                if j in inside:
+                    left[j] -= 1
+                    if not left[j]:
+                        ready.append(j)
+                        est[j] = max(ok[x] if k else end[x] for x, k in dep[j])
+        return out
+
     d, lat, hop = tabs[0]
     pri = [0.0] * n
     for i in range(n - 1, -1, -1):
         pri[i] = d[i] + max([lat[i]] + [(lat[i] + hop) * k + pri[j] for j, k in suc[i]])
-    free = {q: 0.0 for q in set(qs)}
-    left = [len(x) for x in dep]
-    est = [0.0] * n
-    ready = {q: [] for q in sorted(free)}
-    for i in range(n):
-        if not left[i]:
-            ready[qs[i]].append(i)
-    order = []
-    while len(order) < n:
-        t0, q = min((min(max(free[q], est[i]) for i in r), q) for q, r in ready.items() if r)
-        first = min(ready[q], key=lambda i: (max(free[q], est[i]), -pri[i]))
-        i = max((i for i in ready[q] if est[i] <= t0 + CFG["LOOK"] * d[first]), key=lambda i: pri[i])
-        ready[q].remove(i)
-        free[q] = max(free[q], est[i]) + d[i]
-        order.append(i)
-        for j, k in suc[i]:
-            est[j] = max(est[j], free[q] + (lat[i] + hop) * k)
-            left[j] -= 1
-            if not left[j]:
-                ready[qs[j]].append(j)
+    order = deal(list(range(n)), tabs[0], pri, dict.fromkeys(names, 0.0), [0.0] * n, [0.0] * n)
     res = [span(order, tb) for tb in tabs]
     base = [r[0] for r in res]
     cur = best = float(len(tabs))
-    keep, took = order, 0
-    seed = CFG["SEED"]
-    for it in range(CFG["ITER"]):
-        seed = (seed * 1103515245 + 12345) % 2147483648
-        held = res[(seed >> 8) % len(tabs)][1]
-        if not held:
-            continue
-        seed = (seed * 1103515245 + 12345) % 2147483648
-        i = held[(seed >> 8) % len(held)]
-        seed = (seed * 1103515245 + 12345) % 2147483648
-        b = order.index(i)
-        a, step = b, 1 + (seed >> 8) % 8 // 3
-        early = (seed >> 20) & 1
-        while step and a > 0:
-            a -= 1
-            if qs[order[a]] == qs[i]:
-                step -= 1
-        seg = order[a:b + 1]
-        if early:
-            move = {i}
-            for x in reversed(seg):
-                if x in move:
-                    move.update(j for j, _k in dep[x])
-            if seg[0] in move:
+    keep, fresh = order, True
+    swaps, total = CFG["ITER"], CFG["ITER"] + CFG["LNS"]
+    for it in range(total):
+        if it == swaps:
+            order, cur, fresh = keep, best, True
+            res = [span(order, tb) for tb in tabs]
+        if fresh:
+            order = sorted(order, key=lambda x: res[0][2][x] - tabs[0][0][x])
+            tails = []
+            for d, lat, hop in tabs * (it >= swaps):
+                tail, nxt = [0.0] * n, dict.fromkeys(names, 0.0)
+                for i in reversed(order):
+                    v = max(lat[i], nxt[qs[i]])
+                    for j, k in suc[i]:
+                        v = max(v, (lat[i] + hop) * k + tail[j])
+                    tail[i] = nxt[qs[i]] = v + d[i]
+                tails.append(tail)
+            fresh = False
+        m = draw(len(tabs))
+        if it < swaps:
+            held = res[m][1]
+            if not held:
                 continue
-            seg = [x for x in seg if x in move] + [x for x in seg if x not in move]
+            i = held[draw(len(held))]
+            b = order.index(i)
+            a, step = b, 1 + draw(8) // 3
+            while step and a > 0:
+                a -= 1
+                if qs[order[a]] == qs[i]:
+                    step -= 1
+            seg = order[a:b + 1]
+            if draw(2):
+                move = {i}
+                for x in reversed(seg):
+                    if x in move:
+                        move.update(j for j, _k in dep[x])
+                if seg[0] in move:
+                    continue
+                new_seg = [x for x in seg if x in move] + [x for x in seg if x not in move]
+            else:
+                move = {seg[0]}
+                for x in seg:
+                    if x in move:
+                        move.update(j for j, _k in suc[x])
+                if i in move:
+                    continue
+                new_seg = [x for x in seg if x not in move] + [x for x in seg if x in move]
+            slack = CFG["TEMP"] * (1 - it / swaps)
         else:
-            move = {seg[0]}
-            for x in seg:
-                if x in move:
-                    move.update(j for j, _k in suc[x])
-            if i in move:
-                continue
-            seg = [x for x in seg if x not in move] + [x for x in seg if x in move]
-        cand = order[:a] + seg + order[b + 1:]
+            d, lat, hop = tabs[m]
+            size = 12 + draw(CFG["WIN"])
+            a = draw(n - 12)
+            seg = order[a:a + size]
+            inside = set(seg)
+            after = {}
+            for x in order[a + size:a + size + 80]:
+                after.setdefault(qs[x], tails[m][x])
+            noise = 1.2 * (draw(1000) / 1000) ** 2
+            worth = {}
+            for i in reversed(seg):
+                v = max(lat[i], after.get(qs[i], 0.0))
+                for j, k in suc[i]:
+                    v = max(v, (lat[i] + hop) * k + (worth[j] if j in inside else tails[m][j]))
+                worth[i] = v + d[i]
+            for i in seg:
+                worth[i] += noise * draw(1000) / 1000
+            free = dict.fromkeys(names, 0.0)
+            for x in order[max(0, a - 120):a]:
+                free[qs[x]] = res[m][2][x]
+            new_seg = deal(seg, tabs[m], worth, free, list(res[m][2]), list(res[m][3]))
+            slack = CFG["TEMP3"] * (total - it) / (total - swaps)
+        cand = order[:a] + new_seg + order[a + len(seg):]
         new = [span(cand, tb, r, a) for tb, r in zip(tabs, res)]
         val = sum(r[0] / bs for r, bs in zip(new, base))
-        seed = (seed * 1103515245 + 12345) % 2147483648
-        if val <= cur + CFG["TEMP"] * (1 - it / CFG["ITER"]) * ((seed >> 8) % 1000) / 1000:
-            cur, order, res = val, cand, new
-            took += 1
-            if took % 20 == 0:
-                order = sorted(order, key=lambda x: res[0][2][x] - tabs[0][0][x])
+        if val <= cur + slack * draw(1000) / 1000:
+            cur, order, res, fresh = val, cand, new, True
             if val < best:
                 best, keep = val, cand
     SPAN[:] = [base, [span(keep, tb)[0] for tb in tabs]]
+    DEBUG[:] = [ops, span(keep, tabs[0]), tabs[0]]
     return keep
 
 
@@ -229,8 +272,8 @@ def rank_program(g, core, T, topo):
     n = len(T.cores)
     Q = {"v": g.vector, "a": g.scalar, "p": g.tensor, "g": g, "s": g.sync}
     AL, AF = AluOpType, ActivationFunctionType
-    HS, CH, DC, SM = CFG["HS"], CFG["CH"], CFG["DC"], CFG["SM"]
-    tko = 1 if CFG["TK"] == "v" else 0
+    CH, DC, SM = list(CFG["CH"]), CFG["DC"], CFG["SM"]
+    ZT = ["zt", "zt1"]
     ops = []
 
     def A(name, a=0, b=None, s=1, p=None):
@@ -254,30 +297,30 @@ def rank_program(g, core, T, topo):
     def add(q, fn, reads, writes, dma=None, ext=None, cost=None, after=None):
         lat = 0.0
         if dma == "remote":
-            d = (1.2, 0, 0, 0, 0, 0)
+            d = (1.2, 0, 0, 0, 0, 0, 0)
         elif dma:
             wide = (writes if dma[0] == "l" else reads)[0]
-            busy = 0.24 + wide[3] * (2 if SB[wide[0]][1] == BF else 4) * 0.45e-3
-            d, lat = ((busy, 0, 0, 0, 0, 0), 1.4) if q == "s" else ((0.06, 0, 0, 0, 0, 0), 1.4 + busy)
+            size = wide[3] * (2 if SB[wide[0]][1] == BF else 4)
+            d, lat = ((0.24, 0, 0, 0, 0, 0, size), CFG["WL"]) if q == "s" else ((0.06, 0, 0, 0, 0, 0, 0), 1.7)
         elif q == "p":
-            d, lat = (0, 0, 0, 0, 0, cost), 0.06
+            d, lat = (0, 0, 0, 0, 0, cost, 0), 0.06
         else:
             ind = [-x[3] for x in reads if x[3] < 0]
             if ind:
-                d = (0.01, 1, 0, 0, ind[0], 0) if writes[0][3] == 0 else (0.01, 1, 0, ind[0], 0, 0)
+                d = (0.01, 1, 0, 0, ind[0], 0, 0) if writes[0][3] == 0 else (0.01, 1, 0, ind[0], 0, 0, 0)
             else:
                 nel = writes[0][3]
                 if nel == 1 and reads:
                     nel = reads[0][3]
                 big = [x for x in reads + writes if x[3] >= nel]
                 if q == "g":
-                    d = (0.15, 0, 2 * nel, 0, 0, 0)
+                    d = (0.15, 0, 2 * nel, 0, 0, 0, 0)
                 else:
                     two = all(SB.get(x[0], (0, 0))[1] in (BF, U16) for x in big)
                     rate = 0.5 if two and q == "v" else 1.0
                     if cost == "tt" and not any(x[0] in PS for x in reads):
                         rate *= 2
-                    d = (0, 1, max(64, nel * rate), 0, 0, 0)
+                    d = (0.01 * (q == "a"), 1, max(64, nel * rate), 0, 0, 0, 0)
         ops.append({"q": q, "fn": fn, "r": reads, "w": writes, "dma": dma, "ext": ext, "c": d, "lat": lat,
                     "after": after})
         return len(ops) - 1
@@ -359,115 +402,107 @@ def rank_program(g, core, T, topo):
     ts(col("pi", 1), col("pi", 0), 15, AL.bitwise_and)
     ts(A("oi", 16, 32), A("oi", 0, 16), 127, AL.bitwise_and)
     ts(col("pi", 2), col("pi", 0), 31, AL.bitwise_and)
+    ts(col("pi", 3), col("pi", 0), 63, AL.bitwise_and)
     cp(A("o1"), A("oi", 16, 32))
-    cp(A("pf", 0, 3), A("pi", 0, 3))
+    cp(A("pf", 0, 4), A("pi", 0, 4))
     ts(A("tq", 0, 8), A("xi", 0, 8), 32.0, AL.mult, col("pf", 2), AL.add)
     cp(A("o2"), A("tq", 0, 8))
     iota(A("x16"), [[16, 8], [0, 16]], 0, 0)
-    iota(A("xr"), [[0, 8], [1, 16]], 0, 0)
     iota(A("selr", 0, 1), [[0, 1]], 112, 0)
     iota(A("selr", 1, 9), [[16, 8]], 0, 0)
     iota(A("selr", 9, 11), [[16, 2]], 97, 0)
     iota(A("selr", 11, 19), [[16, 8]], 1, 0)
-    iota(A("one"), [[0, 128]], 1, 0)
-    iota(A("win", S2 - 1, WIN), [[0, WIN - S2 + 1]], 256, 0)
     add("g", lambda: g.affine_select(T.emat[:], T.win[:, 16 + SEC:16 + 2 * SEC], [[-1, 8], [0, 16], [-8, 16]],
                                      AL.is_equal, 0.0, 0, 1), A("win", 16 + SEC, 16 + 2 * SEC)[1], A("emat")[1])
+    iota(A("win", S2 - 1, WIN), [[0, WIN - S2 + 1]], 256, 0)
+    iota(A("mb"), [[0, 32], [1024, 16]], -512, 0)
     on_g = [i for i, o in enumerate(ops) if o["q"] == "g"]
     for i, k in zip(on_g, on_g[1:]):
         ops[k]["after"] = i
-    tt(col("pf", 3), col("pf", 0), col("pf", 1), AL.subtract)
-    lin(col("pf", 5), col("pf", 3), 1.0, 15.0)
+    tt(col("pf", 4), col("pf", 0), col("pf", 1), AL.subtract)
+    lin(col("pf", 5), col("pf", 4), 1.0, 15.0)
     lin(col("pf", 6), col("pf", 0), 16.0)
-    lin(col("pf", 8), col("pf", 0), 256.0)
     lin(col("pf", 9), col("pf", 1), 128 * U)
-    lin(col("pf", 10), col("pf", 1), -256 * U)
-    lin(col("pf", 11), col("pf", 0), 1.0, -1.0)
     lin(A("kq"), A("xi", 0, 128), U, col("pf", 9))
     ms(A("win", 0, 16 + SEC), 192.0)
 
     cp(A("tin"), IND("l0s", 0, 128, "o1", 0, 16))
     trn(A("tout"), A("tin"))
-    cp(A("nm"), IND("tout", 0, 256, "o2", 0, 8))
-    cp(A("oe"), A("nm"))
-    act(A("hl", 0, 128), A("nm"), AF.Identity, bias=160 - 31.5 / 64, scale=1.0 / 64)
-    act(A("h64"), A("hl", 0, 128), AF.Identity, bias=POF, scale=-64.0)
+    cp(A("oe"), IND("tout", 0, 256, "o2", 0, 8))
+    act(A("nm"), IND("tout", 0, 256, "o2", 0, 8), AF.Copy)
+    lin(A("hl", 0, 128), A("nm"), 1.0 / 64, 160 - 31.5 / 64)
+    lin(A("h64"), A("hl", 0, 128), -64.0, POF)
     tt(A("hl", 128, 256), A("nm"), A("h64"), AL.add)
     lin(A("h64"), A("hl", 128, 256), S19)
     tt(A("cf", 0, 128), A("h64"), A("kq"), AL.add)
     ts(A("ib"), A("xi", 0, 128), col("pf", 0), AL.is_equal)
     eye("ibn", -1.0)
-    ts(A("e8", p=(0, 8)), A("x16", p=(0, 8)), col("pf", 6, (0, 8)), AL.is_equal)
-    cp(A("thf", p=(0, 8)), A("ths", p=(0, 8)))
-    mm([(A("dg", 0, 4), A("e8", p=(0, 8)), A("thf", p=(0, 8)), True, True)])
-    eye("ibig", -BIG)
+    ms(A("one"), 1.0)
+    eye("i32b", 32 * BIG, "one")
+    ts(A("e8", p=(0, 8)), A("x16", p=(0, 8)), col("pf", 6, (0, 8)), AL.is_equal, -1.0 / 32, AL.mult)
+    ms(A("thf", p=(0, 8)), 0.0)
+    ts(A("thf", 0, 128, 32, p=(0, 8)), A("ths", p=(0, 8)), 0.5, AL.add)
+    mm([(A("dg", 0, 128), A("thf", p=(0, 8)), A("e8", p=(0, 8)), True, True)])
+    act(A("thh"), A("dg", 0, 128), AF.Copy)
+    tt(A("thl"), A("dg", 0, 128), A("thh"), AL.subtract)
     ts(A("zp"), A("xi", 0, 144), col("pf", 5), AL.is_equal, BIG, AL.mult)
-    lin(A("thc", 0, 1), A("dg", 0, 1), 1.0, 0.5)
-    lin(A("thc", 1, 4), A("dg", 1, 4), 1.0, 5120.5 + 1024 * (1 + tko))
-    lin(A("thh"), A("thc"), 1.0)
-    tt(A("thl"), A("thc"), A("thh"), AL.subtract)
-    for t in range(RO):
-        lin(A("thb", 256 * t, 256 * t + 128), A("xi", 0, 128), 0.0, col("thh", t))
-        lin(A("thb", 256 * t + 128, 256 * t + 256), A("xi", 0, 128), 0.0, col("thl", t))
     ms(col("ab", 0), 512.0)
 
     def late_constants():
-        ts(A("s2p"), A("selr", 1, 9), col("pf", 3), AL.is_equal)
+        ts(A("s2p"), A("selr", 1, 9), col("pf", 4), AL.is_equal)
         lin(A("s2n"), A("s2p"), -1.0)
         lin(A("two", 1, 128), A("xi", 1, 128), 0.0, 2 * U)
         lin(A("two", 0, 1), A("xi", 0, 1), 0.0)
-        lin(A("kt"), A("xr"), 0.0, col("pf", 8))
+        lin(col("pf", 8), col("pf", 0), 256.0)
+        lin(A("kt"), A("xi", 0, 128), 0.0, col("pf", 8))
         eye("i64", 64.0)
-        eye("i32", 32.0)
-        eye("i32h", -32.0)
         eye("ihf", 0.5)
         eye("ihn", -0.5)
         eye("imid", -MID)
-        eye("i32b", 32 * BIG)
-        for _b, m0, m1 in HS:
-            act(A("ixw", m0, m1), A("ib", m0, m1), AF.Copy, scale=-8.0 * (m1 - m0))
-            lin(col("pf", 13), col("pf", 6), 1.0, -16.0 * m0)
-            act(A("d16", m0, m1), A("ib", m0, m1), AF.Identity, scale=col("pf", 13))
-        lin(col("pf", 12), col("pf", 1), 1.0, 8.0 * (HS[0][2] - HS[0][1]) * (1 + tko))
-        act(A("fw", 0, 32), A("ib", 96, 128), AF.Copy, scale=-1.0 / S19)
-        act(A("fw", 32, 160), A("ib"), AF.Copy, scale=-1.0 / S19)
-        ts(A("bp"), A("x16"), col("pf", 3), AL.is_equal)
+        eye("ixw", -512.0)
+        lin(col("pf", 13), col("pf", 3), 16.0, 512.0)
+        act(A("d16"), A("ib"), AF.Identity, scale=col("pf", 13))
+        ms(A("fw", 0, 144), 0.0)
+        act(A("fw", 144, 176), A("ib", 96, 128), AF.Copy, scale=-1.0 / S19)
+        act(A("fw", 176, 304), A("ib"), AF.Copy, scale=-1.0 / S19)
+        ts(A("bp"), A("x16"), col("pf", 4), AL.is_equal)
         eye("bn", -1.0, "bp")
         eye("bb", 1.0, "bp")
-        eye("bbh", BIG / 2, "bp")
+        eye("bbh", BIG / 2, "one")
+        eye("i64n", -1.0 / 64)
+        lin(A("qoff"), A("one"), -192.0)
+        lin(col("pf", 11), col("pf", 0), 1.0, -1.0)
         ts(A("sel", 0, 19), A("selr", 0, 19), col("pf", 0), AL.is_equal)
         ts(A("sel2", 0, 10), A("selr", 9, 19), col("pf", 11), AL.is_equal)
         tt(A("sel", 9, 19), A("sel", 9, 19), A("sel2", 0, 10), AL.add)
         ts(A("cf", 128, 145), A("xi", 0, 17), col("pf", 1), AL.is_le, BIG, AL.mult)
-        ts(A("cb", 0, 17), A("xi", 0, 17), col("pf", 1), AL.is_gt, BIG, AL.mult)
-        lin(A("cb", 0, 17), A("cb", 0, 17), 1.0, -1.0)
+        lin(A("cb", 0, 17), A("cf", 128, 145), -1.0, BIG - 1.0)
         lin(A("cb", 17, 145), A("kq"), -1.0, CN * U)
         lin(A("wk", 256, 384), A("kq"), 2.0)
         lin(A("wk", 384, 512), A("kq"), 2.0, (2 * SEC + 0.25 - CN) * U)
-        ts(A("tq", 64, 81), A("xi", 0, 17), col("pf", 1), AL.is_ge, -BIG, AL.mult)
-        lin(A("cm", 0, 17), A("tq", 64, 81), 1.0, col("pf", 10))
+        lin(col("pf", 10), col("pf", 1), -256 * U)
+        ts(A("tq", 16, 33), A("xi", 0, 17), col("pf", 1), AL.is_ge, -BIG, AL.mult)
+        lin(A("cm", 0, 17), A("tq", 16, 33), 1.0, col("pf", 10))
         lin(A("cm", 17, 33), A("cf", 128, 144), 1.0, 1.0)
-        act(A("m0"), A("xr"), AF.Sign)
         ms(A("gg", 0, 17), -BIG)
         ms(A("gg", 145, 162), -BIG)
         ms(A("pm", 289, 290), -NONE)
         ms(A("sc1", 290, 291), NONE)
 
     def last_constants():
-        ts(A("tq", 112, 120), A("xi", 0, 8), 16.0, AL.mult, col("pf", 1), AL.add)
-        cp(A("o3", 0, 16, 2), A("tq", 112, 120))
-        cp(A("o3", 1, 16, 2), A("tq", 112, 120))
-        ts(A("ci"), A("tq", 112, 120), 32.0, AL.mult)
-        ts(col("pi", 3), col("pi", 0), 7, AL.bitwise_and)
-        ts(col("pi", 4), col("pi", 0), 3, AL.logical_shift_right, 1, AL.bitwise_and)
-        ts(col("pi", 5), col("pi", 0), 16, AL.bitwise_and)
-        ts(col("pi", 6), col("pi", 3), 32.0, AL.mult)
-        tt(col("pi", 7), col("pi", 4), col("pi", 5), AL.add)
-        tt(col("pf", 7), col("pi", 6), col("pi", 7), AL.add)
-        ts(A("tq", 120, 128), A("xi", 0, 8), 2.0, AL.mult, col("pf", 7), AL.add)
-        cp(A("o4"), A("tq", 120, 128))
-        for c in range(4):
-            act(A("m5", 128 * c, 128 * c + 128), A("m0"), AF.Copy)
+        ts(A("tq", 40, 48), A("xi", 0, 8), 16.0, AL.mult, col("pf", 1), AL.add)
+        ts(A("ci"), A("tq", 40, 48), 32.0, AL.mult)
+        cp(A("o3", 0, 16, 2), A("tq", 40, 48))
+        cp(A("o3", 1, 16, 2), A("tq", 40, 48))
+        ts(col("pi", 4), col("pi", 0), 7, AL.bitwise_and)
+        ts(col("pi", 5), col("pi", 0), 3, AL.logical_shift_right, 1, AL.bitwise_and)
+        ts(col("pi", 6), col("pi", 0), 16, AL.bitwise_and)
+        ts(col("pi", 7), col("pi", 4), 32.0, AL.mult)
+        tt(col("pi", 8), col("pi", 5), col("pi", 6), AL.add)
+        tt(col("pf", 7), col("pi", 7), col("pi", 8), AL.add)
+        ts(A("o4"), A("xi", 0, 8), 2.0, AL.mult, col("pf", 7), AL.add)
+        eye("i32", 32.0)
+        eye("i32h", -32.0)
 
     def zl(j):
         return A("zp", 15 - j, 143 - j)
@@ -477,66 +512,66 @@ def rank_program(g, core, T, topo):
             for j in range(16)])
 
     def threshold(t):
-        mm([(A("gg", 17, 145), A("ibig"), A("thb", 256 * t, 256 * t + 128), True, False),
-            (A("gg", 17, 145), A("ibig"), A("thb", 256 * t + 128, 256 * t + 256), False, False)])
+        p = (32 * t, 32 * t + 1)
+        mm([(A("gg", 17, 145), A("thh", p=p), A("i32b", p=p), True, False),
+            (A("gg", 17, 145), A("thl", p=p), A("i32b", p=p), False, False)])
+        if t:
+            mm([(A("gg", 17, 145), A("qoff"), A("i32b"), False, False)])
 
     def count():
-        mm([(A("d1", 256, 384), A("tk"), A("one"), True, True)])
-        gat(CFG["CNT"][0], A("acb"), A("d1", 256, 384))
-        mm([(A("d1", 128, 256), A("bb"), A("acb"), True, True)])
-        if CFG["CNT"][1] == "a":
-            act(A("qb"), A("d1", 128, 256), AF.Identity, bias=160 + 32 * (1 + tko) - 15.5 / 32, scale=-1.0 / 64)
-        else:
-            ts(A("qb"), A("d1", 128, 256), -1.0 / 64, AL.mult, 160 + 32 * (1 + tko) - 15.5 / 32, AL.add)
-        mm([(A("gg", 17, 145), A("bbh"), A("acb"), False, False), (A("gg", 17, 145), A("i32b"), A("qb"), False, False)])
-
-    def diff(bank, a, b):
-        lst = []
-        if a == 0:
-            lst += [(A(bank, 1, 16), A("ib"), A("xs", 1, 16), True, False),
-                    (A(bank, 1, 16), A("ibn"), A("xs", 2032, 2047), False, True)]
-        a1 = max(a, 16)
-        lst += [(A(bank, a1 - a, b - a), A("ib"), A("xs", a1, b), True, False),
-                (A(bank, a1 - a, b - a), A("ibn"), A("xs", a1 - 16, b - 16), False, True)]
-        mm(lst)
-        a2 = max(a, 1)
-        act(A("ab", a2, b), A(bank, a2 - a, b - a), AF.Abs)
+        mm([(col("d1", 256), A("tk"), col("one", 0), True, True)])
+        ts(A("acb"), A("bb"), col("d1", 256), AL.mult)
+        mm([(col("d1", 128), A("acb"), col("one", 0), True, True)])
+        ts(A("qb"), A("i64n"), col("d1", 128), AL.mult, QB, AL.add)
+        mm([(A("gg", 17, 145), A("acb"), A("bbh"), False, False), (A("gg", 17, 145), A("qb"), A("i32b"), False, False)])
 
     def diffs(lo, hi):
         for bank, m0, m1 in DC:
-            if lo <= m0 < hi:
-                diff(bank, 16 * m0, 16 * m1)
-
-    def egather(e, m0, m1):
-        gat(e, A("xs", 16 * m0, 16 * m1), IND("tab", 0, 4096, "oe", m0, m1))
+            if not lo <= m0 < hi:
+                continue
+            a, b = 16 * m0, 16 * m1
+            lst = []
+            if a == 0:
+                lst += [(A(bank, 1, 16), A("ib"), A("xs", 1, 16), True, False),
+                        (A(bank, 1, 16), A("ibn"), A("xs", 2032, 2047), False, True)]
+            a1 = max(a, 16)
+            lst += [(A(bank, a1 - a, b - a), A("ib"), A("xs", a1, b), True, False),
+                    (A(bank, a1 - a, b - a), A("ibn"), A("xs", a1 - 16, b - 16), False, True)]
+            mm(lst)
+            a2 = max(a, 1)
+            act(A("ab", a2, b), A(bank, a2 - a, b - a), AF.Abs)
 
     def z_rep():
         nb = 0
         for _b, lo, hi in HS:
-            m0 = max([lo] + [y for mode, x, y in CH if mode == "A" and lo <= x < hi])
+            mine = [(x, y) for mode, x, y in CH if mode not in "AB" and lo <= x < hi]
+            m0, hi = min(mine)[0], max(mine)[1]
             k = -(-(hi - m0) // 32)
             for c in range(k - 1, -1, -1):
                 bank = ("dfa", "dfb")[nb & 1]
                 nb += 1
                 a, b = 16 * (m0 + (hi - m0) * c // k), 16 * (m0 + (hi - m0) * (c + 1) // k)
-                mm([(A(bank, 0, b - a), A("zt"), A("emat", a, b), True, True)])
+                mm([(A(bank, 0, b - a), A(ZT[0]), A("emat", a, b), True, True)])
                 act(A("zrep", a, b), A(bank, 0, b - a), AF.Copy, scale=1.0 / MID)
-
-    def block_max():
-        for j in range(16):
-            scan(A("ysc", 128 * j, 128 * j + 128), A("m0", 0, 128), A("xs", j, 2048, 16), 0.0, AL.mult, AL.max)
 
     YY = A("ysc", 15, 2048, 16)
 
-    def blocks_a():
-        mm([(A("dg", 0, 128), YY, A("ib"), True, False), (A("dg", 0, 128), A("zs"), A("ibn"), False, True)])
-        act(A("zt"), A("dg", 0, 128), AF.Abs)
-        mm([(A("dg", 384, 392), zl(r), A("ysc", 15 + 16 * r, 2048, 256), r == 0, r == 15) for r in range(16)])
-        mm([(A("dg", 128, 256), A("ib"), YY, True, False), (A("dg", 128, 256), A("ibn"), A("zs"), False, True),
-            (A("dg", 256, 384), A("ib"), YY, True, False), (A("dg", 256, 384), A("ib"), A("zs"), False, True)])
-        ts(A("ui", 0, 8), A("dg", 384, 392), 1.0 / BIG, AL.mult)
-        ts(A("sh"), A("dg", 256, 384), 0.5, AL.mult, -0.25, AL.add)
-        act(A("zs"), A("dg", 128, 256), AF.Abs)
+    def blocks(t):
+        for j in range(16):
+            scan(A("ysc", 128 * j, 128 * j + 128), A("mb", 0, 128), A("xs", j, 2048, 16), 0.0, AL.min, AL.max)
+        old = A(ZT[0])
+        ZT.reverse()
+        mm([(A("dg", 0, 128), A("ibn"), old, True, False), (A("dg", 0, 128), YY, A("ib"), False, True)])
+        act(A(ZT[0]), A("dg", 0, 128), AF.Abs)
+        ub, sb, zb = CFG["BB"]
+        for r0 in range(0, 16, 8):
+            mm([(A(ub, 384, 392), zl(r), A("ysc", 15 + 16 * r, 2048, 256), r == 0, r == 15) for r in range(r0, r0 + 8)])
+        mm([(A(sb, 256, 384), old, A("ib"), True, False), (A(sb, 256, 384), A("ib"), YY, False, True)])
+        if t == RO - 2:
+            mm([(A(zb, 128, 256), old, A("ibn"), True, False), (A(zb, 128, 256), A("ib"), YY, False, True)])
+            act(A("zs"), A(zb, 128, 256), AF.Abs)
+        ts(A("sh"), A(sb, 256, 384), 0.5, AL.mult, -0.25, AL.add)
+        ts(A("ui", 0, 8), A(ub, 384, 392), 1.0 / BIG, AL.mult)
         ts(A("ui", 8, 16), A("ui", 0, 8), 31, AL.bitwise_and)
         tt(A("uj"), A("ui", 8, 16), A("ci"), AL.add)
         cp(A("osc"), A("uj"))
@@ -552,51 +587,27 @@ def rank_program(g, core, T, topo):
         red(col("cy", 0), A("pm", 256, 272), AL.max)
         red(col("cy", 1), A("pm", 273, 290), AL.min)
         scan(A("wk", 0, 128), A("two"), A("al"), col("cy", 0), AL.add, AL.min)
-        parts = [(m0, m1) for _b, m0, m1 in HS] if CFG["PH"] == 2 else [(0, 128)]
-        for step in range(8):
-            for a, b in parts:
-                if step == 0:
-                    ts(A("ne", a, b), A("sc1", 163 + a, 163 + b), col("cy", 1), AL.max)
-                elif step == 1:
-                    tt(A("zz", a, b), A("wk", a, b), A("ne", a, b), AL.add)
-                elif step == 2:
-                    tt(A("wk", 128 + a, 128 + b), A("wk", 384 + a, 384 + b), A("ne", a, b), AL.add)
-                elif step == 3:
-                    ts(A("vv", a, b), A("zz", a, b), float(SEC), AL.mult, 0.0, AL.max)
-                elif step == 4:
-                    tt(A("qq", a, b), A("wk", a, b), A("vv", a, b), AL.add)
-                elif step == 5:
-                    tt(A("of", a, b), A("wk", 128 + a, 128 + b), A("qq", a, b), AL.min)
-                elif step == 6:
-                    ts(A("ob", a, b), A("of", a, b), float(SEC), AL.mult, 16.75, AL.add)
+        ts(A("ne"), A("sc1", 163, 291), col("cy", 1), AL.max)
+        tt(A("zz"), A("wk", 0, 128), A("ne"), AL.add)
+        tt(A("wk", 128, 256), A("wk", 384, 512), A("ne"), AL.add)
+        ts(A("vv"), A("zz"), float(SEC), AL.mult, 0.0, AL.max)
+        tt(A("qq"), A("wk", 0, 128), A("vv"), AL.add)
+        tt(A("of"), A("wk", 128, 256), A("qq"), AL.min)
+        ts(A("ob"), A("of"), float(SEC), AL.mult, 16.75, AL.add)
         ts(A("c1"), A("zz"), 192 * S19, AL.max, 256 * S19, AL.min)
 
     d1, d2 = T.cores[(rank + 1) % n], T.cores[(rank + 2) % n]
     mk = masks(topo, core, [d1, d2])
     s1, s2 = T.cores[(rank - 1) % n], T.cores[(rank - 2) % n]
     arrive = masks(topo, s1, [core, T.cores[(rank + 1) % n]])[0][1] + masks(topo, s2, [s1, core])[1][1]
-
     left = mk[0][1] + mk[1][1]
-    SP = CFG["SP"]
 
-    def SND(t, i, a, b, p=None):
-        return A("snd%d" % (i if SP else t), a, b, p=p)
+    def SND(i, a, b, p=None):
+        return A("snd%d" % i, a, b, p=p)
 
     def LND(t, i, a, b, p=None):
-        x = A("lnd%d" % t, 256 * i * SP + a, 256 * i * SP + b, p=p)
+        x = A("lnd%d" % t, 256 * i + a, 256 * i + b, p=p)
         return x[0], x[1] + col("om", HS[i][1])[1]
-
-    def send(t, i):
-        def fn():
-            trs = []
-            for d, (m, _c), a, b in ((d1, mk[0], 0, 0), (d2, mk[1], 144, 128)):
-                ad = topo.addr(d)
-                trs.append(RemoteDMATransfer(dst_ids=[DstId(rid=ad[0], pnc=ad[1])], dma_engine_mask=m,
-                                             remote_sem=T.sem["arr%d" % (2 * t + i)], src=SND(t, i, a, a + 128)[0],
-                                             dst=LND(t, i, b, b + 128)[0]))
-            g.remote_dma_fused(trs, local_sem=T.sem["sent%d" % i])
-            return None
-        add("g", fn, SND(t, i, 0, 304)[1], [], dma="remote", ext=("arr%d" % (2 * t + i), 0))
 
     def select(i, t):
         bank, m0, m1 = HS[i]
@@ -604,25 +615,35 @@ def rank_program(g, core, T, topo):
         for e, a, b in CFG["DG"]:
             if m0 <= a < m1:
                 gat(e, A("g2", 16 * a, 16 * b), IND("win", 0, WIN, "ob", a, b))
-        mm([(A(bank, j, 304, 16, p=p), A("g2", 16 * m0 + j, 16 * (m1 - 1) + j + 1, 16), A("sel", 0, 19), j == 0, False)
+        mm([(A(bank, 0, 304, p=p), A("c1", m0, m1), A("fw"), True, False)])
+        mm([(A(bank, j, 304, 16, p=p), A("g2", 16 * m0 + j, 16 * (m1 - 1) + j + 1, 16), A("sel", 0, 19), False, j == 15)
             for j in range(16)])
-        mm([(A(bank, 144, 304, p=p), A("c1", m0, m1), A("fw"), False, True)])
-        gat(CFG["SC"][i], SND(t, i, 0, 304, p), A(bank, 0, 304, p=p))
-        if SP:
-            ops[-1]["pre"] = ("sent%d" % i, left * t)
-        o = A(*(("pm", 0, m1 - m0), ("gg", 256, 256 + m1 - m0))[i])
-        mm([(o, SND(t, i, 16, 144, p), A("i64", m0, m1, p=p), True, False),
-            (o, SND(t, i, 176, 304, p), A("ib", m0, m1, p=p), False, True)])
+        gat(CFG["SC"][i], SND(i, 0, 304, p), A(bank, 0, 304, p=p))
+        ops[-1]["pre"] = ("sent%d" % i, left * t)
+        o = A(*(("pm", 0, 64), ("gg", 256, 320))[i])
+        mm([(o, SND(i, 16, 144, p), A("i64", m0, m1, p=p), True, False),
+            (o, SND(i, 176, 304, p), A("ib", m0, m1, p=p), False, True)])
         ts(A("op_", m0, m1), o, -POF, AL.add)
+
+        def fn():
+            trs = []
+            for d, (m, _c), a, b in ((d1, mk[0], 0, 0), (d2, mk[1], 144, 128)):
+                ad = topo.addr(d)
+                trs.append(RemoteDMATransfer(dst_ids=[DstId(rid=ad[0], pnc=ad[1])], dma_engine_mask=m,
+                                             remote_sem=T.sem["arr%d" % (2 * t + i)], src=SND(i, a, a + 128)[0],
+                                             dst=LND(t, i, b, b + 128)[0]))
+            g.remote_dma_fused(trs, local_sem=T.sem["sent%d" % i])
+            return None
+        add("g", fn, SND(i, 0, 304)[1], [], dma="remote", ext=("arr%d" % (2 * t + i), 0))
 
     def m_name(i, t):
         bank, m0, m1 = HS[i]
         p = (m0, m1)
-        o = A(*(("gg", 384, 384 + m1 - m0), ("pm", 128, 128 + m1 - m0))[i])
-        c = 256 * i * SP
+        o = A(*(("gg", 384, 448), ("pm", 128, 192))[i])
+        c = 256 * i
         mm([(o, A("lnd%d" % t, c, c + 128, p=p), A("i64", m0, m1, p=p), True, False),
             (o, A("lnd%d" % t, c + 128, c + 256, p=p), A("ib", m0, m1, p=p), False, True)],
-           ext=("arr%d" % (2 * t + i * SP), arrive))
+           ext=("arr%d" % (2 * t + i), arrive))
         ts(A("om", m0, m1), o, -POF, AL.add)
 
     nb = [0]
@@ -630,112 +651,88 @@ def rank_program(g, core, T, topo):
     def distance(i, first):
         bank, lo, hi = HS[i]
         off, a2 = ("op_", "a2") if first else ("om", "a3")
-        y0 = 16 * lo + (0 if first else 16 * (hi - lo))
+        y0 = 16 * (lo if first else hi)
+        more = []
         for mode, m0, m1 in CH:
             if not lo <= m0 < hi:
                 continue
             a, b = 16 * m0, 16 * m1
             y = A("yy", y0 + a, y0 + b)
-            if mode == "A":
-                bk = ("dfa", "dfb")[nb[0] & 1]
-                nb[0] += 1
-                act(y, IND("tab", 0, 4096, off, m0, m1), AF.Copy)
-                mm([(A(bk, 0, b - a), A("zt"), A("emat", a, b), True, False),
-                    (A(bk, 0, b - a), A("imid"), y, False, True)])
-                act(A(a2, a, b), A(bk, 0, b - a), AF.Abs, scale=1.0 / MID)
+            if mode in "VRQS":
+                tt(y, IND("tab", 0, 4096, off, m0, m1), A("zrep", a, b), AL.subtract)
+                if mode in ("RQ" if first else "RS"):
+                    ts(A(a2, a, b), y, 0.0, AL.max, 2.0, AL.mult)
+                    more.append((m0, m1))
+                else:
+                    act(A(a2, a, b), y, AF.Abs)
                 continue
-            tt(y, IND("tab", 0, 4096, off, m0, m1), A("zrep", a, b), AL.subtract)
-            if mode == "V":
-                act(A(a2, a, b), y, AF.Abs)
-            else:
-                ts(A(a2, a, b), y, 0.0, AL.max, 2.0, AL.mult)
+            bk = ("dfa", "dfb")[nb[0] & 1]
+            nb[0] += 1
+            gat("a" if mode == "A" else "v", y, IND("tab", 0, 4096, off, m0, m1))
+            mm([(A(bk, 0, b - a), A(ZT[0]), A("emat", a, b), True, False),
+                (A(bk, 0, b - a), A("imid"), y, False, True)])
+            act(A(a2, a, b), A(bk, 0, b - a), AF.Abs, scale=1.0 / MID)
 
         def part(src, c0, m0, m1, sign, start, stop):
             mm([(A(bank, j, 128, 16, p=(m0, m1)), A(src, c0 + 16 * m0 + j, c0 + 16 * (m1 - 1) + j + 1, 16),
                  A(sign), start and j == 0, stop and j == 15) for j in range(16)])
         if first:
             part(a2, 0, lo, hi, "s2n", True, False)
-        for mode, m0, m1 in CH:
-            if mode == "R" and lo <= m0 < hi:
-                part("yy", y0, m0, m1, "s2p" if first else "s2n", False, False)
+        if more:
+            part("yy", y0, min(more)[0], max(more)[1], "s2p" if first else "s2n", False, False)
         if not first:
             part(a2, 0, lo, hi, "s2p", False, True)
-
-    def choose(i):
-        bank, m0, m1 = HS[i]
-        p = (m0, m1)
-        if tko:
-            ts(A("tk", p=p), A(bank, 0, 128, p=p), 0.0, AL.is_ge, 2.0, AL.mult)
-        else:
-            act(A("tk", p=p), A(bank, 0, 128, p=p), AF.Sign, bias=0.5)
+            act(A("tk", p=(lo, hi)), A(bank, 0, 128, p=(lo, hi)), AF.Sign, bias=0.5)
 
     def new_x(i):
         bank, m0, m1 = HS[i]
         p = (m0, m1)
-        o = A(*(("pm", 192, 192 + m1 - m0), ("pm", 0, m1 - m0))[i])
+        o = A("pm", m0, m1)
         mm([(o, A("one", p=p), A("d16", m0, m1, p=p), True, False)])
         mm([(o, A("tk", p=p), A("ixw", m0, m1, p=p), False, True)])
-        ts(A("oe", m0, m1), o, col("pf", 12), AL.add)
+        ts(A("oe", m0, m1), o, col("pf", 1), AL.add)
         for mode, a, b in CH:
             if m0 <= a < m1:
                 src = IND("yy", 32 * m0, 32 * m1, "oe", a, b)
-                if mode == "A":
-                    gat(CFG["XA"], A("xs", 16 * a, 16 * b), src)
-                else:
+                if mode in "VRQS":
                     tt(A("xs", 16 * a, 16 * b), src, A("zrep", 16 * a, 16 * b), AL.add)
-
-    units = [(i, h[1:]) for i, h in enumerate(HS)] if SP else [(0, (0, 128))]
+                else:
+                    act(A("xs", 16 * a, 16 * b), src, AF.Copy)
 
     def m_diff(t):
-        for i, p in units:
+        for i, h in enumerate(HS):
+            p = h[1:]
             mm([(A("wk", 0, 256, p=p), A("ib", *p, p=p), LND(t, i, 0, 256, p), True, False),
-                (A("wk", 0, 128, p=p), A("ibn", *p, p=p), SND(t, i, 16, 144, p), False, False),
-                (A("wk", 128, 256, p=p), A("ibn", *p, p=p), SND(t, i, 176, 304, p), False, True)])
+                (A("wk", 0, 128, p=p), A("ibn", *p, p=p), SND(i, 16, 144, p), False, False),
+                (A("wk", 128, 256, p=p), A("ibn", *p, p=p), SND(i, 176, 304, p), False, True)])
 
-    def mixed(o, t, i, d, full, half, p, start):
-        s0 = (16, 176)[d]
-        if tko:
-            return [(o, LND(t, i, 128 * d, 128 * d + 128, p), A(full, *p, p=p), start, False)]
-        return [(o, LND(t, i, 128 * d, 128 * d + 128, p), A(half, *p, p=p), start, False),
-                (o, SND(t, i, s0, s0 + 128, p), A(half, *p, p=p), False, False)]
-
-    def new_digits(t):
+    def chosen(t, parts):
         tt(A("uu", 0, 128), A("wk", 0, 128), A("tk"), AL.mult)
         tt(A("uu", 128, 256), A("wk", 128, 256), A("tk"), AL.mult)
-        parts = ((0, 0), (128, 1), (256, 1))
-        for i, p in units:
-            mm([e for c, d in parts for e in mixed(A("dg", c + p[0], c + p[1]), t, i, d, "ib", "ihf", p, c + i == 0)])
-        mm([(A("dg", 256, 384), A("kt"), A("ib"), False, False)])
-        mm([(A("dg", c, c + 128), A("uu", 128 * d, 128 * d + 128), A("ihn"), False, c == 256) for c, d in parts])
-        gat(CFG["HL"], A("hl"), A("dg", 0, 256))
-        act(A("cf", 0, 128), A("dg", 256, 384), AF.Identity, bias=col("pf", 9), scale=S19)
-        windows(t + 1)
-
-    def last_names(i, t):
-        bank, m0, m1 = HS[i]
-        p = (m0, m1)
-        tt(A("uu", 0, 128, p=p), A("wk", 0, 128, p=p), A("tk", p=p), AL.mult)
-        tt(A("uu", 128, 256, p=p), A("wk", 128, 256, p=p), A("tk", p=p), AL.mult)
-        o = A(*(("pm", 192, 192 + m1 - m0), ("pm", 0, m1 - m0))[i])
-        hi = mixed(o, t, i, 0, "i64", "i32", p, True), [(o, A("uu", 0, 128, p=p), A("i32h", *p, p=p), False, False)]
-        lo = mixed(o, t, i, 1, "ib", "ihf", p, False), [(o, A("uu", 128, 256, p=p), A("ihn", *p, p=p), False, True)]
-        mm(hi[0] + lo[0])
-        mm(hi[1] + lo[1])
-        ts(A("nm", m0, m1), o, -POF, AL.add)
+        for i, h in enumerate(HS):
+            p = h[1:]
+            lst = []
+            for c, d, half, _neg in parts:
+                o = A("dg", c + p[0], c + p[1])
+                lst += [(o, LND(t, i, 128 * d, 128 * d + 128, p), A(half, *p, p=p), i == 0 and not lst, False),
+                        (o, SND(i, (16, 176)[d], (144, 304)[d], p), A(half, *p, p=p), False, False)]
+            mm(lst)
+        if t < RO - 1:
+            mm([(A("dg", 256, 384), A("kt"), A("ib"), False, False)])
+        mm([(A("dg", e[0], e[0] + 128), A("uu", 128 * e[1], 128 * e[1] + 128), A(e[3]), False, e == parts[-1])
+            for e in parts])
 
     def windows(t):
         for p0, c0, c in ((0, 16, 0), (1, 15, 0), (0, 16 + SEC, 0), (0, S2, 128), (1, S2 - 1, 128)):
-            x = A("win", c0, c0 + 2048, p=(p0, 128, 16))
-            dma("s", x, A("hl", c, c + 128), "w%d" % t)
+            dma("s", A("win", c0, c0 + 2048, p=(p0, 128, 16)), A("hl", c, c + 128), "w%d" % t)
 
-    if SP:
-        for i in range(2):
-            ms(SND(0, i, 0, 304, HS[1 - i][1:]), 0.0)
+    for i in range(2):
+        ms(SND(i, 0, 304, HS[1 - i][1:]), 0.0)
     windows(0)
     late_constants()
     threshold(0)
-    for e in CFG["E0"]:
-        egather(*e)
+    for e, m0, m1 in CFG["E0"]:
+        gat(e, A("xs", 16 * m0, 16 * m1), IND("tab", 0, 4096, "oe", m0, m1))
     mm([(A("dg", 128, 256), A("zs"), A("ib"), True, True)])
     act(A("zt"), A("dg", 128, 256), AF.Copy)
     diffs(SM, 128)
@@ -746,50 +743,49 @@ def rank_program(g, core, T, topo):
 
     for t in range(RO):
         last = t == RO - 1
+        CH[:] = CFG["CHL"] if last and CFG["CHL"] else CFG["CH"]
         z_rep()
         periods()
-        for i in range(len(HS)):
+        for i in range(2):
             select(i, t)
-            if SP or i:
-                send(t, i * SP)
-        for i in range(len(HS)):
+        for i in range(2):
             distance(i, True)
-        for i in range(len(HS)):
+        for i in range(2):
             m_name(i, t)
         m_diff(t)
         if not last:
             threshold(t + 1)
-        for i in range(len(HS)):
+        for i in range(2):
             distance(i, False)
-            choose(i)
+        for i in range(2):
+            new_x(i)
         if not last:
-            new_x(0)
             diffs(SM, 128)
-            new_x(1)
             sums(SM, 128, False)
-            new_digits(t)
+            chosen(t, ((0, 0, "ihf", "ihn"), (128, 1, "ihf", "ihn"), (256, 1, "ihf", "ihn")))
+            gat(CFG["HL"], A("hl"), A("dg", 0, 256))
+            lin(A("cf", 0, 128), A("dg", 256, 384), S19, col("pf", 9))
+            windows(t + 1)
             count()
             diffs(0, SM)
             sums(0, SM, True)
-            block_max()
-            blocks_a()
-        else:
-            for i in range(len(HS)):
-                last_names(i, t)
-            cp(A("tin"), IND("nm", 0, 128, "o3", 0, 16))
-            trn(A("tout"), A("tin"))
-            cp(A("oe"), IND("tout", 0, 256, "o4", 0, 8))
-            act(A("nl"), IND("tout", 0, 256, "o4", 0, 8), AF.Copy)
-            dma(CFG["LQ"][0], (T.ly[:], []), A("nl"), "out")
-            for e, m0, m1 in CFG["EL"]:
-                egather(e, m0, m1)
-                dma("s", (T.xy[:, 16 * m0:16 * m1], []), A("xs", 16 * m0, 16 * m1), "out")
-            for m0, m1 in CFG["ES"]:
-                scan(A("ysc", 16 * m0, 16 * m1), A("m5", 0, 16 * (m1 - m0)), A("xs", 16 * m0, 16 * m1), 0.0,
-                     AL.mult, AL.max)
-            tt(A("zd"), YY, A("zs"), AL.subtract)
-            act(A("zt"), A("zd"), AF.Abs)
-            dma(CFG["LQ"][1], (T.zy[:], []), A("zt"), "out")
+            blocks(t)
+            continue
+        chosen(t, ((0, 0, "i32", "i32h"), (0, 1, "ihf", "ihn")))
+        lin(A("nm"), A("dg", 0, 128), 1.0, -POF)
+        cp(A("tin"), IND("nm", 0, 128, "o3", 0, 16))
+        trn(A("tout"), A("tin"))
+        act(A("nl"), IND("tout", 0, 256, "o4", 0, 8), AF.Copy)
+        dma(CFG["LQ"][0], (T.ly[:], []), A("nl"), "out")
+        for j0, j1 in CFG["TL"]:
+            for j in range(j0, j1):
+                gat(CFG["TE"][j], A("ab", 128 * j, 128 * j + 128), A("xs", j, 2048, 16))
+            a, b = 128 * j0, 128 * j1
+            dma("s", (T.xy[:, a:b], []), A("ab", a, b), "out")
+            scan(A("ysc", a, b), A("mb", 0, b - a), A("ab", a, b), 0.0, AL.min, AL.max)
+        tt(A("zd"), YY, A("zs"), AL.subtract)
+        act(A("zt"), A("zd"), AF.Abs)
+        dma(CFG["LQ"][1], (T.zy[:], []), A("zt"), "out")
 
     if not ORDER:
         hist = {}
@@ -894,5 +890,5 @@ def rank_program(g, core, T, topo):
                             "clock": clock, "rows": o.get("rows")})
     for s, v in cnt.items():
         g.wait_ge(T.sem[s], v)
-    for i in range(1 + SP):
+    for i in range(2):
         g.wait_ge(T.sem["sent%d" % i], RO * left)

from concourse.bass import DstId, RemoteDMATransfer
from concourse.mybir import AluOpType, AxisListType, ActivationFunctionType

F32, BF, I32, U16 = "float32", "bfloat16", "int32", "uint16"
RO = 4
BIG = 2.0 ** 21
SEC = 2048
S2 = 16 + 2 * SEC + 1
WIN = 6176
U = 1.0 / SEC
S19 = U / 256
CN = 2.625
NONE = (CN - SEC) * U
POF = 65 * 160.0
MID = 208.0
QB = 192 - 15.5 / 32
HS = (("d1", 64, 128), ("d0", 0, 64))
CFG = {
    "DG": (("v", 96, 128), ("a", 64, 96), ("v", 28, 64), ("a", 0, 28)),
    "E0": (("v", 100, 128), ("a", 76, 100), ("v", 52, 76), ("a", 0, 14), ("v", 32, 52), ("v", 14, 32)),
    "CH": (("A", 64, 84), ("R", 96, 128), ("V", 84, 96), ("A", 0, 20), ("S", 32, 64), ("V", 20, 32)),
    "CHL": None,
    "DC": (("dfa", 97, 128), ("dfb", 65, 97), ("d0", 33, 65), ("dfa", 21, 33), ("dfb", 0, 21)),
    "SM": 65,
    "TL": ((0, 4), (4, 8), (8, 12), (12, 16)), "TE": "vava" * 4, "LQ": "aa",
    "SC": "aa", "HL": "a", "BB": ("d0", "d1", "dg"),
    "RATES": ((0.1, 0.05, 1.1, 1.56, 3.8, 0.42e-3, 0.9, 0.4e-3), (0.08, 0.05, 1.25, 1.1, 2.0, 0.42e-3, 0.9, 0.25e-3),
              (0.13, 0.05, 1.25, 2.0, 5.5, 0.42e-3, 0.9, 0.4e-3), (0.26, 0.05, 1.15, 1.4, 3.0, 0.42e-3, 1.8, 0.3e-3)),
    "LOOK": 0.5, "ITER": 2000, "TEMP": 0.001, "LNS": 12000, "WIN": 60, "TEMP3": 0.001, "SEED": 12345, "WL": 1.3,
}
SPAN = []
DEBUG = []
ORDER = []

SB = {
    "tab": (4096, BF), "win": (WIN, BF), "xs": (2048, BF), "ab": (2048, BF), "yy": (4096, BF),
    "a2": (2048, BF), "a3": (2048, BF), "zrep": (2048, BF), "emat": (2048, BF), "g2": (2048, BF), "ysc": (2048, BF),
    "l0s": (128, I32), "zs": (128, BF), "zd": (128, BF), "zt": (128, BF), "zt1": (128, BF),
    "ths": (4, I32), "thf": (128, F32), "thh": (128, BF), "thl": (128, BF),
    "pi": (10, I32), "pf": (14, F32), "kt": (128, BF), "vv": (128, I32), "xi": (160, F32), "x16": (128, F32),
    "selr": (20, F32), "s2p": (8, BF), "s2n": (8, BF), "one": (128, BF), "hl": (256, BF),
    "tk": (128, BF), "uu": (256, BF), "zp": (144, BF), "ib": (128, BF), "ibn": (128, BF),
    "i64": (128, BF), "i32": (128, BF), "ihf": (128, BF), "ihn": (128, BF), "i32h": (128, BF),
    "ixw": (128, BF), "d16": (128, BF), "fw": (304, BF), "i64n": (128, BF), "qoff": (128, BF),
    "bp": (128, F32), "bn": (128, F32), "e8": (128, F32), "sel": (20, BF), "sel2": (12, BF), "cm": (34, BF),
    "kq": (128, F32), "two": (128, F32), "cf": (145, F32), "cb": (145, F32),
    "oi": (32, I32), "o1": (16, U16), "o2": (8, U16), "o3": (16, U16), "o4": (8, U16), "ci": (8, I32),
    "tin": (256, F32), "tout": (256, F32), "nm": (128, F32), "nl": (128, F32),
    "oe": (128, U16), "ob": (128, U16), "op_": (128, U16), "om": (128, U16), "osc": (8, U16),
    "tq": (64, F32), "h64": (128, F32), "sc1": (292, F32), "cy": (2, F32), "ne": (128, F32), "al": (128, F32),
    "zz": (128, F32), "qq": (128, F32), "of": (128, F32), "c1": (128, BF), "acb": (128, BF), "qb": (128, BF),
    "ui": (16, I32), "uj": (8, I32), "sh": (128, I32), "imid": (128, BF), "i32b": (128, BF),
    "bb": (128, BF), "bbh": (128, BF), "mb": (512, BF), "snd0": (304, BF), "snd1": (304, BF),
}
for _t in range(RO):
    SB["lnd%d" % _t] = (512, BF)
PS = ["dfa", "dfb", "gg", "wk", "dg", "pm", "d0", "d1"]
SCRATCH = {k: ("sbuf", [128, v[0]], v[1]) for k, v in SB.items()}
for _p in PS:
    SCRATCH[_p] = ("psum", [128, 512], F32)
SEMAPHORES = ["sv", "sa", "sp", "sg", "l_l", "l_t", "l_z", "l_h", "sent0", "sent1", "out"]
SEMAPHORES += ["w%d" % t for t in range(RO)] + ["arr%d" % t for t in range(2 * RO)]
ESEM = {"v": "sv", "a": "sa", "p": "sp", "g": "sg"}


def masks(topo, src, dsts):
    lists = [topo.engines(src, d) for d in dsts]
    a, b = lists
    if a == b:
        h = len(a) // 2
        a, b = a[:h], a[h:]
    elif len(a) > len(b):
        a = [e for e in a if e not in b]
    else:
        b = [e for e in b if e not in a]
    return [(sum(1 << e for e in x), len(x)) for x in (a, b)]


def arrange(ops):
    n = len(ops)
    qs = [o["q"] for o in ops]
    dep = [list(o["dep"].items()) for o in ops]
    suc = [o["suc"] for o in ops]
    names = sorted(set(qs))
    anc = [0] * n
    hard, soft = [], []
    for i in range(n):
        far = 0
        for j, k in dep[i]:
            far |= anc[j]
        hard.append([j for j, k in dep[i] if k and not far >> j & 1])
        soft.append([j for j, k in dep[i] if not k and not far >> j & 1])
        for j in hard[i]:
            far |= 1 << j
        anc[i] = far
    tabs = []
    for hop, fix, kf, gat, sca, pec, rem, byte in CFG["RATES"]:
        d = [o["c"][0] + o["c"][1] * fix + (o["c"][2] + o["c"][3] * gat + o["c"][4] * sca) * 0.83e-3 * kf
             + o["c"][5] * pec * kf + o["c"][6] * byte for o in ops]
        lat = [rem if o["dma"] == "remote" else o["lat"] for o in ops]
        tabs.append((d, lat, hop))
    state = [CFG["SEED"]]

    def draw(k):
        state[0] = (state[0] * 1103515245 + 12345) % 2147483648
        return (state[0] >> 8) % k

    def span(order, tab, old=None, a=0):
        d, lat, hop = tab
        if old is None:
            end, ok, why = [0.0] * n, [0.0] * n, [-1] * n
        else:
            end, ok, why = list(old[2]), list(old[3]), list(old[4])
        prev = dict.fromkeys(names, -1)
        k, miss = a - 1, len(names)
        while k >= 0 and miss:
            if prev[qs[order[k]]] < 0:
                prev[qs[order[k]]] = order[k]
                miss -= 1
            k -= 1
        for i in order[a:]:
            q = qs[i]
            w = prev[q]
            st = end[w] if w >= 0 else 0.0
            for j in hard[i]:
                if ok[j] > st:
                    st, w = ok[j], j
            for j in soft[i]:
                if end[j] > st:
                    st, w = end[j], j
            st += d[i]
            end[i] = st
            ok[i] = st + lat[i] + hop
            why[i] = w
            prev[q] = i
        top = max(ok)
        i = ok.index(top)
        held = []
        while i >= 0:
            if why[i] >= 0 and why[i] not in ops[i]["dep"]:
                held.append(i)
            i = why[i]
        return top, held, end, ok, why

    def deal(seg, tab, worth, free, end, ok):
        d, lat, hop = tab
        inside = set(seg)
        left = {i: sum(1 for j, _k in dep[i] if j in inside) for i in seg}
        ready = [i for i in seg if not left[i]]
        est = {i: max([0.0] + [ok[j] if k else end[j] for j, k in dep[i]]) for i in ready}
        out = []
        while ready:
            first = min(ready, key=lambda x: max(free[qs[x]], est[x]) + d[x])
            q = qs[first]
            lim = max(free[q], est[first]) + d[first]
            i = max((x for x in ready if qs[x] == q and est[x] < lim), key=lambda x: worth[x] - max(free[q], est[x]))
            ready.remove(i)
            end[i] = free[q] = max(free[q], est[i]) + d[i]
            ok[i] = end[i] + lat[i] + hop
            out.append(i)
            for j, _k in suc[i]:
                if j in inside:
                    left[j] -= 1
                    if not left[j]:
                        ready.append(j)
                        est[j] = max(ok[x] if k else end[x] for x, k in dep[j])
        return out

    d, lat, hop = tabs[0]
    pri = [0.0] * n
    for i in range(n - 1, -1, -1):
        pri[i] = d[i] + max([lat[i]] + [(lat[i] + hop) * k + pri[j] for j, k in suc[i]])
    order = deal(list(range(n)), tabs[0], pri, dict.fromkeys(names, 0.0), [0.0] * n, [0.0] * n)
    res = [span(order, tb) for tb in tabs]
    base = [r[0] for r in res]
    cur = best = float(len(tabs))
    keep, fresh = order, True
    swaps, total = CFG["ITER"], CFG["ITER"] + CFG["LNS"]
    for it in range(total):
        if it == swaps:
            order, cur, fresh = keep, best, True
            res = [span(order, tb) for tb in tabs]
        if fresh:
            order = sorted(order, key=lambda x: res[0][2][x] - tabs[0][0][x])
            tails = []
            for d, lat, hop in tabs * (it >= swaps):
                tail, nxt = [0.0] * n, dict.fromkeys(names, 0.0)
                for i in reversed(order):
                    v = max(lat[i], nxt[qs[i]])
                    for j, k in suc[i]:
                        v = max(v, (lat[i] + hop) * k + tail[j])
                    tail[i] = nxt[qs[i]] = v + d[i]
                tails.append(tail)
            fresh = False
        m = draw(len(tabs))
        if it < swaps:
            held = res[m][1]
            if not held:
                continue
            i = held[draw(len(held))]
            b = order.index(i)
            a, step = b, 1 + draw(8) // 3
            while step and a > 0:
                a -= 1
                if qs[order[a]] == qs[i]:
                    step -= 1
            seg = order[a:b + 1]
            if draw(2):
                move = {i}
                for x in reversed(seg):
                    if x in move:
                        move.update(j for j, _k in dep[x])
                if seg[0] in move:
                    continue
                new_seg = [x for x in seg if x in move] + [x for x in seg if x not in move]
            else:
                move = {seg[0]}
                for x in seg:
                    if x in move:
                        move.update(j for j, _k in suc[x])
                if i in move:
                    continue
                new_seg = [x for x in seg if x not in move] + [x for x in seg if x in move]
            slack = CFG["TEMP"] * (1 - it / swaps)
        else:
            d, lat, hop = tabs[m]
            size = 12 + draw(CFG["WIN"])
            a = draw(n - 12)
            seg = order[a:a + size]
            inside = set(seg)
            after = {}
            for x in order[a + size:a + size + 80]:
                after.setdefault(qs[x], tails[m][x])
            noise = 1.2 * (draw(1000) / 1000) ** 2
            worth = {}
            for i in reversed(seg):
                v = max(lat[i], after.get(qs[i], 0.0))
                for j, k in suc[i]:
                    v = max(v, (lat[i] + hop) * k + (worth[j] if j in inside else tails[m][j]))
                worth[i] = v + d[i]
            for i in seg:
                worth[i] += noise * draw(1000) / 1000
            free = dict.fromkeys(names, 0.0)
            for x in order[max(0, a - 120):a]:
                free[qs[x]] = res[m][2][x]
            new_seg = deal(seg, tabs[m], worth, free, list(res[m][2]), list(res[m][3]))
            slack = CFG["TEMP3"] * (total - it) / (total - swaps)
        cand = order[:a] + new_seg + order[a + len(seg):]
        new = [span(cand, tb, r, a) for tb, r in zip(tabs, res)]
        val = sum(r[0] / bs for r, bs in zip(new, base))
        if val <= cur + slack * draw(1000) / 1000:
            cur, order, res, fresh = val, cand, new, True
            if val < best:
                best, keep = val, cand
    SPAN[:] = [base, [span(keep, tb)[0] for tb in tabs]]
    DEBUG[:] = [ops, span(keep, tabs[0]), tabs[0]]
    return keep


def meet(x, y):
    return x[1] < y[2] and y[1] < x[2] and x[4] < y[5] and y[4] < x[5]


def covers(x, y):
    return x[1] <= y[1] and y[2] <= x[2] and x[4] <= y[4] and y[5] <= x[5]


def rank_program(g, core, T, topo):
    rank = T.rank_of(core)
    if rank is None:
        return
    n = len(T.cores)
    Q = {"v": g.vector, "a": g.scalar, "p": g.tensor, "g": g, "s": g.sync}
    AL, AF = AluOpType, ActivationFunctionType
    CH, DC, SM = list(CFG["CH"]), CFG["DC"], CFG["SM"]
    ZT = ["zt", "zt1"]
    ops = []

    def A(name, a=0, b=None, s=1, p=None):
        w = 512 if name in PS else SB[name][0]
        if b is None:
            b = w
        rows = slice(None) if p is None else slice(*p)
        reg = [(name, a, b, len(range(a, b, abs(s)))) + ((0, 128) if p is None else p[:2])]
        if s < 0:
            return T[name][rows, slice(b - 1, a - 1 if a > 0 else None, s)], reg
        if s == 1:
            return T[name][rows, a:b], reg
        return T[name][rows, a:b:s], reg

    def IND(name, a, b, off, c, d):
        return T[name][:, a:b].indirect(T[off][:, c:d]), [(name, a, b, 0, 0, 128), (off, c, d, -16 * (d - c), 0, 128)]

    def sc(x):
        return (x, []) if not isinstance(x, tuple) else x

    def add(q, fn, reads, writes, dma=None, ext=None, cost=None, after=None):
        lat = 0.0
        if dma == "remote":
            d = (1.2, 0, 0, 0, 0, 0, 0)
        elif dma:
            wide = (writes if dma[0] == "l" else reads)[0]
            size = wide[3] * (2 if SB[wide[0]][1] == BF else 4)
            d, lat = ((0.24, 0, 0, 0, 0, 0, size), CFG["WL"]) if q == "s" else ((0.06, 0, 0, 0, 0, 0, 0), 1.7)
        elif q == "p":
            d, lat = (0, 0, 0, 0, 0, cost, 0), 0.06
        else:
            ind = [-x[3] for x in reads if x[3] < 0]
            if ind:
                d = (0.01, 1, 0, 0, ind[0], 0, 0) if writes[0][3] == 0 else (0.01, 1, 0, ind[0], 0, 0, 0)
            else:
                nel = writes[0][3]
                if nel == 1 and reads:
                    nel = reads[0][3]
                big = [x for x in reads + writes if x[3] >= nel]
                if q == "g":
                    d = (0.15, 0, 2 * nel, 0, 0, 0, 0)
                else:
                    two = all(SB.get(x[0], (0, 0))[1] in (BF, U16) for x in big)
                    rate = 0.5 if two and q == "v" else 1.0
                    if cost == "tt" and not any(x[0] in PS for x in reads):
                        rate *= 2
                    d = (0.01 * (q == "a"), 1, max(64, nel * rate), 0, 0, 0, 0)
        ops.append({"q": q, "fn": fn, "r": reads, "w": writes, "dma": dma, "ext": ext, "c": d, "lat": lat,
                    "after": after})
        return len(ops) - 1

    def tt(o, a, b, op):
        add("v", lambda: g.vector.tensor_tensor(o[0], a[0], b[0], op), a[1] + b[1], o[1], cost="tt")

    def ts(o, a, s1, op0, s2=None, op1=None):
        s1, s2 = sc(s1), sc(s2)
        if op1 is None:
            add("v", lambda: g.vector.tensor_scalar(o[0], a[0], s1[0], None, op0), a[1] + s1[1], o[1])
        else:
            add("v", lambda: g.vector.tensor_scalar(o[0], a[0], s1[0], s2[0], op0, op1), a[1] + s1[1] + s2[1], o[1])

    def cp(o, a):
        add("v", lambda: g.vector.tensor_copy(o[0], a[0]), a[1] + o[1][1:], o[1][:1])

    def ms(o, v):
        add("v", lambda: g.vector.memset(o[0], v), [], o[1])

    def scan(o, a, b, init, op0, op1):
        init = sc(init)
        add("v", lambda: g.vector.tensor_tensor_scan(o[0], a[0], b[0], init[0], op0, op1), a[1] + b[1] + init[1], o[1])

    def red(o, a, op):
        add("v", lambda: g.vector.tensor_reduce(o[0], a[0], AxisListType.X, op, negate=True), a[1], o[1])

    def trn(o, a):
        add("v", lambda: g.vector.transpose(o[0], a[0]), a[1], o[1])

    def act(o, a, f, bias=0.0, scale=1.0):
        bias, scale = sc(bias), sc(scale)
        add("a", lambda: g.scalar.activation(o[0], a[0], f, bias=bias[0], scale=scale[0]),
            a[1] + bias[1] + scale[1], o[1])

    def mm(lst, ext=None):
        def fn():
            r = None
            for o, l, rr, st, sp in lst:
                r = g.tensor.matmul(o[0], l[0], rr[0], st, sp)
            return r
        add("p", fn, [x for e in lst for x in e[1][1] + e[2][1]], [x for e in lst for x in e[0][1]], ext=ext,
            cost=sum(max(min(64, e[1][1][0][3]), e[2][1][0][3]) * (4 if SB[e[1][1][0][0]][1] == F32 else 1) for e in lst))
        ops[-1]["rows"] = lst[0][1][1][0][4:6]

    def iota(o, pat, base, cm, fl=True):
        if fl:
            add("g", lambda: g.iota(o[0], pat, base, cm, allow_small_or_imprecise_dtypes=True), [], o[1])
        else:
            add("g", lambda: g.iota(o[0], pat, base, cm), [], o[1])

    def dma(q, o, a, sem, after=None):
        return add(q, lambda: Q[q].dma_start(o[0], a[0]), a[1], o[1], dma=sem, after=after)

    def gat(e, o, src):
        if e == "v":
            cp(o, src)
        else:
            act(o, src, AF.Copy)

    def col(name, c, p=None):
        return A(name, c, c + 1, p=p)

    def lin(o, a, scale, bias=0.0):
        act(o, a, AF.Identity, bias=bias, scale=scale)

    def eye(name, v, src="ib"):
        act(A(name, 0, 128), A(src, 0, 128), AF.Copy, scale=v)

    first = dma("s", A("l0s"), (T.l0[:], []), "l_l")
    first = dma("s", A("tab"), (T.x0[:], []), "l_t", after=first)
    dma("s", A("zs"), (T.z0[:], []), "l_z", after=first)
    dma("a", A("ths", p=(0, 8)), (T.th[:], []), "l_h")

    iota(col("pi", 0), [[0, 1]], 0, 1, False)
    iota(A("oi", 0, 16), [[1, 8], [0, 2]], 0, 8, False)
    iota(A("xi"), [[1, 160]], 0, 0)
    ms(A("win", 16 + SEC, S2 - 1), MID)
    ts(col("pi", 1), col("pi", 0), 15, AL.bitwise_and)
    ts(A("oi", 16, 32), A("oi", 0, 16), 127, AL.bitwise_and)
    ts(col("pi", 2), col("pi", 0), 31, AL.bitwise_and)
    ts(col("pi", 3), col("pi", 0), 63, AL.bitwise_and)
    cp(A("o1"), A("oi", 16, 32))
    cp(A("pf", 0, 4), A("pi", 0, 4))
    ts(A("tq", 0, 8), A("xi", 0, 8), 32.0, AL.mult, col("pf", 2), AL.add)
    cp(A("o2"), A("tq", 0, 8))
    iota(A("x16"), [[16, 8], [0, 16]], 0, 0)
    iota(A("selr", 0, 1), [[0, 1]], 112, 0)
    iota(A("selr", 1, 9), [[16, 8]], 0, 0)
    iota(A("selr", 9, 11), [[16, 2]], 97, 0)
    iota(A("selr", 11, 19), [[16, 8]], 1, 0)
    add("g", lambda: g.affine_select(T.emat[:], T.win[:, 16 + SEC:16 + 2 * SEC], [[-1, 8], [0, 16], [-8, 16]],
                                     AL.is_equal, 0.0, 0, 1), A("win", 16 + SEC, 16 + 2 * SEC)[1], A("emat")[1])
    iota(A("win", S2 - 1, WIN), [[0, WIN - S2 + 1]], 256, 0)
    iota(A("mb"), [[0, 32], [1024, 16]], -512, 0)
    on_g = [i for i, o in enumerate(ops) if o["q"] == "g"]
    for i, k in zip(on_g, on_g[1:]):
        ops[k]["after"] = i
    tt(col("pf", 4), col("pf", 0), col("pf", 1), AL.subtract)
    lin(col("pf", 5), col("pf", 4), 1.0, 15.0)
    lin(col("pf", 6), col("pf", 0), 16.0)
    lin(col("pf", 9), col("pf", 1), 128 * U)
    lin(A("kq"), A("xi", 0, 128), U, col("pf", 9))
    ms(A("win", 0, 16 + SEC), 192.0)

    cp(A("tin"), IND("l0s", 0, 128, "o1", 0, 16))
    trn(A("tout"), A("tin"))
    cp(A("oe"), IND("tout", 0, 256, "o2", 0, 8))
    act(A("nm"), IND("tout", 0, 256, "o2", 0, 8), AF.Copy)
    lin(A("hl", 0, 128), A("nm"), 1.0 / 64, 160 - 31.5 / 64)
    lin(A("h64"), A("hl", 0, 128), -64.0, POF)
    tt(A("hl", 128, 256), A("nm"), A("h64"), AL.add)
    lin(A("h64"), A("hl", 128, 256), S19)
    tt(A("cf", 0, 128), A("h64"), A("kq"), AL.add)
    ts(A("ib"), A("xi", 0, 128), col("pf", 0), AL.is_equal)
    eye("ibn", -1.0)
    ms(A("one"), 1.0)
    eye("i32b", 32 * BIG, "one")
    ts(A("e8", p=(0, 8)), A("x16", p=(0, 8)), col("pf", 6, (0, 8)), AL.is_equal, -1.0 / 32, AL.mult)
    ms(A("thf", p=(0, 8)), 0.0)
    ts(A("thf", 0, 128, 32, p=(0, 8)), A("ths", p=(0, 8)), 0.5, AL.add)
    mm([(A("dg", 0, 128), A("thf", p=(0, 8)), A("e8", p=(0, 8)), True, True)])
    act(A("thh"), A("dg", 0, 128), AF.Copy)
    tt(A("thl"), A("dg", 0, 128), A("thh"), AL.subtract)
    ts(A("zp"), A("xi", 0, 144), col("pf", 5), AL.is_equal, BIG, AL.mult)
    ms(col("ab", 0), 512.0)

    def late_constants():
        ts(A("s2p"), A("selr", 1, 9), col("pf", 4), AL.is_equal)
        lin(A("s2n"), A("s2p"), -1.0)
        lin(A("two", 1, 128), A("xi", 1, 128), 0.0, 2 * U)
        lin(A("two", 0, 1), A("xi", 0, 1), 0.0)
        lin(col("pf", 8), col("pf", 0), 256.0)
        lin(A("kt"), A("xi", 0, 128), 0.0, col("pf", 8))
        eye("i64", 64.0)
        eye("ihf", 0.5)
        eye("ihn", -0.5)
        eye("imid", -MID)
        eye("ixw", -512.0)
        lin(col("pf", 13), col("pf", 3), 16.0, 512.0)
        act(A("d16"), A("ib"), AF.Identity, scale=col("pf", 13))
        ms(A("fw", 0, 144), 0.0)
        act(A("fw", 144, 176), A("ib", 96, 128), AF.Copy, scale=-1.0 / S19)
        act(A("fw", 176, 304), A("ib"), AF.Copy, scale=-1.0 / S19)
        ts(A("bp"), A("x16"), col("pf", 4), AL.is_equal)
        eye("bn", -1.0, "bp")
        eye("bb", 1.0, "bp")
        eye("bbh", BIG / 2, "one")
        eye("i64n", -1.0 / 64)
        lin(A("qoff"), A("one"), -192.0)
        lin(col("pf", 11), col("pf", 0), 1.0, -1.0)
        ts(A("sel", 0, 19), A("selr", 0, 19), col("pf", 0), AL.is_equal)
        ts(A("sel2", 0, 10), A("selr", 9, 19), col("pf", 11), AL.is_equal)
        tt(A("sel", 9, 19), A("sel", 9, 19), A("sel2", 0, 10), AL.add)
        ts(A("cf", 128, 145), A("xi", 0, 17), col("pf", 1), AL.is_le, BIG, AL.mult)
        lin(A("cb", 0, 17), A("cf", 128, 145), -1.0, BIG - 1.0)
        lin(A("cb", 17, 145), A("kq"), -1.0, CN * U)
        lin(A("wk", 256, 384), A("kq"), 2.0)
        lin(A("wk", 384, 512), A("kq"), 2.0, (2 * SEC + 0.25 - CN) * U)
        lin(col("pf", 10), col("pf", 1), -256 * U)
        ts(A("tq", 16, 33), A("xi", 0, 17), col("pf", 1), AL.is_ge, -BIG, AL.mult)
        lin(A("cm", 0, 17), A("tq", 16, 33), 1.0, col("pf", 10))
        lin(A("cm", 17, 33), A("cf", 128, 144), 1.0, 1.0)
        ms(A("gg", 0, 17), -BIG)
        ms(A("gg", 145, 162), -BIG)
        ms(A("pm", 289, 290), -NONE)
        ms(A("sc1", 290, 291), NONE)

    def last_constants():
        ts(A("tq", 40, 48), A("xi", 0, 8), 16.0, AL.mult, col("pf", 1), AL.add)
        ts(A("ci"), A("tq", 40, 48), 32.0, AL.mult)
        cp(A("o3", 0, 16, 2), A("tq", 40, 48))
        cp(A("o3", 1, 16, 2), A("tq", 40, 48))
        ts(col("pi", 4), col("pi", 0), 7, AL.bitwise_and)
        ts(col("pi", 5), col("pi", 0), 3, AL.logical_shift_right, 1, AL.bitwise_and)
        ts(col("pi", 6), col("pi", 0), 16, AL.bitwise_and)
        ts(col("pi", 7), col("pi", 4), 32.0, AL.mult)
        tt(col("pi", 8), col("pi", 5), col("pi", 6), AL.add)
        tt(col("pf", 7), col("pi", 7), col("pi", 8), AL.add)
        ts(A("o4"), A("xi", 0, 8), 2.0, AL.mult, col("pf", 7), AL.add)
        eye("i32", 32.0)
        eye("i32h", -32.0)

    def zl(j):
        return A("zp", 15 - j, 143 - j)

    def sums(m0, m1, stop):
        mm([(A("gg", 17 + m0, 17 + m1), zl(j), A("ab", 16 * m0 + j, 16 * (m1 - 1) + j + 1, 16), False, stop and j == 15)
            for j in range(16)])

    def threshold(t):
        p = (32 * t, 32 * t + 1)
        mm([(A("gg", 17, 145), A("thh", p=p), A("i32b", p=p), True, False),
            (A("gg", 17, 145), A("thl", p=p), A("i32b", p=p), False, False)])
        if t:
            mm([(A("gg", 17, 145), A("qoff"), A("i32b"), False, False)])

    def count():
        mm([(col("d1", 256), A("tk"), col("one", 0), True, True)])
        ts(A("acb"), A("bb"), col("d1", 256), AL.mult)
        mm([(col("d1", 128), A("acb"), col("one", 0), True, True)])
        ts(A("qb"), A("i64n"), col("d1", 128), AL.mult, QB, AL.add)
        mm([(A("gg", 17, 145), A("acb"), A("bbh"), False, False), (A("gg", 17, 145), A("qb"), A("i32b"), False, False)])

    def diffs(lo, hi):
        for bank, m0, m1 in DC:
            if not lo <= m0 < hi:
                continue
            a, b = 16 * m0, 16 * m1
            lst = []
            if a == 0:
                lst += [(A(bank, 1, 16), A("ib"), A("xs", 1, 16), True, False),
                        (A(bank, 1, 16), A("ibn"), A("xs", 2032, 2047), False, True)]
            a1 = max(a, 16)
            lst += [(A(bank, a1 - a, b - a), A("ib"), A("xs", a1, b), True, False),
                    (A(bank, a1 - a, b - a), A("ibn"), A("xs", a1 - 16, b - 16), False, True)]
            mm(lst)
            a2 = max(a, 1)
            act(A("ab", a2, b), A(bank, a2 - a, b - a), AF.Abs)

    def z_rep():
        nb = 0
        for _b, lo, hi in HS:
            mine = [(x, y) for mode, x, y in CH if mode not in "AB" and lo <= x < hi]
            m0, hi = min(mine)[0], max(mine)[1]
            k = -(-(hi - m0) // 32)
            for c in range(k - 1, -1, -1):
                bank = ("dfa", "dfb")[nb & 1]
                nb += 1
                a, b = 16 * (m0 + (hi - m0) * c // k), 16 * (m0 + (hi - m0) * (c + 1) // k)
                mm([(A(bank, 0, b - a), A(ZT[0]), A("emat", a, b), True, True)])
                act(A("zrep", a, b), A(bank, 0, b - a), AF.Copy, scale=1.0 / MID)

    YY = A("ysc", 15, 2048, 16)

    def blocks(t):
        for j in range(16):
            scan(A("ysc", 128 * j, 128 * j + 128), A("mb", 0, 128), A("xs", j, 2048, 16), 0.0, AL.min, AL.max)
        old = A(ZT[0])
        ZT.reverse()
        mm([(A("dg", 0, 128), A("ibn"), old, True, False), (A("dg", 0, 128), YY, A("ib"), False, True)])
        act(A(ZT[0]), A("dg", 0, 128), AF.Abs)
        ub, sb, zb = CFG["BB"]
        for r0 in range(0, 16, 8):
            mm([(A(ub, 384, 392), zl(r), A("ysc", 15 + 16 * r, 2048, 256), r == 0, r == 15) for r in range(r0, r0 + 8)])
        mm([(A(sb, 256, 384), old, A("ib"), True, False), (A(sb, 256, 384), A("ib"), YY, False, True)])
        if t == RO - 2:
            mm([(A(zb, 128, 256), old, A("ibn"), True, False), (A(zb, 128, 256), A("ib"), YY, False, True)])
            act(A("zs"), A(zb, 128, 256), AF.Abs)
        ts(A("sh"), A(sb, 256, 384), 0.5, AL.mult, -0.25, AL.add)
        ts(A("ui", 0, 8), A(ub, 384, 392), 1.0 / BIG, AL.mult)
        ts(A("ui", 8, 16), A("ui", 0, 8), 31, AL.bitwise_and)
        tt(A("uj"), A("ui", 8, 16), A("ci"), AL.add)
        cp(A("osc"), A("uj"))
        cp(IND("tab", 0, 4096, "osc", 0, 8), A("sh"))

    def periods():
        mm([(A("pm", 256, 289), A("ib"), A("cm", 0, 33), True, False)])
        scan(A("sc1", 0, 145), A("gg", 17, 162), A("cf"), 0.0, AL.max, AL.min)
        scan(A("sc1", 145, 290, -1), A("gg", 0, 145, -1), A("cb", 0, 145, -1), NONE, AL.max, AL.min)
        mm([(A("pm", 256, 289), A("bp"), A("sc1", 128, 161), False, False),
            (A("pm", 256, 289), A("bn"), A("sc1", 129, 162), False, True)])
        tt(A("al"), A("wk", 256, 384), A("sc1", 0, 128), AL.subtract)
        red(col("cy", 0), A("pm", 256, 272), AL.max)
        red(col("cy", 1), A("pm", 273, 290), AL.min)
        scan(A("wk", 0, 128), A("two"), A("al"), col("cy", 0), AL.add, AL.min)
        ts(A("ne"), A("sc1", 163, 291), col("cy", 1), AL.max)
        tt(A("zz"), A("wk", 0, 128), A("ne"), AL.add)
        tt(A("wk", 128, 256), A("wk", 384, 512), A("ne"), AL.add)
        ts(A("vv"), A("zz"), float(SEC), AL.mult, 0.0, AL.max)
        tt(A("qq"), A("wk", 0, 128), A("vv"), AL.add)
        tt(A("of"), A("wk", 128, 256), A("qq"), AL.min)
        ts(A("ob"), A("of"), float(SEC), AL.mult, 16.75, AL.add)
        ts(A("c1"), A("zz"), 192 * S19, AL.max, 256 * S19, AL.min)

    d1, d2 = T.cores[(rank + 1) % n], T.cores[(rank + 2) % n]
    mk = masks(topo, core, [d1, d2])
    s1, s2 = T.cores[(rank - 1) % n], T.cores[(rank - 2) % n]
    arrive = masks(topo, s1, [core, T.cores[(rank + 1) % n]])[0][1] + masks(topo, s2, [s1, core])[1][1]
    left = mk[0][1] + mk[1][1]

    def SND(i, a, b, p=None):
        return A("snd%d" % i, a, b, p=p)

    def LND(t, i, a, b, p=None):
        x = A("lnd%d" % t, 256 * i + a, 256 * i + b, p=p)
        return x[0], x[1] + col("om", HS[i][1])[1]

    def select(i, t):
        bank, m0, m1 = HS[i]
        p = (m0, m1)
        for e, a, b in CFG["DG"]:
            if m0 <= a < m1:
                gat(e, A("g2", 16 * a, 16 * b), IND("win", 0, WIN, "ob", a, b))
        mm([(A(bank, 0, 304, p=p), A("c1", m0, m1), A("fw"), True, False)])
        mm([(A(bank, j, 304, 16, p=p), A("g2", 16 * m0 + j, 16 * (m1 - 1) + j + 1, 16), A("sel", 0, 19), False, j == 15)
            for j in range(16)])
        gat(CFG["SC"][i], SND(i, 0, 304, p), A(bank, 0, 304, p=p))
        ops[-1]["pre"] = ("sent%d" % i, left * t)
        o = A(*(("pm", 0, 64), ("gg", 256, 320))[i])
        mm([(o, SND(i, 16, 144, p), A("i64", m0, m1, p=p), True, False),
            (o, SND(i, 176, 304, p), A("ib", m0, m1, p=p), False, True)])
        ts(A("op_", m0, m1), o, -POF, AL.add)

        def fn():
            trs = []
            for d, (m, _c), a, b in ((d1, mk[0], 0, 0), (d2, mk[1], 144, 128)):
                ad = topo.addr(d)
                trs.append(RemoteDMATransfer(dst_ids=[DstId(rid=ad[0], pnc=ad[1])], dma_engine_mask=m,
                                             remote_sem=T.sem["arr%d" % (2 * t + i)], src=SND(i, a, a + 128)[0],
                                             dst=LND(t, i, b, b + 128)[0]))
            g.remote_dma_fused(trs, local_sem=T.sem["sent%d" % i])
            return None
        add("g", fn, SND(i, 0, 304)[1], [], dma="remote", ext=("arr%d" % (2 * t + i), 0))

    def m_name(i, t):
        bank, m0, m1 = HS[i]
        p = (m0, m1)
        o = A(*(("gg", 384, 448), ("pm", 128, 192))[i])
        c = 256 * i
        mm([(o, A("lnd%d" % t, c, c + 128, p=p), A("i64", m0, m1, p=p), True, False),
            (o, A("lnd%d" % t, c + 128, c + 256, p=p), A("ib", m0, m1, p=p), False, True)],
           ext=("arr%d" % (2 * t + i), arrive))
        ts(A("om", m0, m1), o, -POF, AL.add)

    nb = [0]

    def distance(i, first):
        bank, lo, hi = HS[i]
        off, a2 = ("op_", "a2") if first else ("om", "a3")
        y0 = 16 * (lo if first else hi)
        more = []
        for mode, m0, m1 in CH:
            if not lo <= m0 < hi:
                continue
            a, b = 16 * m0, 16 * m1
            y = A("yy", y0 + a, y0 + b)
            if mode in "VRQS":
                tt(y, IND("tab", 0, 4096, off, m0, m1), A("zrep", a, b), AL.subtract)
                if mode in ("RQ" if first else "RS"):
                    ts(A(a2, a, b), y, 0.0, AL.max, 2.0, AL.mult)
                    more.append((m0, m1))
                else:
                    act(A(a2, a, b), y, AF.Abs)
                continue
            bk = ("dfa", "dfb")[nb[0] & 1]
            nb[0] += 1
            gat("a" if mode == "A" else "v", y, IND("tab", 0, 4096, off, m0, m1))
            mm([(A(bk, 0, b - a), A(ZT[0]), A("emat", a, b), True, False),
                (A(bk, 0, b - a), A("imid"), y, False, True)])
            act(A(a2, a, b), A(bk, 0, b - a), AF.Abs, scale=1.0 / MID)

        def part(src, c0, m0, m1, sign, start, stop):
            mm([(A(bank, j, 128, 16, p=(m0, m1)), A(src, c0 + 16 * m0 + j, c0 + 16 * (m1 - 1) + j + 1, 16),
                 A(sign), start and j == 0, stop and j == 15) for j in range(16)])
        if first:
            part(a2, 0, lo, hi, "s2n", True, False)
        if more:
            part("yy", y0, min(more)[0], max(more)[1], "s2p" if first else "s2n", False, False)
        if not first:
            part(a2, 0, lo, hi, "s2p", False, True)
            act(A("tk", p=(lo, hi)), A(bank, 0, 128, p=(lo, hi)), AF.Sign, bias=0.5)

    def new_x(i):
        bank, m0, m1 = HS[i]
        p = (m0, m1)
        o = A("pm", m0, m1)
        mm([(o, A("one", p=p), A("d16", m0, m1, p=p), True, False)])
        mm([(o, A("tk", p=p), A("ixw", m0, m1, p=p), False, True)])
        ts(A("oe", m0, m1), o, col("pf", 1), AL.add)
        for mode, a, b in CH:
            if m0 <= a < m1:
                src = IND("yy", 32 * m0, 32 * m1, "oe", a, b)
                if mode in "VRQS":
                    tt(A("xs", 16 * a, 16 * b), src, A("zrep", 16 * a, 16 * b), AL.add)
                else:
                    act(A("xs", 16 * a, 16 * b), src, AF.Copy)

    def m_diff(t):
        for i, h in enumerate(HS):
            p = h[1:]
            mm([(A("wk", 0, 256, p=p), A("ib", *p, p=p), LND(t, i, 0, 256, p), True, False),
                (A("wk", 0, 128, p=p), A("ibn", *p, p=p), SND(i, 16, 144, p), False, False),
                (A("wk", 128, 256, p=p), A("ibn", *p, p=p), SND(i, 176, 304, p), False, True)])

    def chosen(t, parts):
        tt(A("uu", 0, 128), A("wk", 0, 128), A("tk"), AL.mult)
        tt(A("uu", 128, 256), A("wk", 128, 256), A("tk"), AL.mult)
        for i, h in enumerate(HS):
            p = h[1:]
            lst = []
            for c, d, half, _neg in parts:
                o = A("dg", c + p[0], c + p[1])
                lst += [(o, LND(t, i, 128 * d, 128 * d + 128, p), A(half, *p, p=p), i == 0 and not lst, False),
                        (o, SND(i, (16, 176)[d], (144, 304)[d], p), A(half, *p, p=p), False, False)]
            mm(lst)
        if t < RO - 1:
            mm([(A("dg", 256, 384), A("kt"), A("ib"), False, False)])
        mm([(A("dg", e[0], e[0] + 128), A("uu", 128 * e[1], 128 * e[1] + 128), A(e[3]), False, e == parts[-1])
            for e in parts])

    def windows(t):
        for p0, c0, c in ((0, 16, 0), (1, 15, 0), (0, 16 + SEC, 0), (0, S2, 128), (1, S2 - 1, 128)):
            dma("s", A("win", c0, c0 + 2048, p=(p0, 128, 16)), A("hl", c, c + 128), "w%d" % t)

    for i in range(2):
        ms(SND(i, 0, 304, HS[1 - i][1:]), 0.0)
    windows(0)
    late_constants()
    threshold(0)
    for e, m0, m1 in CFG["E0"]:
        gat(e, A("xs", 16 * m0, 16 * m1), IND("tab", 0, 4096, "oe", m0, m1))
    mm([(A("dg", 128, 256), A("zs"), A("ib"), True, True)])
    act(A("zt"), A("dg", 128, 256), AF.Copy)
    diffs(SM, 128)
    sums(SM, 128, False)
    diffs(0, SM)
    sums(0, SM, True)
    last_constants()

    for t in range(RO):
        last = t == RO - 1
        CH[:] = CFG["CHL"] if last and CFG["CHL"] else CFG["CH"]
        z_rep()
        periods()
        for i in range(2):
            select(i, t)
        for i in range(2):
            distance(i, True)
        for i in range(2):
            m_name(i, t)
        m_diff(t)
        if not last:
            threshold(t + 1)
        for i in range(2):
            distance(i, False)
        for i in range(2):
            new_x(i)
        if not last:
            diffs(SM, 128)
            sums(SM, 128, False)
            chosen(t, ((0, 0, "ihf", "ihn"), (128, 1, "ihf", "ihn"), (256, 1, "ihf", "ihn")))
            gat(CFG["HL"], A("hl"), A("dg", 0, 256))
            lin(A("cf", 0, 128), A("dg", 256, 384), S19, col("pf", 9))
            windows(t + 1)
            count()
            diffs(0, SM)
            sums(0, SM, True)
            blocks(t)
            continue
        chosen(t, ((0, 0, "i32", "i32h"), (0, 1, "ihf", "ihn")))
        lin(A("nm"), A("dg", 0, 128), 1.0, -POF)
        cp(A("tin"), IND("nm", 0, 128, "o3", 0, 16))
        trn(A("tout"), A("tin"))
        act(A("nl"), IND("tout", 0, 256, "o4", 0, 8), AF.Copy)
        dma(CFG["LQ"][0], (T.ly[:], []), A("nl"), "out")
        for j0, j1 in CFG["TL"]:
            for j in range(j0, j1):
                gat(CFG["TE"][j], A("ab", 128 * j, 128 * j + 128), A("xs", j, 2048, 16))
            a, b = 128 * j0, 128 * j1
            dma("s", (T.xy[:, a:b], []), A("ab", a, b), "out")
            scan(A("ysc", a, b), A("mb", 0, b - a), A("ab", a, b), 0.0, AL.min, AL.max)
        tt(A("zd"), YY, A("zs"), AL.subtract)
        act(A("zt"), A("zd"), AF.Abs)
        dma(CFG["LQ"][1], (T.zy[:], []), A("zt"), "out")

    if not ORDER:
        hist = {}
        sent = {}
        for i, o in enumerate(ops):
            q = o["q"]
            dep = {}
            for regs, wr in ((o["r"], False), (o["w"], True)):
                for x in regs:
                    name = x[0]
                    for h, y, hw in hist.get(name, []):
                        p = ops[h]
                        if name in PS and p["q"] != q:
                            dep[h] = 1
                        elif name in PS and q == "p" and p["rows"] != o["rows"] and x[4] < y[5] and y[4] < x[5]:
                            dep[h] = 1
                        elif name in PS and q == "p":
                            dep.setdefault(h, 0)
                        elif o["dma"] and p["dma"] == o["dma"]:
                            dep.setdefault(h, 0)
                        elif (wr or hw) and meet(x, y):
                            dep[h] = 1
            if o["dma"] == "remote":
                sent[o["ext"][0]] = i
            elif o["ext"] is not None:
                dep[sent[o["ext"][0]]] = 1
            if o["after"] is not None:
                dep.setdefault(o["after"], 0)
            o["dep"] = dep
            for regs, wr in ((o["r"], False), (o["w"], True)):
                for x in regs:
                    name = x[0]
                    lst = hist.setdefault(name, [])
                    if name in PS:
                        if lst and ops[lst[-1][0]]["q"] != q:
                            lq = ops[lst[-1][0]]["q"]
                            k = len(lst)
                            while k and ops[lst[k - 1][0]]["q"] == lq:
                                k -= 1
                            lst[:] = lst[k:]
                    elif wr and not o["dma"]:
                        lst[:] = [h for h in lst if h[0] == i or not covers(x, h[1])]
                    lst.append((i, x, wr))
        for o in ops:
            o["suc"] = []
        for i, o in enumerate(ops):
            for d, kind in o["dep"].items():
                ops[d]["suc"].append((i, kind))
        ORDER.extend(arrange(ops))
    ops = [ops[i] for i in ORDER]

    cnt = {}
    known = {q: {} for q in Q}
    hist = {}
    for o in ops:
        q = o["q"]
        need = {}
        for regs, wr in ((o["r"], False), (o["w"], True)):
            for x in regs:
                name = x[0]
                for h in hist.get(name, []):
                    if name in PS and h["q"] != q:
                        hit = True
                    elif name in PS and q == "p":
                        hit = h["rows"] != o["rows"] and x[4] < h["x"][5] and h["x"][4] < x[5]
                    elif o["dma"] and h["sem"] == o["dma"]:
                        hit = False
                    else:
                        hit = (wr or h["wr"]) and meet(x, h["x"])
                    if hit:
                        s = h["sem"]
                        v = cnt[s] if h["dma"] else h["val"]
                        if v > need.get(s, (0, None))[0]:
                            need[s] = (v, h["clock"])
        kq = known[q]
        for s, (v, clock) in sorted(need.items(), key=lambda e: -len(e[1][1])):
            if kq.get(s, 0) < v:
                Q[q].wait_ge(T.sem[s], v)
                kq[s] = v
            for s2, v2 in clock.items():
                if kq.get(s2, 0) < v2:
                    kq[s2] = v2
        for e in (o["ext"], o.get("pre")):
            if e is not None and kq.get(e[0], 0) < e[1]:
                Q[q].wait_ge(T.sem[e[0]], e[1])
                kq[e[0]] = e[1]
        ins = o["fn"]()
        if o["dma"] == "remote":
            continue
        sem = o["dma"] or ESEM[q]
        inc = 16 if o["dma"] else 1
        ins.then_inc(T.sem[sem], inc)
        cnt[sem] = cnt.get(sem, 0) + inc
        clock = dict(kq)
        for regs, wr in ((o["r"], False), (o["w"], True)):
            for x in regs:
                name = x[0]
                lst = hist.setdefault(name, [])
                if wr and name not in PS:
                    lst[:] = [h for h in lst if not (covers(x, h["x"]) and h["sem"] != o["dma"])]
                lst.append({"q": q, "x": x, "wr": wr, "sem": sem, "val": cnt[sem], "dma": bool(o["dma"]),
                            "clock": clock, "rows": o.get("rows")})
    for s, v in cnt.items():
        g.wait_ge(T.sem[s], v)
    for i in range(2):
        g.wait_ge(T.sem["sent%d" % i], RO * left)
